import numpy as np, ml_dtypes
CORES = [36,164,52,180,100,228,116,244]
N = 8
import mx_ref
BF = ml_dtypes.bfloat16
def gentries(a):
    return np.ascontiguousarray(a.reshape(8, 16, -1).transpose(0, 2, 1)).reshape(8, -1)
def gtable(e):
    e = np.asarray(e); return np.ascontiguousarray(e.reshape(8, -1, 16).transpose(0, 2, 1)).reshape(128, -1).astype(np.int32)
def gcols(t, e):
    v = np.concatenate([t.reshape(8, 16, -1, 4), np.zeros((8, 16, 1, 4), BF)], axis=2)
    return np.ascontiguousarray(np.stack([v[g][:, e[g]] for g in range(8)])).reshape(128, -1)
def tile(rs):
    return np.stack(rs, axis=2).reshape(128, -1).astype(BF)
def pick(q, e):
    c = np.concatenate([q[0].reshape(128, -1, 4), np.zeros((128, 1, 4), np.uint8)], axis=1); s = np.concatenate([q[1], np.ones((16, 1), np.uint8)], axis=1)
    return (np.ascontiguousarray(c[:, e].reshape(128, -1)), np.ascontiguousarray(s[:, e]))
def join(*qs):
    return (np.concatenate([q[0] for q in qs], axis=1), np.concatenate([q[1] for q in qs], axis=1))
def put(q, e, v):
    c, s = q[0].reshape(128, -1, 4).copy(), q[1].copy(); c[:, e] = v[0].reshape(128, -1, 4); s[:, e] = v[1]
    return (c.reshape(128, -1), s)
def pk(c, s):
    return (np.ascontiguousarray(c), mx_ref.live(s))
def emit(q):
    return q[0], q[1]
def packed(v, rng):
    q = [mx_ref.quantize(np.ascontiguousarray(v[r])) for r in range(N)]
    return np.stack([a for a, b in q]), np.stack([mx_ref.plane(b, rng) for a, b in q])
def values_of_codes():
    e, c = np.zeros((128, 128, 4), np.float32), np.zeros((128, 2, 4), np.uint8)
    e[np.arange(128), np.arange(128), 0] = 1
    c[:127, :, 0] = np.arange(256).reshape(2, 128).T[:127]
    return mx_ref.matmul(mx_ref.quantize(e.reshape(128, 512).astype(BF)), (c.reshape(128, 8), np.full((16, 2), 127, np.uint8))).T.reshape(-1).astype(np.float64)
CODE_VALUE, SCALE_VALUE = values_of_codes(), 2.0 ** (np.arange(256) - 127.0)
def decode(q):
    return (CODE_VALUE[q[0]].reshape(16, 8, -1, 4) * SCALE_VALUE[q[1]][:, None, :, None] + 0.0).reshape(128, -1).astype(np.float32)
def f(rng, *shape):
    return mx_ref.flush((rng.standard_normal(shape, dtype=np.float32) * np.exp2(rng.integers(-2, 3, shape[:-1] + (1,)))).astype(BF))
def wide(rng, *shape, cols=0):
    v = rng.standard_normal(shape, dtype=np.float32) * np.exp2(rng.integers(-12, 13, shape)).astype(np.float32)
    if cols: v *= np.repeat(np.exp2(rng.integers(-cols, cols + 1, shape[:-2] + (1, shape[-1] // 4))) * (rng.random(shape[:-2] + (1, shape[-1] // 4)) > 0.0625), 4, axis=-1).astype(np.float32)
    return mx_ref.flush(v.astype(BF))
C, H, R = 288, 16, 3
def score(a, b):
    e = np.zeros((8, 16, 8, 16, 4), np.float32)
    for g in range(8): e[g, :, g] = 1
    z = (a.astype(np.float32) * b.astype(np.float32)).astype(BF)
    return mx_ref.matmul(mx_ref.quantize(e.reshape(128, 512).astype(BF)), mx_ref.quantize(z))[::16] + np.float32(0.0)
def big(v, k, low):
    v = v.astype(np.float32) * np.float32(k)
    v[np.abs(v) < np.float32(low)] = 0
    return v.astype(BF)
def state(rng):
    return big(f(rng, N, 128, 4 * C), 16, 2.0 ** -12)
def any_lists(rng):
    return rng.integers(0, C, (N, 8, 2, C)), rng.integers(0, N * H, (N, 8, C))
def unit():
    w = np.zeros((128, 4, 128, 4), np.float32)
    i = np.arange(128)
    for b in range(4): w[i, b, i, b] = 32
    return w.reshape(128, 2048).astype(BF)
def pack(rng, x, a, b, k=1, still=None):
    w = big(f(rng, N, 128, 2048), k, 2.0 ** -16)
    if still is not None: w[still] = unit()
    c, p = packed(w, rng)
    return {"x": x, "c1": np.stack([gtable(e.reshape(8, 2 * C)) for e in a]), "c2": np.stack([gtable(e) for e in b]), "v": np.array(f(rng, N, 128, 512)), "wc": c, "ws": p}
def signs(rng):
    return np.stack([rng.permutation(8) % 2 * 2.0 - 1.0 for r in range(N)])
def halves(rng):
    a, b = any_lists(rng)
    q, k, w = [np.zeros((N, 8, C // 2), int) for i in range(3)]
    for r in range(N):
        for g in range(8):
            o = rng.permutation(C)
            q[r, g], k[r, g] = o[:C // 2], o[C // 2:]
            c = 2 * rng.permutation(C // 4)[:H] + 1
            w[r, g] = rng.permutation(np.concatenate([c, c, c, rng.choice(c, C // 2 - 3 * H)]))
            i = rng.permutation(C // 2) % 2
            for n in range(2):
                a[r, g, n, q[r, g]] = k[r, g][np.where(i == n, w[r, g], w[r, g] - 1)]
                a[r, g, n, k[r, g]] = rng.permutation(q[r, g])
    return a, b, q, k, w
def setup_inputs(rng):
    a, b = any_lists(rng)
    return pack(rng, state(rng), a, b)
def setup_inputs_ties(rng):
    x = state(rng)
    e = rng.permutation(N)
    for r in range(N):
        k = np.zeros(C, int) if r == e[0] else rng.permutation(C) % 3
        t = x[r].reshape(128, C, 4)[:, :3].copy()
        t[:, 2] = 0
        x[r] = t[:, k].reshape(128, 4 * C)
    x[e[1]] = 0
    a, b = any_lists(rng)
    return pack(rng, x, a, b)
def setup_inputs_near(rng):
    a, b, q, k, w = halves(rng)
    s = signs(rng)
    d = ((np.arange(C // 2)[:, None] >> np.arange(8)) & 1) * np.exp2(np.arange(8) - 12.0)
    x = np.zeros((N, 8, 16, C, 4))
    z = np.zeros((8, N * H), int)
    for r in range(N):
        for g in range(8):
            m, i, j = rng.integers(4, 8, (13, C // 2, 4)) * rng.choice([-1.0, 1.0], (13, C // 2, 4)), q[r, g], k[r, g]
            p = x[r, g]
            p[0, i, 0] = s[r, g]
            p[0, j, 0] = 1
            p[8:10, i] = 2.0 ** -11
            p[8, j] = d[:, :4]
            p[9, j] = d[:, 4:]
            p[1:4, i] = m[:3] * 0.25
            p[4:8, j] = m[3:7] * 0.25
            p[10:13, i] = m[7:10] * 2.0 ** -9
            p[13:16, j] = m[10:] * 2.0 ** -9
            t, n = np.zeros(C, int), np.zeros(C, int)
            t[i] = j[w[r, g]]
            t[j] = a[r, g, 0, j]
            n[j] = np.arange(C // 2)
            z[g, H * r:H * r + H] = n[np.argsort(-np.bincount(t, minlength=C), kind="stable")[:H]]
    for g in range(8):
        o = np.argsort(z[g], kind="stable")
        t = np.argsort(o)
        for r in range(N): b[r, g, q[r, g]] = o[t[b[r, g, k[r, g][w[r, g]]]] ^ 1]
    return pack(rng, x.astype(np.float32).reshape(N, 128, 4 * C).astype(BF), a, b)
def setup_inputs_huge(rng):
    a, b, q, k, w = halves(rng)
    s = signs(rng)
    c = int(rng.integers(N))
    s[c] = 1
    b = rng.choice(np.flatnonzero(np.arange(N * H) // H != c), (N, 8, C))
    x = np.zeros((N, 8, 16, C, 4))
    odd = np.arange(C // 2) % 2 == 1
    for r in range(N):
        for g in range(8):
            x[r, g][:, q[r, g]] = s[r, g] * (1 + 0.25 * rng.random((16, C // 2, 4)))
            x[r, g][:, k[r, g]] = np.where(odd == (s[r, g] > 0), 1.5, 1.0)[None, :, None] + 0.25 * rng.random((16, C // 2, 4))
    x[c] *= -(2.0 ** -26)
    for g in range(8):
        i = np.concatenate([q[c, g], k[c, g][np.arange(C // 2) % 4 < 2]])
        b[c, g, i] = H * c + rng.integers(0, H, len(i))
    return pack(rng, (x * 2.0 ** 14).astype(np.float32).reshape(N, 128, 4 * C).astype(BF), a, b, 2.0 ** -3, c)
def setup_inputs_star(rng):
    a, b = any_lists(rng)
    e = rng.permutation(N)
    a[e[0]] = rng.integers(0, C, (8, 1, 1))
    b[e[0]] = rng.integers(0, N * H, (8, 1))
    for g in range(8):
        a[e[1], g] = rng.permutation(C)
        t, i = rng.permutation(C)[:2], rng.integers(0, 2, C)
        a[e[2], g, 0], a[e[2], g, 1] = t[i], t[1 - i]
    a[e[3]] = C - 1 - np.minimum(C - 1, (C * rng.random((8, 2, C)) ** 4).astype(int))
    b[e[1]] = H * e[1] + rng.integers(0, H, (8, C))
    b[e[2]] = H * e[3] + rng.integers(0, H, (8, C))
    return pack(rng, state(rng), a, b)
def setup_inputs_spread(rng):
    a, b = any_lists(rng)
    return pack(rng, big(wide(rng, N, 128, 4 * C, cols=2), 2.0 ** -3, 2.0 ** -12), a, b)
def check_inputs(d):
    b = []
    for k in ("x", "v"):
        a = np.abs(d[k].astype(np.float32))
        if not (np.isfinite(a).all() and ((a == 0) | (a >= 2.0 ** -30) & (a <= 2.0 ** 30)).all()): b.append("a value of " + k)
    for k, n in (("c1", C), ("c2", N * H)):
        if not ((d[k] >= 0) & (d[k] < n)).all(): b.append("an entry of " + k)
    if ((d["wc"] & 127) == 127).any(): b.append("a code of wc")
    s = np.stack([mx_ref.live(p) for p in d["ws"]])
    if not ((s >= 1) & (s <= 157)).all(): b.append("a scale of ws")
    return b
def reference(x, c1, c2, v, wc, ws):
    now = [x[r] for r in range(N)]
    hl = np.zeros((N, 8, R * H), np.float32)
    for t in range(R):
        points, hubs = [], []
        for r in range(N):
            e = gentries(c1[r])
            e0, e1 = e[:, :C], e[:, C:]
            p = np.where(score(now[r], gcols(now[r], e1)) > score(now[r], gcols(now[r], e0)), e1, e0)
            n = np.stack([np.bincount(p[g], minlength=C) for g in range(8)])
            h = np.argsort(-n, axis=1, kind="stable")[:, :H]
            points.append(p)
            hubs.append(mx_ref.quantize(gcols(now[r], h)))
            hl[r, :, H * t:H * t + H] = h
        slots = decode(join(*hubs)).astype(BF)
        for r in range(N):
            a0 = gentries(c2[r])
            a1 = np.take_along_axis(a0, points[r], axis=1)
            a = np.where(score(now[r], gcols(slots, a1)) > score(now[r], gcols(slots, a0)), a1, a0)
            m = ((now[r].astype(np.float32) + gcols(slots, a).astype(np.float32)) * np.float32(0.5)).astype(BF)
            q, w = mx_ref.quantize(m), pk(wc[r], ws[r])
            now[r] = tile([mx_ref.matmul(pick(w, np.arange(128 * b, 128 * b + 128)), q) * np.float32(0.03125) for b in range(4)])
    y = np.zeros((N, 128, C), np.float32)
    oc, osc = np.zeros((N, 128, 4 * C), np.uint8), np.zeros((N, 16, C), np.uint8)
    for r in range(N):
        q = mx_ref.quantize(now[r])
        y[r] = mx_ref.matmul(mx_ref.quantize(v[r]), q)
        oc[r], osc[r] = emit(q)
    return {"y": y, "hl": hl, "oc": oc, "osc": osc}

@@ -1,0 +1,542 @@
+from concourse.bass import DstId, RemoteDMATransfer
+from concourse.mybir import dt, AluOpType, AxisListType, ActivationFunctionType
+
+A = AluOpType
+AF = ActivationFunctionType
+C, H, R, N = 288, 16, 3, 8
+Q = C // 4
+PAD = 128 - Q
+ZW = PAD + C
+NP = C // 16
+HC = C // 2
+UB = 2048
+FW = 2 * N * H - H
+OWN = (N - 1) * H
+BIG = 4096.0
+
+DIRECT_CODES = 3
+DIRECT_SCALES = 4
+HELPERS_ON_OTHER_DIE = True
+
+X4, U8, BF, F32, I32, U16 = "float8_e4m3fn_x4", "uint8", "bfloat16", "float32", "int32", "uint16"
+
+
+def _sb(n, d):
+    return ("sbuf", [128, n], d)
+
+
+SCRATCH = {
+    "X": _sb(4 * C, BF), "X2": _sb(4 * C, BF), "Xh": _sb(4 * C, BF), "Xp": _sb(4 * C, BF), "Z": _sb(8 * C, BF),
+    "Zq": _sb(2 * ZW, X4), "Zs": _sb(2 * ZW, U8),
+    "c1s": _sb(36, I32), "c2s": _sb(18, I32), "vt": _sb(512, BF), "Vq": _sb(128, X4), "Vs": _sb(128, U8),
+    "Wq": _sb(512, X4), "Ws": _sb(512, U8),
+    "pci": _sb(1, I32), "ci": _sb(4, I32), "CF": _sb(32, F32), "IO": _sb(32, F32),
+    "one": _sb(512, BF), "ONt": _sb(512, BF), "ONq": _sb(128, X4), "ONs": _sb(128, U8),
+    "Kt": _sb(560, BF), "Kq": _sb(140, X4), "Ks": _sb(140, U8),
+    "Et": _sb(2048, BF), "Eq": _sb(512, X4), "Es": _sb(512, U8),
+    "ioP": _sb(C, BF), "ioR": _sb(C, BF), "tabF": _sb(128, BF), "tabH": _sb(4 * C, F32), "rm4": _sb(3 * C, BF),
+    "offP": _sb(144, U16), "offW": _sb(144, U16), "offc": _sb(36, U16), "offd": _sb(18, U16),
+    "LA": _sb(2 * C, BF), "PA": _sb(2 * C, BF), "SA": _sb(2 * C, BF), "dQ": _sb(Q, F32),
+    "LR": _sb(2 * C, BF), "PR": _sb(2 * C, BF), "SR": _sb(2 * C, BF),
+    "LB": _sb(3 * C, BF), "PB": _sb(3 * C, BF), "SB": _sb(3 * C, BF), "dg": _sb(Q, F32), "t1": _sb(Q, F32), "t2": _sb(Q, F32),
+    "D0": _sb(2 * Q, F32), "D1": _sb(2 * Q, F32), "PW": _sb(2 * Q, BF), "s0c": _sb(Q, F32),
+    "OH": _sb(20 * C, BF), "OHq": _sb(5 * C, X4), "OHs": _sb(5 * C, U8), "ab": _sb(4 * C, BF),
+    "cb": _sb(C, BF), "ge": _sb(C, BF), "junk": _sb(C, BF), "cnt": _sb(C, F32), "eq": _sb(C, BF), "pf": _sb(C, BF),
+    "AC": _sb(8, F32), "hf": _sb(32, F32), "gm": _sb(32, F32), "bc": _sb(32, F32), "RW": _sb(34, F32), "MB": _sb(34, F32), "SC": _sb(34, F32),
+    "offH": _sb(2, U16), "tie": _sb(16, F32), "KY": _sb(17, F32), "DK": _sb(17, F32), "dk1": _sb(17, F32), "dk2": _sb(17, F32), "OW": _sb(17, F32),
+    "tr0": _sb(128, F32), "tabR": _sb(128, F32), "r0": _sb(128, F32), "rm32": _sb(128, F32),
+    "O": _sb(128, F32), "OT": _sb(128, F32), "OS": _sb(128, F32), "offB": _sb(4, U16),
+    "Bt": _sb(512, BF), "h64": _sb(64, F32), "HL": _sb(R * H, F32),
+    "F": _sb(512, BF), "U": _sb(UB + 4 * C, BF), "off0": _sb(Q, U16), "off1": _sb(Q, U16), "offM": _sb(Q, U16),
+    "ix0": _sb(Q, F32), "offX": _sb(Q, U16), "cf0": _sb(Q, F32), "cfr": _sb(Q, F32), "sel2": _sb(Q, F32), "sf": _sb(Q, F32),
+    "Mt": _sb(4 * C, BF), "Mq": _sb(C, X4), "Ms": _sb(C, U8), "Xq": _sb(C, X4), "Xs": _sb(C, U8), "Y": _sb(C, F32),
+}
+for _t in range(R):
+    SCRATCH["Fq%d" % _t] = _sb(FW, X4)
+    SCRATCH["Fs%d" % _t] = _sb(FW, U8)
+    SCRATCH["hq%d" % _t] = _sb(H, X4)
+    SCRATCH["hs%d" % _t] = _sb(H, U8)
+for _b in range(8):
+    SCRATCH["ps%d" % _b] = ("psum", [128, 512], F32)
+
+NDMA = 20
+SEMAPHORES = (["cV", "cS", "cP", "cG", "sent"] + ["dma%d" % i for i in range(NDMA)]
+              + ["arr%d" % t for t in range(R)] + ["hin%d" % t for t in range(R)])
+
+
+def _mask(engines):
+    m = 0
+    for e in engines:
+        m |= 1 << e
+    return m
+
+
+def _plan(T, topo, rank):
+    core = T.cores[rank]
+    peers = [(rank + k) % N for k in range(1, N)]
+    cand = [c for c in topo.cores_of(core) if T.rank_of(c) is None
+            and (topo.die(c) != topo.die(core)) == HELPERS_ON_OTHER_DIE
+            and all(topo.may_write(c, T.cores[d]) for d in peers)]
+    rev = peers[::-1]
+    return {"q": (peers[:DIRECT_CODES], cand[0], peers[DIRECT_CODES:]),
+            "s": (rev[:DIRECT_SCALES], cand[-1], rev[DIRECT_SCALES:])}
+
+
+def _view(T, kind, name, a, b):
+    return T[name][:, a:b].bitcast(dt.uint8) if kind == "q" else T[name][:, a:b]
+
+
+def _spread(T, topo, src_core, rank, kind, t, src, dests):
+    ids, dsts = [], []
+    for d in dests:
+        rid, pid = topo.addr(T.cores[d], src_core)
+        ids.append(DstId(rid=rid, pnc=pid))
+        pos = ((rank - d - 1) % N) * H
+        dsts.append(_view(T, kind, "F%s%d" % (kind, t), pos, pos + H))
+    eng = topo.engines(src_core, T.cores[dests[0]])
+    return RemoteDMATransfer(dst_ids=ids, dma_engine_mask=_mask(eng), remote_sem=T.sem["arr%d" % t], srcs=[src], dsts=dsts), len(eng)
+
+
+def _feed_engines(T, topo, rank, helper):
+    core = T.cores[rank]
+    off = topo.engines(core, T.cores[(rank + 1) % N])
+    return [e for e in topo.engines(core, helper) if e not in off]
+
+
+def _helper(g, core, T, topo):
+    for rank in range(N):
+        if core not in topo.cores_of(T.cores[rank]):
+            continue
+        for kind, (direct, helper, rest) in _plan(T, topo, rank).items():
+            if helper != core or not rest:
+                continue
+            sent = 0
+            for t in range(R):
+                g.wait_ge(T.sem["hin%d" % t], len(_feed_engines(T, topo, rank, core)))
+                tr, n = _spread(T, topo, core, rank, kind, t, _view(T, kind, "h%s%d" % (kind, t), 0, H), rest)
+                g.remote_dma_fused([tr], local_sem=T.sem.sent)
+                sent += n
+            g.wait_ge(T.sem.sent, sent)
+
+
+def _emit(g, T, ops, tail):
+    queue = {"V": g.vector, "S": g.scalar, "P": g.tensor, "G": g, "Y": g.sync}
+    writer, readers = {}, {}
+    known = {e: {} for e in queue}
+    marked = set()
+    ndma = 0
+    for i, o in enumerate(ops):
+        e = o["e"]
+        deps = set()
+        for k in o["r"]:
+            if k in writer:
+                deps.add(writer[k])
+        for k in o["w"]:
+            if k in writer:
+                deps.add(writer[k])
+            deps.update(readers.get(k, ()))
+        need = {}
+        for d in deps:
+            u = ops[d]["u"]
+            if d == i or u is None or (u == "P" and e == "P"):
+                continue
+            if d > need.get(u, -1):
+                need[u] = d
+        waits = []
+        kn = known[e]
+        for u, d in sorted(need.items(), key=lambda x: -x[1]):
+            if kn.get(u, -1) >= d:
+                continue
+            waits.append(d)
+            marked.add(d)
+            for u2, d2 in ops[d]["clock"].items():
+                if d2 > kn.get(u2, -1):
+                    kn[u2] = d2
+        o["waits"] = waits
+        if o["dma"]:
+            o["u"] = "dma%d" % ndma
+            ndma += 1
+        o["clock"] = dict(kn)
+        if o["u"] is not None:
+            o["clock"][o["u"]] = i
+        for k in o["r"]:
+            readers.setdefault(k, []).append(i)
+        for k in o["w"]:
+            writer[k] = i
+            readers[k] = []
+    count = {e: 0 for e in queue}
+    for i, o in enumerate(ops):
+        q = queue[o["e"]]
+        for sem, val in o["pre"]:
+            q.wait_ge(T.sem[sem], val)
+        for d in o["waits"]:
+            q.wait_ge(T.sem[ops[d]["sem"]], ops[d]["val"])
+        ins = o["f"]()
+        if o["dma"]:
+            o["sem"], o["val"] = o["u"], 16
+            ins.then_inc(T.sem[o["sem"]], 16)
+        elif i in marked:
+            count[o["e"]] += 1
+            o["sem"], o["val"] = "c" + o["e"], count[o["e"]]
+            ins.then_inc(T.sem[o["sem"]], 1)
+    for i, o in enumerate(ops):
+        if o["dma"] and i not in marked:
+            queue[o["e"]].wait_ge(T.sem[o["sem"]], 16)
+    for sem, val in tail:
+        g.wait_ge(T.sem[sem], val)
+
+
+def rank_program(g, core, T, topo):
+    rank = T.rank_of(core)
+    if rank is None:
+        _helper(g, core, T, topo)
+        return
+    ops = []
+    V, S, P, Y = g.vector, g.scalar, g.tensor, g.sync
+
+    def op(e, f, r, w, dma=False, pre=(), remote=False):
+        ops.append({"e": e, "f": f, "r": list(r), "w": list(w), "dma": dma, "pre": list(pre), "u": None if (dma or remote) else e})
+
+    def ts(out, in0, s1, s2, o0, o1, r, w):
+        if o1 is None:
+            op("V", lambda: V.tensor_scalar(out, in0, s1, None, o0), r, w)
+        else:
+            op("V", lambda: V.tensor_scalar(out, in0, s1, s2, o0, o1), r, w)
+
+    def tt(out, in0, in1, o, r, w):
+        op("V", lambda: V.tensor_tensor(out, in0, in1, o), r, w)
+
+    def cp(out, in_, r, w):
+        op("V", lambda: V.tensor_copy(out, in_), r, w)
+
+    def ms(ap, c, w):
+        op("V", lambda: V.memset(ap, c), [], w)
+
+    def scan(out, d0, d1, init, o0, o1, r, w):
+        op("V", lambda: V.tensor_tensor_scan(out, d0, d1, init, o0, o1), r, w)
+
+    def qz(q, s, a, b, tile, r, w):
+        op("V", lambda: V.quantize_mx(T[q][:, a:b], T[s][:, a:b], tile), r, w)
+
+    def act(out, in_, func, r, w, **kw):
+        op("S", lambda: S.activation(out, in_, func, **kw), r, w)
+
+    def mm(bank, n, lq, ls, la, rq, rs, ra, start, stop, r, pre=()):
+        op("P", lambda: P.matmul_mx(T["ps%d" % bank][:, 0:n], T[lq][:, la:la + 128], T[ls][:, la:la + 128],
+                                    T[rq][:, ra:ra + n], T[rs][:, ra:ra + n], start, stop), r, ["ps%d" % bank], pre=pre)
+
+    def iota(out, pat, base, cm, w, flag=True):
+        if flag:
+            op("G", lambda: g.iota(out, pat, base, cm, allow_small_or_imprecise_dtypes=True), [], w)
+        else:
+            op("G", lambda: g.iota(out, pat, base, cm), [], w)
+
+    def asel(out, in_, pat, cmp, base, cm, r, w):
+        op("G", lambda: g.affine_select(out, in_, pat, cmp, 0.0, base, cm), r, w)
+
+    def dma(e, out, in_, r, w):
+        q = Y if e == "Y" else S
+        op(e, lambda: q.dma_start(out, in_), r, w, dma=True)
+
+    def col(i):
+        return T.CF[:, i:i + 1]
+
+    def ac(i):
+        return T.AC[:, i:i + 1]
+
+    def names(p, n):
+        return [p + str(i) for i in range(n)]
+
+    XA = names("X0", 4) + names("X1", 4)
+    cQ, cT, cU, cHB, cTAU, cNS, cT576, cT128, cMB, cHM, cNH = range(11)
+    cCM, cDM, cE, cEB = 12, 16, 20, 24
+
+    dma("S", T.c1s[:], T.c1[:], [], ["c1s"])
+    dma("Y", T.X[:], T.x[:], [], XA)
+    dma("S", T.c2s[:], T.c2[:], [], ["c2s"])
+    dma("Y", T.Wq[:].bitcast(dt.uint8), T.wc[:], [], ["Wq"])
+    dma("Y", T.Ws[:], T.ws[:], [], ["Ws"])
+    dma("Y", T.vt[:], T.v[:], [], ["vt"])
+
+    ms(T.one[:], 1.0, ["one"])
+    iota(T.pci[:], [[0, 1]], 0, 1, ["pci"], flag=False)
+    iota(T.IO[:], [[1, 32]], 0, 0, ["IO"])
+    iota(T.ioP[:, 0:HC], [[1, HC]], -HC, 0, ["ioPa"])
+    iota(T.ioP[:, HC:C], [[1, HC]], 1, 0, ["ioPb"])
+    IOP = ["ioPa", "ioPb"]
+    asel(T.ONt[:], T.one[:], [[-16, 8], [0, 64]], A.is_ge, 0, 1, ["one"], ["ONt"])
+    asel(T.ONt[:], T.ONt[:], [[16, 8], [0, 64]], A.is_ge, 15, -1, ["ONt"], ["ONt"])
+    asel(T.Kt[:, 48:560], T.ONt[:], [[0, 8], [-1, 64]], A.is_ge, 15, 0, ["ONt"], ["Ktb"])
+    ms(T.Bt[:], 0.0, ["Bt"])
+    ts(T.ci[:, 0:1], T.pci[:], 15, None, A.bitwise_and, None, ["pci"], ["ci0"])
+    ts(T.ci[:, 1:2], T.pci[:], 3, None, A.bitwise_and, None, ["pci"], ["ci1"])
+    ts(T.ci[:, 2:3], T.pci[:], 2, 3, A.logical_shift_right, A.bitwise_and, ["pci"], ["ci2"])
+    ts(T.ci[:, 3:4], T.pci[:], 4, 1, A.logical_shift_right, A.bitwise_and, ["pci"], ["ci3"])
+    ms(T.rm4[:], 1.0, ["rm4"])
+    cp(T.CF[:, 0:4], T.ci[:], names("ci", 4), ["cf"])
+    for k in range(2):
+        qz("Zq", "Zs", k * ZW, k * ZW + 128, T.Bt[:], ["Bt"], ["Zpad%d" % k, "Zq%d0" % k])
+    ms(T.rm4[:, 0:3 * C:4], 0.0, ["rm4"])
+    ts(T.CF[:, cCM:cCM + 4], T.IO[:, 0:4], col(cU), None, A.is_equal, None, ["IO", "cf"], ["cm"])
+    ts(T.CF[:, cDM:cDM + 4], T.IO[:, 0:4], col(cT), None, A.is_equal, None, ["IO", "cf"], ["dm"])
+    ts(T.CF[:, cE:cE + 4], T.IO[:, 0:4], col(cT), 1.0 / BIG, A.is_gt, A.mult, ["IO", "cf"], ["e"])
+    ts(T.CF[:, cEB:cEB + 4], T.IO[:, 0:4], col(cT), BIG, A.is_gt, A.mult, ["IO", "cf"], ["eb"])
+    ms(T.Kt[:, 0:48], 0.0, ["Kta"])
+    ms(T.RW[:, 33:34], 0.0, ["RWc"])
+    ms(T.MB[:, 0:1], 0.0, ["MBa"])
+    ms(T.KY[:, 16:17], 0.0, ["KYb"])
+    act(T.U[:, 4 * C:4 * C + 512], T.one[:], AF.Copy, ["one"], ["Ug0"])
+    act(T.U[:, 4 * C + 512:UB], T.one[:, 0:UB - 4 * C - 512], AF.Copy, ["one"], ["Ug1"])
+    act(col(cTAU), col(cQ), AF.Identity, ["cf"], ["tau"], bias=0.5 - H)
+    act(col(cNS), col(cQ), AF.Identity, ["cf"], ["ns"], scale=-1.0, bias=-0.5)
+    act(col(cT576), col(cT), AF.Identity, ["cf"], ["t576"], bias=float(2 * C))
+    act(col(cT128), col(cT), AF.Identity, ["cf"], ["t128"], scale=float(N * H))
+    act(col(cMB), col(cU), AF.Identity, ["cf"], ["mb"], scale=float(4 * Q), bias=col(cT))
+    act(col(cHM), col(cHB), AF.Identity, ["cf"], ["hm"], bias=-1.0)
+    act(col(cNH), col(cHB), AF.Identity, ["cf"], ["nh"], scale=-1000.0)
+    act(T.tie[:], T.IO[:, 0:H], AF.Identity, ["IO"], ["tie"], scale=-1.0 / H, bias=(H - 1.0) / H)
+    own = (rank + 1) * H
+    iota(T.ioR[:], [[1, C]], -HC, 0, ["ioR"])
+    iota(T.hf[:], [[1, 2], [0, 16]], 0, 0, ["hf"])
+    for e in range(2, 4):
+        iota(T.OH[:, 16 * C + e:20 * C:4], [[0, C]], 0, 0, ["OH4%d" % e])
+    iota(T.tabF[:, 0:own], [[1, own]], N * H - own, 0, ["tabFa"])
+    if own < N * H:
+        iota(T.tabF[:, own:N * H], [[1, N * H - own]], 0, 0, ["tabFb"])
+    for cc in range(4):
+        iota(T.tr0[:, 32 * cc:32 * cc + 32], [[1000, 2], [-2, 4], [0, 4]], H - 1 - 8 * cc, 0, ["tr0%d" % cc])
+    iota(T.r0[:], [[0, 4], [1, 32]], 0, 0, ["r0"])
+    iota(T.ix0[:], [[4, 4], [16, NP]], 0, 0, ["ix0"])
+    iota(T.cf0[:], [[1, Q]], 0, 0, ["cf0"])
+    for b in range(4):
+        asel(T.Et[:, 512 * b:512 * b + 512], T.one[:], [[-1, 512]], A.is_equal, b, 4, ["one"], ["Et%d" % b])
+
+    cp(T.offc[:], T.c1s[:], ["c1s"], ["offc"])
+    for t in range(4):
+        ts(T.offP[:, 36 * t:36 * t + 36], T.c1s[:], 4, t, A.mult, A.add, ["c1s"], ["offP%d" % t])
+    act(T.LA[:], T.ioP[:].indirect(T.offc[:]), AF.Copy, IOP + ["offc"], ["LA"])
+    for k in range(2):
+        for u in range(4):
+            act(T.PA[:, C * k + u:C * k + C:4], T.LA[:, C * k + Q * u:C * k + Q * u + Q], AF.Copy, ["LA", "cm"], ["PA%d%d" % (k, u)], scale=col(cCM + u))
+    for t in range(4):
+        act(T.D0[:, 2 * t:2 * Q:8], T.IO[:, 0:NP], AF.Identity, ["IO", "eb"], ["D0e%d" % t], scale=0.0, bias=col(cEB + t))
+    cp(T.X2[:], T.X[:], XA, ["X20", "X21"])
+
+    plan = _plan(T, topo, rank)
+    sent = [0]
+
+    def send(kind, t):
+        direct, helper, rest = plan[kind]
+        src = _view(T, kind, "F%s%d" % (kind, t), OWN, OWN + H)
+        trs = []
+        if rest:
+            eng = _feed_engines(T, topo, rank, helper)
+            rid, pid = topo.addr(helper, core)
+            trs.append(RemoteDMATransfer(dst_ids=[DstId(rid=rid, pnc=pid)], dma_engine_mask=_mask(eng), remote_sem=T.sem["hin%d" % t],
+                                         srcs=[src], dsts=[_view(T, kind, "h%s%d" % (kind, t), 0, H)]))
+            sent[0] += len(eng)
+        if direct:
+            tr, n = _spread(T, topo, core, rank, kind, t, src, direct)
+            trs.append(tr)
+            sent[0] += n
+        op("G", lambda: g.remote_dma_fused(trs, local_sem=T.sem.sent), ["Fown%d" % t], [], remote=True)
+
+    arrivals = 0
+    for s in range(N):
+        if s != rank:
+            for kind, (direct, helper, rest) in _plan(T, topo, s).items():
+                arrivals += len(topo.engines(T.cores[s] if rank in direct else helper, core))
+
+    def scores(k, halves):
+        base = k * ZW
+        zr = names("Z%d" % k, 4)
+        if halves:
+            for h in range(2):
+                qz("Zq", "Zs", base + PAD + h * HC, base + PAD + (h + 1) * HC,
+                   T.Z[:, 4 * C * k + 2 * C * h:4 * C * k + 2 * C * (h + 1)], zr, ["Zq%d%d" % (k, h)])
+        else:
+            qz("Zq", "Zs", base + PAD, base + ZW, T.Z[:, 4 * C * k:4 * C * (k + 1)], zr, ["Zq%d0" % k, "Zq%d1" % k])
+        for u in range(4):
+            mm(k, 128, "Kq", "Ks", 12 - 4 * u, "Zq", "Zs", base + Q * u, u == 0, u == 3,
+               ["Kq", "Zpad%d" % k, "Zq%d0" % k] + (["Zq%d1" % k] if u >= 2 else []))
+
+    for t in range(R):
+        first, last = t == 0, t == R - 1
+        for k in range(2):
+            if first:
+                for e in range(4):
+                    tt(T.Z[:, 4 * C * k + e:4 * C * (k + 1):4], T.X[:].indirect(T.offP[:, 36 * e + 18 * k:36 * e + 18 * k + 18]),
+                       T.X2[:, e:4 * C:4], A.mult, XA + ["X20", "X21", "offP%d" % e], ["Z%d%d" % (k, e)])
+            elif k == 0:
+                for c in range(2):
+                    tt(T.Z[:, 2 * C * c:2 * C * (c + 1)], T.X[:].indirect(T.offW[:, 36 * c:36 * c + 36]), T.X2[:, 2 * C * c:2 * C * (c + 1)],
+                       A.mult, XA + ["X2%d" % c, "offW"], ["Z0%d" % (2 * c), "Z0%d" % (2 * c + 1)])
+            else:
+                tt(T.Z[:, 4 * C:8 * C], T.X[:].indirect(T.offW[:, Q:2 * Q]), T.X2[:], A.mult, XA + ["X20", "X21", "offW"], names("Z1", 4))
+            if first and k == 0:
+                qz("Kq", "Ks", 0, 140, T.Kt[:], ["Kta", "Ktb"], ["Kq"])
+            scores(k, k == 1)
+            if first and k == 0:
+                scan(T.SA[:], T.rm4[:, 0:2 * C], T.PA[:], 0.0, A.mult, A.add, ["rm4"] + names("PA0", 4) + names("PA1", 4), ["SA"])
+                tt(T.dQ[:], T.SA[:, C + 3:2 * C:4], T.SA[:, 3:C:4], A.subtract, ["SA"], ["dQ"])
+                act(T.LR[:], T.ioR[:].indirect(T.offc[:]), AF.Copy, ["ioR", "offc"], ["LR"])
+                for e in range(4):
+                    act(T.D1[:, 2 * e + 1:2 * Q:8], T.SA[:, 4 * e + 3:C:16], AF.Copy, ["SA", "dm"], ["D1o%d" % e], scale=col(cDM + e))
+                for e in range(4):
+                    act(T.D0[:, 2 * e + 1:2 * Q:8], T.dQ[:, e:Q:4], AF.Identity, ["dQ", "dm", "e"], ["D0o%d" % e], scale=col(cDM + e), bias=col(cE + e))
+            if k == 0:
+                act(T.s0c[:], T.ps0[:, PAD:128], AF.Copy, [], ["s0c", "ps0"])
+        if first:
+            act(T.gm[:], T.hf[:], AF.Abs, ["hf", "hm"], ["gm"], bias=col(cHM))
+            qz("ONq", "ONs", 0, 128, T.ONt[:], ["ONt"], ["ONq"])
+            cp(T.offd[:], T.c2s[:], ["c2s"], ["offd"])
+            ts(T.dk1[:], T.IO[:, 0:17], col(cQ), -10000.0, A.is_equal, A.mult, ["IO", "cf"], ["dk1"])
+            ts(T.dk2[:], T.IO[:, 0:17], col(cQ), 1.0, A.subtract, A.is_equal, ["IO", "cf"], ["dk2"])
+        tt(T.D1[:, 0:2 * Q:2], T.ps1[:, PAD:128], T.s0c[:], A.is_gt, ["s0c"], ["D1e", "ps1"])
+        scan(T.PW[:], T.D0[:], T.D1[:], 0.0, A.mult, A.add, ["D1e"] + names("D1o", 4) + names("D0o", 4) + names("D0e", 4), ["PW"])
+        for e in range(4):
+            r = 12 + e
+            act(T.ab[:, e:4 * C:4], T.ioP[:], AF.Abs, IOP + ["PW"], ["ab%d" % e], scale=-1.0, bias=T.PW[:, 8 * r + 7:8 * r + 8])
+        act(T.OH[:, 12 * C:16 * C], T.ab[:], AF.Relu, names("ab", 4), ["OH3"], scale=-1.0, bias=1.0)
+        if first:
+            act(T.LB[:, 0:C], T.tabF[:].indirect(T.offd[:]), AF.Copy, ["tabFa", "tabFb", "offd"], ["LB0"])
+            act(T.LB[:, C:3 * C], T.LB[:, 0:C].indirect(T.offc[:]), AF.Copy, ["LB0", "offc"], ["LB1"])
+            act(T.tabR[:], T.tr0[:], AF.Identity, names("tr0", 4) + ["nh"], ["tabR"], bias=col(cNH))
+            act(T.rm32[:], T.r0[:], AF.Sign, ["r0"], ["rm32"])
+
+        def planes(i):
+            for e in range(4 if i < 4 else 2):
+                r = 4 * i + e
+                ts(T.OH[:, 4 * C * i + e:4 * C * (i + 1):4], T.ioP[:], T.PW[:, 8 * r + 7:8 * r + 8], None, A.is_equal, None,
+                   IOP + ["PW"], ["OH%d%d" % (i, e)])
+
+        def count(i, start, stop):
+            rr = ["OH3"] if i == 3 else names("OH%d" % i, 4)
+            qz("OHq", "OHs", C * i, C * i + C, T.OH[:, 4 * C * i:4 * C * (i + 1)], rr, ["OHq%d" % i])
+            mm(2, C, "ONq", "ONs", 0, "OHq", "OHs", C * i, start, stop, ["ONq", "OHq%d" % i])
+
+        planes(0)
+        planes(1)
+        count(0, True, False)
+        planes(2)
+        count(1, False, False)
+        planes(4)
+        count(2, False, False)
+        count(4, False, False)
+        count(3, False, True)
+        if first:
+            ts(T.dk2[:, 16:17], T.dk2[:, 16:17], -1.0, None, A.add, None, ["dk2"], ["dk2"])
+            ts(T.dk2[:], T.dk2[:], 1024.0, None, A.mult, None, ["dk2"], ["dk2"])
+            tt(T.DK[:], T.dk1[:], T.dk2[:], A.add, ["dk1", "dk2"], ["DK"])
+        ts(T.cb[:], T.ps2[:, 0:C], H + 1.0, H + 0.5, A.min, A.subtract, [], ["cb", "ps2"])
+        ts(T.ge[:], T.cb[:], col(cTAU), None, A.is_ge, None, ["cb", "tau"], ["ge"])
+        act(T.junk[:], T.cb[:], AF.Relu, ["cb"], ["junk", "RWb"], bias=0.5, accum_out=T.RW[:, 32:33])
+        act(T.cnt[:], T.ps2[:, 0:C], AF.Copy, [], ["cnt", "ps2"])
+        op("V", lambda: V.tensor_reduce(ac(0), T.ge[:], AxisListType.X, A.add), ["ge"], ["ac0"])
+        ts(T.bc[:], T.gm[:], ac(0), None, A.mult, None, ["gm", "ac0"], ["bc"])
+        op("V", lambda: V.transpose(T.RW[:, 0:32], T.bc[:]), ["bc"], ["RWa"])
+        act(T.junk[:, 0:33], T.RW[:, 0:33], AF.Sign, ["RWa", "RWb", "ns"], ["junk", "ac1"], bias=col(cNS), accum_out=ac(1))
+        ts(T.MB[:, 1:34], T.RW[:, 0:33], col(cQ), None, A.is_le, None, ["RWa", "RWb", "cf"], ["MBb"])
+        scan(T.SC[:], T.MB[:], T.RW[:], 0.0, A.mult, A.max, ["MBa", "MBb", "RWa", "RWb", "RWc"], ["SC"])
+        ts(T.eq[:], T.cb[:], 2.0, ac(1), A.mult, A.is_equal, ["cb", "ac1"], ["eq"])
+        scan(T.pf[:], T.eq[:], T.eq[:], T.SC[:, 33:34], A.add, A.max, ["eq", "SC"], ["pf"])
+        act(T.junk[:], T.pf[:], AF.Sign, ["pf", "ns"], ["junk", "ac2"], bias=col(cNS), accum_out=ac(2))
+        ts(T.offH[:, 0:1], ac(2), -0.5, C / 2.0, A.mult, A.add, ["ac2"], ["offH"])
+        tt(T.KY[:, 0:H], T.cnt[:].indirect(T.offH[:, 0:1]), T.tie[:], A.add, ["cnt", "offH", "tie"], ["KYa"])
+        scan(T.OW[:], T.DK[:], T.KY[:], 0.0, A.add, A.max, ["DK", "KYa", "KYb"], ["OW"])
+        act(T.junk[:, 0:H], T.KY[:, 0:H], AF.Sign, ["KYa", "OW"], ["junk", "ac3"], scale=-1.0, bias=T.OW[:, 16:17], accum_out=ac(3))
+        ts(T.O[:], T.tabR[:], ac(3), ac(2), A.is_equal, A.mult, ["tabR", "ac3", "ac2"], ["O"])
+        op("V", lambda: V.transpose(T.OT[:], T.O[:]), ["O"], ["OT"])
+        scan(T.OS[:], T.rm32[:], T.OT[:], 0.0, A.mult, A.add, ["rm32", "OT"], ["OS"])
+        ts(T.offB[:], T.OS[:, 31:128:32], -2.0, col(cT576), A.mult, A.add, ["OS", "t576"], ["offB"])
+        cp(T.Bt[:, 0:4 * H], T.X[:].indirect(T.offB[:]), XA + ["offB"], ["Bt"])
+        qz("Fq%d" % t, "Fs%d" % t, OWN, OWN + 128, T.Bt[:], ["Bt"], ["Fown%d" % t])
+        send("q", t)
+        send("s", t)
+        if first:
+            iota(T.tabH[:], [[1, C], [0, 4]], 0, 0, ["tabH"])
+            ts(T.offX[:], T.ix0[:], col(cMB), None, A.add, None, ["ix0", "mb"], ["offX"])
+            for k in range(3):
+                for u in range(4):
+                    act(T.PB[:, C * k + u:C * k + C:4], T.LB[:, C * k + Q * u:C * k + Q * u + Q], AF.Copy, ["LB0", "LB1", "cm"],
+                        ["PB%d%d" % (k, u)], scale=col(cCM + u))
+            qz("Eq", "Es", 0, 512, T.Et[:], names("Et", 4), ["Eq"])
+        act(T.Xp[:], T.X[:].indirect(T.offX[:]), AF.Copy, XA + ["offX"], ["Xp"])
+        ts(T.Xh[:], T.X[:], 0.5, None, A.mult, None, XA, ["Xh"])
+        if first:
+            ts(T.cfr[:], T.cf0[:], 4.0 / UB, None, A.mult, None, ["cf0"], ["cfr"])
+            scan(T.SB[:], T.rm4[:], T.PB[:], 0.0, A.mult, A.add, ["rm4"] + names("PB0", 4) + names("PB1", 4) + names("PB2", 4), ["SB"])
+            tt(T.dg[:], T.SB[:, 2 * C + 3:3 * C:4], T.SB[:, C + 3:2 * C:4], A.subtract, ["SB"], ["dg"])
+            for u in range(4):
+                ts(T.off0[:, NP * u:NP * u + NP], T.SB[:, 4 * u + 3:C:16], col(cT128), None, A.add, None, ["SB", "t128"], ["off0%d" % u])
+        tt(T.t1[:], T.D1[:, 0:2 * Q:2], T.dg[:], A.mult, ["D1e", "dg"], ["t1"])
+        tt(T.t2[:], T.t1[:], T.SB[:, C + 3:2 * C:4], A.add, ["t1", "SB"], ["t2"])
+        for u in range(4):
+            ts(T.off1[:, NP * u:NP * u + NP], T.t2[:, u:Q:4], col(cT128), None, A.add, None, ["t2", "t128"], ["off1%d" % u])
+        if first:
+            for u in range(4):
+                act(T.PR[:, u:2 * C:4], T.LR[:, u:2 * C:4], AF.Copy, ["LR", "cm"], ["PR%d" % u], scale=col(cCM + u))
+            qz("Vq", "Vs", 0, 128, T.vt[:], ["vt"], ["Vq"])
+            scan(T.SR[:], T.rm4[:, 0:2 * C], T.PR[:], 0.0, A.mult, A.add, ["rm4"] + names("PR", 4), ["SR"])
+            ts(T.offW[:], T.SR[:, 3:2 * C:4], 4.0, col(cT576), A.mult, A.add, ["SR", "t576"], ["offW"])
+        act(T.h64[:], T.tabH[:].indirect(T.offB[:]), AF.Copy, ["tabH", "offB"], ["h64"])
+        act(T.HL[:, H * t:H * t + H], T.h64[:, 0:64:4], AF.Copy, ["h64"], ["HL%d" % t])
+        if last:
+            dma("Y", T.hl[:], T.HL[0:128:16, :], names("HL", R), [])
+        for b in range(4):
+            mm(4 + b, 128, "Eq", "Es", 128 * b, "Fq%d" % t, "Fs%d" % t, 0, True, True, ["Eq", "Fown%d" % t],
+               pre=[("arr%d" % t, arrivals)] if b == 0 else ())
+        for b in range(4):
+            if b % 2 == 0:
+                cp(T.F[:, 128 * b:128 * b + 128], T["ps%d" % (4 + b)][:, 0:128], [], ["F%d" % b, "ps%d" % (4 + b)])
+            else:
+                act(T.F[:, 128 * b:128 * b + 128], T["ps%d" % (4 + b)][:, 0:128], AF.Copy, [], ["F%d" % b, "ps%d" % (4 + b)])
+        FA = names("F", 4)
+        for k in range(2):
+            o = "off%d" % k
+            act(T.U[:, UB * k:UB * k + 4 * C], T.F[:].indirect(T[o][:]), AF.Copy, FA + names(o, 4), ["U%d" % k], scale=0.5)
+            tt(T.Z[:, 4 * C * k:4 * C * (k + 1)], T.F[:].indirect(T[o][:]), T.Xp[:], A.mult, FA + names(o, 4) + ["Xp"], names("Z%d" % k, 4))
+            scores(k, k == 1)
+        act(T.s0c[:], T.ps0[:, PAD:128], AF.Copy, [], ["s0c", "ps0"])
+        tt(T.sel2[:], T.ps1[:, PAD:128], T.s0c[:], A.is_gt, ["s0c"], ["sel2", "ps1"])
+        tt(T.sf[:], T.sel2[:], T.cfr[:], A.add, ["sel2", "cfr"], ["sf"])
+        for u in range(4):
+            ts(T.offM[:, NP * u:NP * u + NP], T.sf[:, u:Q:4], float(UB), col(cMB), A.mult, A.add, ["sf", "mb"], ["offM%d" % u])
+
+        def evac(c, b, eng):
+            bank = "ps%d" % (4 * (1 - c) + b)
+            out = T.X[:, 2 * C * c + b:2 * C * (c + 1):4]
+            if eng == "V":
+                ts(out, T[bank][:, 0:HC], 0.03125, None, A.mult, None, [], ["X%d%d" % (c, b), bank])
+            else:
+                act(out, T[bank][:, 0:HC], AF.Copy, [], ["X%d%d" % (c, b), bank], scale=0.03125)
+
+        def finish(c):
+            if not last:
+                act(T.X2[:, 2 * C * c:2 * C * (c + 1)], T.X[:, 2 * C * c:2 * C * (c + 1)], AF.Copy, names("X%d" % c, 4), ["X2%d" % c])
+                return
+            qz("Xq", "Xs", HC * c, HC * c + HC, T.X[:, 2 * C * c:2 * C * (c + 1)], names("X%d" % c, 4), ["Xq%d" % c])
+            mm(4 + c, HC, "Vq", "Vs", 0, "Xq", "Xs", HC * c, True, True, ["Vq", "Xq%d" % c])
+            dma("Y", T.oc[:, 2 * C * c:2 * C * (c + 1)], T.Xq[:, HC * c:HC * c + HC].bitcast(dt.uint8), ["Xq%d" % c], [])
+
+        for c in range(2):
+            tt(T.Mt[:, 2 * C * c:2 * C * (c + 1)], T.U[:].indirect(T.offM[:, 2 * NP * c:2 * NP * (c + 1)]), T.Xh[:, 2 * C * c:2 * C * (c + 1)],
+               A.add, ["U0", "U1", "Ug0", "Ug1", "Xh", "offM%d" % (2 * c), "offM%d" % (2 * c + 1)], ["Mt%d" % c])
+            qz("Mq", "Ms", HC * c, HC * c + HC, T.Mt[:, 2 * C * c:2 * C * (c + 1)], ["Mt%d" % c], ["Mq%d" % c])
+            for b in range(4):
+                mm(4 * (1 - c) + b, HC, "Wq", "Ws", 128 * b, "Mq", "Ms", HC * c, True, True, ["Wq", "Ws", "Mq%d" % c])
+            if c == 0:
+                for b in range(4):
+                    evac(0, b, "S")
+        finish(0)
+        for b in range(4):
+            evac(1, b, "VS"[b % 2])
+        finish(1)
+        if last:
+            act(T.Y[:, 0:HC], T.ps4[:, 0:HC], AF.Copy, [], ["Y0", "ps4"])
+            cp(T.Y[:, HC:C], T.ps5[:, 0:HC], [], ["Y1", "ps5"])
+            dma("S", T.y[:, 0:HC], T.Y[:, 0:HC], ["Y0"], [])
+            for k in range(4):
+                dma("YS"[k // 2], T.osc[4 * k:4 * k + 4, :], T.Xs[32 * k:32 * k + 4, :], ["Xq0", "Xq1"], [])
+            dma("Y", T.y[:, HC:C], T.Y[:, HC:C], ["Y1"], [])
+    _emit(g, T, ops, [("sent", sent[0])])

@@ -1,5 +1,5 @@
 from concourse.bass import DstId, RemoteDMATransfer
-from concourse.mybir import dt, AluOpType, AxisListType, ActivationFunctionType
+from concourse.mybir import dt, AluOpType, ActivationFunctionType
 
 A = AluOpType
 AF = ActivationFunctionType
@@ -41,11 +41,12 @@ SCRATCH = {
     "LB": _sb(3 * C, BF), "PB": _sb(3 * C, BF), "SB": _sb(3 * C, BF), "dg": _sb(Q, F32), "t1": _sb(Q, F32), "t2": _sb(Q, F32),
     "D0": _sb(2 * Q, F32), "D1": _sb(2 * Q, F32), "PW": _sb(2 * Q, BF), "s0c": _sb(Q, F32),
     "OH": _sb(20 * C, BF), "OHq": _sb(5 * C, X4), "OHs": _sb(5 * C, U8), "ab": _sb(4 * C, BF),
-    "cb": _sb(C, BF), "ge": _sb(C, BF), "junk": _sb(C, BF), "cnt": _sb(C, F32), "eq": _sb(C, BF), "pf": _sb(C, BF),
-    "AC": _sb(8, F32), "hf": _sb(32, F32), "gm": _sb(32, F32), "bc": _sb(32, F32), "RW": _sb(34, F32), "MB": _sb(34, F32), "SC": _sb(34, F32),
+    "cb": _sb(C, BF), "junk": _sb(C, BF), "junk2": _sb(C, BF), "cnt": _sb(C, F32), "eq": _sb(C, BF), "pf": _sb(C, BF),
+    "AC": _sb(8, F32), "hf": _sb(32, F32), "gm0": _sb(32, F32), "gm": _sb(32, F32), "bc": _sb(32, F32),
+    "RW": _sb(34, F32), "MB": _sb(34, F32), "SC": _sb(34, F32),
     "offH": _sb(2, U16), "tie": _sb(16, F32), "KY": _sb(17, F32), "DK": _sb(17, F32), "dk1": _sb(17, F32), "dk2": _sb(17, F32), "OW": _sb(17, F32),
-    "tr0": _sb(128, F32), "tabR": _sb(128, F32), "r0": _sb(128, F32), "rm32": _sb(128, F32),
-    "O": _sb(128, F32), "OT": _sb(128, F32), "OS": _sb(128, F32), "offB": _sb(4, U16),
+    "tr0": _sb(128, F32), "tabR": _sb(128, BF), "r0": _sb(128, F32), "rm32": _sb(128, BF),
+    "O": _sb(128, BF), "OT": _sb(128, BF), "OS": _sb(128, BF), "offB": _sb(4, U16),
     "Bt": _sb(512, BF), "h64": _sb(64, F32), "HL": _sb(R * H, F32),
     "F": _sb(512, BF), "U": _sb(UB + 4 * C, BF), "off0": _sb(Q, U16), "off1": _sb(Q, U16), "offM": _sb(Q, U16),
     "ix0": _sb(Q, F32), "offX": _sb(Q, U16), "cf0": _sb(Q, F32), "cfr": _sb(Q, F32), "sel2": _sb(Q, F32), "sf": _sb(Q, F32),
@@ -248,12 +249,12 @@ def rank_program(g, core, T, topo):
         return [p + str(i) for i in range(n)]
 
     XA = names("X0", 4) + names("X1", 4)
-    cQ, cT, cU, cHB, cTAU, cNS, cT576, cT128, cMB, cHM, cNH = range(11)
+    cQ, cT, cU, cHB, cS2, cNS, cT576, cT128, cMB, cHM, cNH, cN2 = range(12)
     cCM, cDM, cE, cEB = 12, 16, 20, 24
 
-    dma("S", T.c1s[:], T.c1[:], [], ["c1s"])
     dma("Y", T.X[:], T.x[:], [], XA)
-    dma("S", T.c2s[:], T.c2[:], [], ["c2s"])
+    dma("S", T.c1s[:], T.c1[:], [], ["c1s"])
+    dma("Y", T.c2s[:], T.c2[:], [], ["c2s"])
     dma("Y", T.Wq[:].bitcast(dt.uint8), T.wc[:], [], ["Wq"])
     dma("Y", T.Ws[:], T.ws[:], [], ["Ws"])
     dma("Y", T.vt[:], T.v[:], [], ["vt"])
@@ -282,12 +283,13 @@ def rank_program(g, core, T, topo):
     ts(T.CF[:, cE:cE + 4], T.IO[:, 0:4], col(cT), 1.0 / BIG, A.is_gt, A.mult, ["IO", "cf"], ["e"])
     ts(T.CF[:, cEB:cEB + 4], T.IO[:, 0:4], col(cT), BIG, A.is_gt, A.mult, ["IO", "cf"], ["eb"])
     ms(T.Kt[:, 0:48], 0.0, ["Kta"])
-    ms(T.RW[:, 33:34], 0.0, ["RWc"])
+    ms(T.RW[:, 33:34], -float(C), ["RWc"])
     ms(T.MB[:, 0:1], 0.0, ["MBa"])
     ms(T.KY[:, 16:17], 0.0, ["KYb"])
     act(T.U[:, 4 * C:4 * C + 512], T.one[:], AF.Copy, ["one"], ["Ug0"])
     act(T.U[:, 4 * C + 512:UB], T.one[:, 0:UB - 4 * C - 512], AF.Copy, ["one"], ["Ug1"])
-    act(col(cTAU), col(cQ), AF.Identity, ["cf"], ["tau"], bias=0.5 - H)
+    act(col(cS2), col(cQ), AF.Identity, ["cf"], ["s2"], scale=2.0, bias=-float(C))
+    act(col(cN2), col(cQ), AF.Identity, ["cf"], ["n2"], scale=-2.0, bias=C - 1.0)
     act(col(cNS), col(cQ), AF.Identity, ["cf"], ["ns"], scale=-1.0, bias=-0.5)
     act(col(cT576), col(cT), AF.Identity, ["cf"], ["t576"], bias=float(2 * C))
     act(col(cT128), col(cT), AF.Identity, ["cf"], ["t128"], scale=float(N * H))
@@ -315,12 +317,12 @@ def rank_program(g, core, T, topo):
     for t in range(4):
         ts(T.offP[:, 36 * t:36 * t + 36], T.c1s[:], 4, t, A.mult, A.add, ["c1s"], ["offP%d" % t])
     act(T.LA[:], T.ioP[:].indirect(T.offc[:]), AF.Copy, IOP + ["offc"], ["LA"])
+    cp(T.X2[:], T.X[:], XA, ["X20", "X21"])
     for k in range(2):
         for u in range(4):
             act(T.PA[:, C * k + u:C * k + C:4], T.LA[:, C * k + Q * u:C * k + Q * u + Q], AF.Copy, ["LA", "cm"], ["PA%d%d" % (k, u)], scale=col(cCM + u))
     for t in range(4):
         act(T.D0[:, 2 * t:2 * Q:8], T.IO[:, 0:NP], AF.Identity, ["IO", "eb"], ["D0e%d" % t], scale=0.0, bias=col(cEB + t))
-    cp(T.X2[:], T.X[:], XA, ["X20", "X21"])
 
     plan = _plan(T, topo, rank)
     sent = [0]
@@ -353,45 +355,56 @@ def rank_program(g, core, T, topo):
         if halves:
             for h in range(2):
                 qz("Zq", "Zs", base + PAD + h * HC, base + PAD + (h + 1) * HC,
-                   T.Z[:, 4 * C * k + 2 * C * h:4 * C * k + 2 * C * (h + 1)], zr, ["Zq%d%d" % (k, h)])
+                   T.Z[:, 4 * C * k + 2 * C * h:4 * C * k + 2 * C * (h + 1)], zr if halves == 2 else zr[2 * h:2 * h + 2], ["Zq%d%d" % (k, h)])
         else:
             qz("Zq", "Zs", base + PAD, base + ZW, T.Z[:, 4 * C * k:4 * C * (k + 1)], zr, ["Zq%d0" % k, "Zq%d1" % k])
         for u in range(4):
             mm(k, 128, "Kq", "Ks", 12 - 4 * u, "Zq", "Zs", base + Q * u, u == 0, u == 3,
                ["Kq", "Zpad%d" % k, "Zq%d0" % k] + (["Zq%d1" % k] if u >= 2 else []))
 
+    def zhalf(k, c, win, off, a, other, r):
+        tt(T.Z[:, 4 * C * k + 2 * C * c:4 * C * k + 2 * C * (c + 1)], win[:].indirect(off[:, a + 36 * c:a + 36 * c + 36]),
+           other[:, 2 * C * c:2 * C * (c + 1)], A.mult, r, ["Z%d%d" % (k, 2 * c), "Z%d%d" % (k, 2 * c + 1)])
+
+    def zplane(k, e):
+        tt(T.Z[:, 4 * C * k + e:4 * C * (k + 1):4], T.X[:].indirect(T.offP[:, 36 * e + 18 * k:36 * e + 18 * k + 18]),
+           T.X2[:, e:4 * C:4], A.mult, XA + ["X20", "X21", "offP%d" % e], ["Z%d%d" % (k, e)])
+
+    def keep_s0():
+        act(T.s0c[:], T.ps0[:, PAD:128], AF.Copy, [], ["s0c", "ps0"])
+
     for t in range(R):
         first, last = t == 0, t == R - 1
-        for k in range(2):
-            if first:
-                for e in range(4):
-                    tt(T.Z[:, 4 * C * k + e:4 * C * (k + 1):4], T.X[:].indirect(T.offP[:, 36 * e + 18 * k:36 * e + 18 * k + 18]),
-                       T.X2[:, e:4 * C:4], A.mult, XA + ["X20", "X21", "offP%d" % e], ["Z%d%d" % (k, e)])
-            elif k == 0:
-                for c in range(2):
-                    tt(T.Z[:, 2 * C * c:2 * C * (c + 1)], T.X[:].indirect(T.offW[:, 36 * c:36 * c + 36]), T.X2[:, 2 * C * c:2 * C * (c + 1)],
-                       A.mult, XA + ["X2%d" % c, "offW"], ["Z0%d" % (2 * c), "Z0%d" % (2 * c + 1)])
-            else:
-                tt(T.Z[:, 4 * C:8 * C], T.X[:].indirect(T.offW[:, Q:2 * Q]), T.X2[:], A.mult, XA + ["X20", "X21", "offW"], names("Z1", 4))
-            if first and k == 0:
-                qz("Kq", "Ks", 0, 140, T.Kt[:], ["Kta", "Ktb"], ["Kq"])
-            scores(k, k == 1)
-            if first and k == 0:
-                scan(T.SA[:], T.rm4[:, 0:2 * C], T.PA[:], 0.0, A.mult, A.add, ["rm4"] + names("PA0", 4) + names("PA1", 4), ["SA"])
-                tt(T.dQ[:], T.SA[:, C + 3:2 * C:4], T.SA[:, 3:C:4], A.subtract, ["SA"], ["dQ"])
-                act(T.LR[:], T.ioR[:].indirect(T.offc[:]), AF.Copy, ["ioR", "offc"], ["LR"])
-                for e in range(4):
-                    act(T.D1[:, 2 * e + 1:2 * Q:8], T.SA[:, 4 * e + 3:C:16], AF.Copy, ["SA", "dm"], ["D1o%d" % e], scale=col(cDM + e))
-                for e in range(4):
-                    act(T.D0[:, 2 * e + 1:2 * Q:8], T.dQ[:, e:Q:4], AF.Identity, ["dQ", "dm", "e"], ["D0o%d" % e], scale=col(cDM + e), bias=col(cE + e))
-            if k == 0:
-                act(T.s0c[:], T.ps0[:, PAD:128], AF.Copy, [], ["s0c", "ps0"])
         if first:
-            act(T.gm[:], T.hf[:], AF.Abs, ["hf", "hm"], ["gm"], bias=col(cHM))
+            for e in range(4):
+                zplane(0, e)
+            scan(T.SA[:], T.rm4[:, 0:2 * C], T.PA[:], 0.0, A.mult, A.add, ["rm4"] + names("PA0", 4) + names("PA1", 4), ["SA"])
+            qz("Kq", "Ks", 0, 140, T.Kt[:], ["Kta", "Ktb"], ["Kq"])
+            scores(0, 0)
+            tt(T.dQ[:], T.SA[:, C + 3:2 * C:4], T.SA[:, 3:C:4], A.subtract, ["SA"], ["dQ"])
+            act(T.LR[:], T.ioR[:].indirect(T.offc[:]), AF.Copy, ["ioR", "offc"], ["LR"])
+            for e in range(4):
+                act(T.D1[:, 2 * e + 1:2 * Q:8], T.SA[:, 4 * e + 3:C:16], AF.Copy, ["SA", "dm"], ["D1o%d" % e], scale=col(cDM + e))
+            for e in range(4):
+                act(T.D0[:, 2 * e + 1:2 * Q:8], T.dQ[:, e:Q:4], AF.Identity, ["dQ", "dm", "e"], ["D0o%d" % e], scale=col(cDM + e), bias=col(cE + e))
+            keep_s0()
+            for e in range(4):
+                zplane(1, e)
             qz("ONq", "ONs", 0, 128, T.ONt[:], ["ONt"], ["ONq"])
+            scores(1, 2)
+            act(T.gm0[:], T.hf[:], AF.Abs, ["hf", "hm"], ["gm0"], bias=col(cHM))
+            act(T.gm[:], T.gm0[:], AF.Identity, ["gm0"], ["gm"], scale=1000.0 + C, bias=-float(C))
             cp(T.offd[:], T.c2s[:], ["c2s"], ["offd"])
             ts(T.dk1[:], T.IO[:, 0:17], col(cQ), -10000.0, A.is_equal, A.mult, ["IO", "cf"], ["dk1"])
             ts(T.dk2[:], T.IO[:, 0:17], col(cQ), 1.0, A.subtract, A.is_equal, ["IO", "cf"], ["dk2"])
+        else:
+            zhalf(0, 0, T.X, T.offW, 0, T.X2, XA + ["X20", "offW"])
+            zhalf(0, 1, T.X, T.offW, 0, T.X2, XA + ["X21", "offW"])
+            zhalf(1, 0, T.X, T.offW, Q, T.X2, XA + ["X20", "offW"])
+            scores(0, 0)
+            keep_s0()
+            zhalf(1, 1, T.X, T.offW, Q, T.X2, XA + ["X21", "offW"])
+            scores(1, 1)
         tt(T.D1[:, 0:2 * Q:2], T.ps1[:, PAD:128], T.s0c[:], A.is_gt, ["s0c"], ["D1e", "ps1"])
         scan(T.PW[:], T.D0[:], T.D1[:], 0.0, A.mult, A.add, ["D1e"] + names("D1o", 4) + names("D0o", 4) + names("D0e", 4), ["PW"])
         for e in range(4):
@@ -399,10 +412,9 @@ def rank_program(g, core, T, topo):
             act(T.ab[:, e:4 * C:4], T.ioP[:], AF.Abs, IOP + ["PW"], ["ab%d" % e], scale=-1.0, bias=T.PW[:, 8 * r + 7:8 * r + 8])
         act(T.OH[:, 12 * C:16 * C], T.ab[:], AF.Relu, names("ab", 4), ["OH3"], scale=-1.0, bias=1.0)
         if first:
-            act(T.LB[:, 0:C], T.tabF[:].indirect(T.offd[:]), AF.Copy, ["tabFa", "tabFb", "offd"], ["LB0"])
-            act(T.LB[:, C:3 * C], T.LB[:, 0:C].indirect(T.offc[:]), AF.Copy, ["LB0", "offc"], ["LB1"])
             act(T.tabR[:], T.tr0[:], AF.Identity, names("tr0", 4) + ["nh"], ["tabR"], bias=col(cNH))
             act(T.rm32[:], T.r0[:], AF.Sign, ["r0"], ["rm32"])
+            act(T.LB[:, 0:C], T.tabF[:].indirect(T.offd[:]), AF.Copy, ["tabFa", "tabFb", "offd"], ["LB0"])
 
         def planes(i):
             for e in range(4 if i < 4 else 2):
@@ -422,29 +434,30 @@ def rank_program(g, core, T, topo):
         count(1, False, False)
         planes(4)
         count(2, False, False)
-        count(4, False, False)
-        count(3, False, True)
         if first:
             ts(T.dk2[:, 16:17], T.dk2[:, 16:17], -1.0, None, A.add, None, ["dk2"], ["dk2"])
+        count(4, False, False)
+        if first:
             ts(T.dk2[:], T.dk2[:], 1024.0, None, A.mult, None, ["dk2"], ["dk2"])
+        count(3, False, True)
+        if first:
             tt(T.DK[:], T.dk1[:], T.dk2[:], A.add, ["dk1", "dk2"], ["DK"])
-        ts(T.cb[:], T.ps2[:, 0:C], H + 1.0, H + 0.5, A.min, A.subtract, [], ["cb", "ps2"])
-        ts(T.ge[:], T.cb[:], col(cTAU), None, A.is_ge, None, ["cb", "tau"], ["ge"])
-        act(T.junk[:], T.cb[:], AF.Relu, ["cb"], ["junk", "RWb"], bias=0.5, accum_out=T.RW[:, 32:33])
-        act(T.cnt[:], T.ps2[:, 0:C], AF.Copy, [], ["cnt", "ps2"])
-        op("V", lambda: V.tensor_reduce(ac(0), T.ge[:], AxisListType.X, A.add), ["ge"], ["ac0"])
-        ts(T.bc[:], T.gm[:], ac(0), None, A.mult, None, ["gm", "ac0"], ["bc"])
+        act(T.junk[:], T.ps2[:, 0:C], AF.Sign, ["ns"], ["junk", "ac0", "ps2"], bias=col(cNS), accum_out=ac(0))
+        act(T.junk2[:], T.ps2[:, 0:C], AF.Sign, [], ["junk2", "RWb", "ps2"], bias=-(H + 0.5), accum_out=T.RW[:, 32:33])
+        ts(T.bc[:], T.gm[:], ac(0), None, A.min, None, ["gm", "ac0"], ["bc"])
         op("V", lambda: V.transpose(T.RW[:, 0:32], T.bc[:]), ["bc"], ["RWa"])
-        act(T.junk[:, 0:33], T.RW[:, 0:33], AF.Sign, ["RWa", "RWb", "ns"], ["junk", "ac1"], bias=col(cNS), accum_out=ac(1))
-        ts(T.MB[:, 1:34], T.RW[:, 0:33], col(cQ), None, A.is_le, None, ["RWa", "RWb", "cf"], ["MBb"])
-        scan(T.SC[:], T.MB[:], T.RW[:], 0.0, A.mult, A.max, ["MBa", "MBb", "RWa", "RWb", "RWc"], ["SC"])
+        act(T.junk[:, 0:33], T.RW[:, 0:33], AF.Sign, ["RWa", "RWb", "n2"], ["junk", "ac1"], bias=col(cN2), accum_out=ac(1))
+        ts(T.MB[:, 1:34], T.RW[:, 0:33], col(cS2), -1000.0, A.is_gt, A.mult, ["RWa", "RWb", "s2"], ["MBb"])
+        ts(T.cb[:], T.ps2[:, 0:C], H + 1.0, H + 0.5, A.min, A.subtract, [], ["cb", "ps2"])
+        act(T.cnt[:], T.ps2[:, 0:C], AF.Copy, [], ["cnt", "ps2"])
+        scan(T.SC[:], T.MB[:], T.RW[:], -float(C), A.add, A.max, ["MBa", "MBb", "RWa", "RWb", "RWc"], ["SC"])
         ts(T.eq[:], T.cb[:], 2.0, ac(1), A.mult, A.is_equal, ["cb", "ac1"], ["eq"])
-        scan(T.pf[:], T.eq[:], T.eq[:], T.SC[:, 33:34], A.add, A.max, ["eq", "SC"], ["pf"])
-        act(T.junk[:], T.pf[:], AF.Sign, ["pf", "ns"], ["junk", "ac2"], bias=col(cNS), accum_out=ac(2))
+        scan(T.pf[:], T.eq[:], T.eq[:], T.SC[:, 33:34], A.add, A.add, ["eq", "SC"], ["pf"])
+        act(T.junk[:], T.pf[:], AF.Sign, ["pf", "n2"], ["junk", "ac2"], bias=col(cN2), accum_out=ac(2))
         ts(T.offH[:, 0:1], ac(2), -0.5, C / 2.0, A.mult, A.add, ["ac2"], ["offH"])
         tt(T.KY[:, 0:H], T.cnt[:].indirect(T.offH[:, 0:1]), T.tie[:], A.add, ["cnt", "offH", "tie"], ["KYa"])
         scan(T.OW[:], T.DK[:], T.KY[:], 0.0, A.add, A.max, ["DK", "KYa", "KYb"], ["OW"])
-        act(T.junk[:, 0:H], T.KY[:, 0:H], AF.Sign, ["KYa", "OW"], ["junk", "ac3"], scale=-1.0, bias=T.OW[:, 16:17], accum_out=ac(3))
+        act(T.junk2[:, 0:H], T.KY[:, 0:H], AF.Sign, ["KYa", "OW"], ["junk2", "ac3"], scale=-1.0, bias=T.OW[:, 16:17], accum_out=ac(3))
         ts(T.O[:], T.tabR[:], ac(3), ac(2), A.is_equal, A.mult, ["tabR", "ac3", "ac2"], ["O"])
         op("V", lambda: V.transpose(T.OT[:], T.O[:]), ["O"], ["OT"])
         scan(T.OS[:], T.rm32[:], T.OT[:], 0.0, A.mult, A.add, ["rm32", "OT"], ["OS"])
@@ -456,6 +469,7 @@ def rank_program(g, core, T, topo):
         if first:
             iota(T.tabH[:], [[1, C], [0, 4]], 0, 0, ["tabH"])
             ts(T.offX[:], T.ix0[:], col(cMB), None, A.add, None, ["ix0", "mb"], ["offX"])
+            act(T.LB[:, C:3 * C], T.LB[:, 0:C].indirect(T.offc[:]), AF.Copy, ["LB0", "offc"], ["LB1"])
             for k in range(3):
                 for u in range(4):
                     act(T.PB[:, C * k + u:C * k + C:4], T.LB[:, C * k + Q * u:C * k + Q * u + Q], AF.Copy, ["LB0", "LB1", "cm"],
@@ -465,6 +479,7 @@ def rank_program(g, core, T, topo):
         ts(T.Xh[:], T.X[:], 0.5, None, A.mult, None, XA, ["Xh"])
         if first:
             ts(T.cfr[:], T.cf0[:], 4.0 / UB, None, A.mult, None, ["cf0"], ["cfr"])
+            qz("Vq", "Vs", 0, 128, T.vt[:], ["vt"], ["Vq"])
             scan(T.SB[:], T.rm4[:], T.PB[:], 0.0, A.mult, A.add, ["rm4"] + names("PB0", 4) + names("PB1", 4) + names("PB2", 4), ["SB"])
             tt(T.dg[:], T.SB[:, 2 * C + 3:3 * C:4], T.SB[:, C + 3:2 * C:4], A.subtract, ["SB"], ["dg"])
             for u in range(4):
@@ -476,7 +491,6 @@ def rank_program(g, core, T, topo):
         if first:
             for u in range(4):
                 act(T.PR[:, u:2 * C:4], T.LR[:, u:2 * C:4], AF.Copy, ["LR", "cm"], ["PR%d" % u], scale=col(cCM + u))
-            qz("Vq", "Vs", 0, 128, T.vt[:], ["vt"], ["Vq"])
             scan(T.SR[:], T.rm4[:, 0:2 * C], T.PR[:], 0.0, A.mult, A.add, ["rm4"] + names("PR", 4), ["SR"])
             ts(T.offW[:], T.SR[:, 3:2 * C:4], 4.0, col(cT576), A.mult, A.add, ["SR", "t576"], ["offW"])
         act(T.h64[:], T.tabH[:].indirect(T.offB[:]), AF.Copy, ["tabH", "offB"], ["h64"])
@@ -487,7 +501,7 @@ def rank_program(g, core, T, topo):
             mm(4 + b, 128, "Eq", "Es", 128 * b, "Fq%d" % t, "Fs%d" % t, 0, True, True, ["Eq", "Fown%d" % t],
                pre=[("arr%d" % t, arrivals)] if b == 0 else ())
         for b in range(4):
-            if b % 2 == 0:
+            if b % 2 == 1:
                 cp(T.F[:, 128 * b:128 * b + 128], T["ps%d" % (4 + b)][:, 0:128], [], ["F%d" % b, "ps%d" % (4 + b)])
             else:
                 act(T.F[:, 128 * b:128 * b + 128], T["ps%d" % (4 + b)][:, 0:128], AF.Copy, [], ["F%d" % b, "ps%d" % (4 + b)])
@@ -495,9 +509,12 @@ def rank_program(g, core, T, topo):
         for k in range(2):
             o = "off%d" % k
             act(T.U[:, UB * k:UB * k + 4 * C], T.F[:].indirect(T[o][:]), AF.Copy, FA + names(o, 4), ["U%d" % k], scale=0.5)
-            tt(T.Z[:, 4 * C * k:4 * C * (k + 1)], T.F[:].indirect(T[o][:]), T.Xp[:], A.mult, FA + names(o, 4) + ["Xp"], names("Z%d" % k, 4))
-            scores(k, k == 1)
-        act(T.s0c[:], T.ps0[:, PAD:128], AF.Copy, [], ["s0c", "ps0"])
+        tt(T.Z[:, 0:4 * C], T.F[:].indirect(T.off0[:]), T.Xp[:], A.mult, FA + names("off0", 4) + ["Xp"], names("Z0", 4))
+        zhalf(1, 0, T.F, T.off1, 0, T.Xp, FA + names("off1", 4) + ["Xp"])
+        scores(0, 0)
+        zhalf(1, 1, T.F, T.off1, 0, T.Xp, FA + names("off1", 4) + ["Xp"])
+        scores(1, 1)
+        keep_s0()
         tt(T.sel2[:], T.ps1[:, PAD:128], T.s0c[:], A.is_gt, ["s0c"], ["sel2", "ps1"])
         tt(T.sf[:], T.sel2[:], T.cfr[:], A.add, ["sel2", "cfr"], ["sf"])
         for u in range(4):
@@ -513,24 +530,33 @@ def rank_program(g, core, T, topo):
 
         def finish(c):
             if not last:
-                act(T.X2[:, 2 * C * c:2 * C * (c + 1)], T.X[:, 2 * C * c:2 * C * (c + 1)], AF.Copy, names("X%d" % c, 4), ["X2%d" % c])
+                if c == 0:
+                    cp(T.X2[:, 0:2 * C], T.X[:, 0:2 * C], names("X0", 4), ["X20"])
+                else:
+                    act(T.X2[:, 2 * C:4 * C], T.X[:, 2 * C:4 * C], AF.Copy, names("X1", 4), ["X21"])
                 return
             qz("Xq", "Xs", HC * c, HC * c + HC, T.X[:, 2 * C * c:2 * C * (c + 1)], names("X%d" % c, 4), ["Xq%d" % c])
             mm(4 + c, HC, "Vq", "Vs", 0, "Xq", "Xs", HC * c, True, True, ["Vq", "Xq%d" % c])
             dma("Y", T.oc[:, 2 * C * c:2 * C * (c + 1)], T.Xq[:, HC * c:HC * c + HC].bitcast(dt.uint8), ["Xq%d" % c], [])
 
-        for c in range(2):
-            tt(T.Mt[:, 2 * C * c:2 * C * (c + 1)], T.U[:].indirect(T.offM[:, 2 * NP * c:2 * NP * (c + 1)]), T.Xh[:, 2 * C * c:2 * C * (c + 1)],
-               A.add, ["U0", "U1", "Ug0", "Ug1", "Xh", "offM%d" % (2 * c), "offM%d" % (2 * c + 1)], ["Mt%d" % c])
-            qz("Mq", "Ms", HC * c, HC * c + HC, T.Mt[:, 2 * C * c:2 * C * (c + 1)], ["Mt%d" % c], ["Mq%d" % c])
+        def mix(a, b, r, w):
+            tt(T.Mt[:, C * a:C * b], T.U[:].indirect(T.offM[:, NP * a:NP * b]), T.Xh[:, C * a:C * b], A.add, ["U0", "U1", "Ug0", "Ug1", "Xh"] + r, w)
+
+        def layer(c, r):
+            qz("Mq", "Ms", HC * c, HC * c + HC, T.Mt[:, 2 * C * c:2 * C * (c + 1)], r, ["Mq%d" % c])
             for b in range(4):
                 mm(4 * (1 - c) + b, HC, "Wq", "Ws", 128 * b, "Mq", "Ms", HC * c, True, True, ["Wq", "Ws", "Mq%d" % c])
-            if c == 0:
-                for b in range(4):
-                    evac(0, b, "S")
+
+        mix(0, 2, ["offM0", "offM1"], ["Mt0"])
+        mix(2, 3, ["offM2"], ["Mt1"])
+        layer(0, ["Mt0"])
+        for b in range(4):
+            evac(0, b, "S")
+        mix(3, 4, ["offM3"], ["Mt2"])
+        layer(1, ["Mt1", "Mt2"])
         finish(0)
         for b in range(4):
-            evac(1, b, "VS"[b % 2])
+            evac(1, b, "SV"[b % 2])
         finish(1)
         if last:
             act(T.Y[:, 0:HC], T.ps4[:, 0:HC], AF.Copy, [], ["Y0", "ps4"])

@@ -4,15 +4,22 @@ from concourse.mybir import dt, AluOpType, ActivationFunctionType
 A = AluOpType
 AF = ActivationFunctionType
 C, H, R, N = 288, 16, 3, 8
-Q = C // 4
-PAD = 128 - Q
-ZW = PAD + C
-NP = C // 16
 HC = C // 2
-UB = 2048
+BASE, NH = (0, 160), (160, 128)
+QH = (40, 32)
+MO = (0, 40)
+NM = 72
+PAD = 128 - QH[0]
+ZC = {(0, 1): 0, (0, 0): 160, (1, 1): 320, (1, 0): 448}
+SW = C + 2
 FW = 2 * N * H - H
 OWN = (N - 1) * H
 BIG = 4096.0
+KP, KN, OP, ON = 0, 140, 280, 408
+
+SCALAR_GATHERS = True
+WORDS = [("S", [(0, 0), (0, 1), (0, 2), (0, 3)]), ("V", [(0, 4), (0, 5), (0, 6), (0, 7)]), ("V", [(0, 8), (0, 9)]),
+         ("V", [(1, 4), (1, 5), (1, 6), (1, 7)]), ("S", [(1, 0), (1, 1), (1, 2), (1, 3)])]
 
 DIRECT_CODES = 3
 DIRECT_SCALES = 4
@@ -27,36 +34,38 @@ def _sb(n, d):
 
 SCRATCH = {
     "X": _sb(4 * C, BF), "X2": _sb(4 * C, BF), "Xh": _sb(4 * C, BF), "Xp": _sb(4 * C, BF), "Z": _sb(8 * C, BF),
-    "Zq": _sb(2 * ZW, X4), "Zs": _sb(2 * ZW, U8),
+    "Zq": _sb(PAD + 2 * C, X4), "Zs": _sb(PAD + 2 * C, U8),
     "c1s": _sb(36, I32), "c2s": _sb(18, I32), "vt": _sb(512, BF), "Vq": _sb(128, X4), "Vs": _sb(128, U8),
     "Wq": _sb(512, X4), "Ws": _sb(512, U8),
-    "pci": _sb(1, I32), "ci": _sb(4, I32), "CF": _sb(32, F32), "IO": _sb(32, F32),
-    "one": _sb(512, BF), "ONt": _sb(512, BF), "ONq": _sb(128, X4), "ONs": _sb(128, U8),
-    "Kt": _sb(560, BF), "Kq": _sb(140, X4), "Ks": _sb(140, U8),
-    "Et": _sb(2048, BF), "Eq": _sb(512, X4), "Es": _sb(512, U8),
-    "ioP": _sb(C, BF), "ioR": _sb(C, BF), "tabF": _sb(128, BF), "tabH": _sb(4 * C, F32), "rm4": _sb(3 * C, BF),
+    "pci": _sb(1, I32), "ci": _sb(5, I32), "CF": _sb(32, F32), "IO": _sb(32, F32), "IO4": _sb(NM, F32), "En": _sb(NM, F32),
+    "one": _sb(516, BF), "KI": _sb(512, BF), "KJ": _sb(512, BF), "Ct": _sb(4 * 536, BF), "Cq": _sb(536, X4), "Cs": _sb(536, U8),
+    "Et": _sb(516, BF), "Eq": _sb(512, X4), "Es": _sb(512, U8),
+    "ioN": _sb(C, BF), "ioV": _sb(C, BF), "ioS": _sb(SW, F32), "ioR": _sb(C, BF), "ioF": _sb(C, F32), "tabF": _sb(128, BF),
+    "rm4": _sb(3 * C, BF), "IM": _sb(2 * C, BF), "MK": _sb(2 * C, BF), "MU": _sb(2 * C, BF), "PI": _sb(36, F32), "offQ": _sb(36, U16),
     "offP": _sb(144, U16), "offW": _sb(144, U16), "offc": _sb(36, U16), "offd": _sb(18, U16),
-    "LA": _sb(2 * C, BF), "PA": _sb(2 * C, BF), "SA": _sb(2 * C, BF), "dQ": _sb(Q, F32),
+    "LA": _sb(2 * C, BF), "SA": _sb(2 * C, BF), "dQ": _sb(NM, F32),
     "LR": _sb(2 * C, BF), "PR": _sb(2 * C, BF), "SR": _sb(2 * C, BF),
-    "LB": _sb(3 * C, BF), "PB": _sb(3 * C, BF), "SB": _sb(3 * C, BF), "dg": _sb(Q, F32), "t1": _sb(Q, F32), "t2": _sb(Q, F32),
-    "D0": _sb(2 * Q, F32), "D1": _sb(2 * Q, F32), "PW": _sb(2 * Q, BF), "s0c": _sb(Q, F32),
-    "OH": _sb(20 * C, BF), "OHq": _sb(5 * C, X4), "OHs": _sb(5 * C, U8), "ab": _sb(4 * C, BF),
+    "LB": _sb(3 * C, BF), "PB": _sb(3 * C, BF), "SB": _sb(3 * C, BF),
+    "dg": _sb(NM, F32), "t1": _sb(NM, F32), "t2": _sb(NM, F32),
+    "D0": _sb(2 * NM, F32), "D1": _sb(2 * NM, F32), "PW": _sb(2 * NM, BF),
+    "OH": _sb(20 * SW, BF), "OHq": _sb(5 * SW, X4), "OHs": _sb(5 * SW, U8),
     "cb": _sb(C, BF), "junk": _sb(C, BF), "junk2": _sb(C, BF), "cnt": _sb(C, F32), "eq": _sb(C, BF), "pf": _sb(C, BF),
-    "AC": _sb(8, F32), "hf": _sb(32, F32), "gm0": _sb(32, F32), "gm": _sb(32, F32), "bc": _sb(32, F32),
+    "AC": _sb(8, F32), "gm": _sb(32, F32), "bc": _sb(32, F32),
     "RW": _sb(34, F32), "MB": _sb(34, F32), "SC": _sb(34, F32),
-    "offH": _sb(2, U16), "tie": _sb(16, F32), "KY": _sb(17, F32), "DK": _sb(17, F32), "dk1": _sb(17, F32), "dk2": _sb(17, F32), "OW": _sb(17, F32),
-    "tr0": _sb(128, F32), "tabR": _sb(128, BF), "r0": _sb(128, F32), "rm32": _sb(128, BF),
-    "O": _sb(128, BF), "OT": _sb(128, BF), "OS": _sb(128, BF), "offB": _sb(4, U16),
-    "Bt": _sb(512, BF), "h64": _sb(64, F32), "HL": _sb(R * H, F32),
-    "F": _sb(512, BF), "U": _sb(UB + 4 * C, BF), "off0": _sb(Q, U16), "off1": _sb(Q, U16), "offM": _sb(Q, U16),
-    "ix0": _sb(Q, F32), "offX": _sb(Q, U16), "cf0": _sb(Q, F32), "cfr": _sb(Q, F32), "sel2": _sb(Q, F32), "sf": _sb(Q, F32),
+    "offH": _sb(2, U16), "offR": _sb(2, U16), "offG": _sb(4, U16), "offS": _sb(4, U16), "kG": _sb(4, F32), "kS": _sb(4, F32),
+    "tie": _sb(16, F32), "KY": _sb(17, F32), "DK": _sb(17, F32), "dk2": _sb(17, F32), "OW": _sb(17, F32),
+    "Bu": _sb(64, BF), "Bt": _sb(512, BF), "h16": _sb(16, F32), "HL": _sb(R * H, F32),
+    "F": _sb(512, BF), "U0": _sb(8 * NH[0], BF), "U1": _sb(8 * NH[1], BF),
+    "off0": _sb(80, U16), "off1": _sb(80, U16), "offM": _sb(NM, U16), "offX": _sb(NM, U16),
+    "ix0": _sb(80, F32), "ixr": _sb(80, F32), "sel2": _sb(NM, F32), "sf": _sb(80, F32),
+    "tp": _sb(80, F32), "tm": _sb(80, F32), "ts": _sb(80, F32), "offT": _sb(6, U16),
     "Mt": _sb(4 * C, BF), "Mq": _sb(C, X4), "Ms": _sb(C, U8), "Xq": _sb(C, X4), "Xs": _sb(C, U8), "Y": _sb(C, F32),
 }
 for _t in range(R):
     SCRATCH["Fq%d" % _t] = _sb(FW, X4)
     SCRATCH["Fs%d" % _t] = _sb(FW, U8)
-    SCRATCH["hq%d" % _t] = _sb(H, X4)
-    SCRATCH["hs%d" % _t] = _sb(H, U8)
+SCRATCH["hq"] = _sb(R * H, X4)
+SCRATCH["hs"] = _sb(R * H, U8)
 for _b in range(8):
     SCRATCH["ps%d" % _b] = ("psum", [128, 512], F32)
 
@@ -114,7 +123,7 @@ def _helper(g, core, T, topo):
             sent = 0
             for t in range(R):
                 g.wait_ge(T.sem["hin%d" % t], len(_feed_engines(T, topo, rank, core)))
-                tr, n = _spread(T, topo, core, rank, kind, t, _view(T, kind, "h%s%d" % (kind, t), 0, H), rest)
+                tr, n = _spread(T, topo, core, rank, kind, t, _view(T, kind, "h" + kind, H * t, H * t + H), rest)
                 g.remote_dma_fused([tr], local_sem=T.sem.sent)
                 sent += n
             g.wait_ge(T.sem.sent, sent)
@@ -249,80 +258,100 @@ def rank_program(g, core, T, topo):
         return [p + str(i) for i in range(n)]
 
     XA = names("X0", 4) + names("X1", 4)
-    cQ, cT, cU, cHB, cS2, cNS, cT576, cT128, cMB, cHM, cNH, cN2 = range(12)
-    cCM, cDM, cE, cEB = 12, 16, 20, 24
+    cQ, cT, cU, cHB, cG, cS2, cNS, cT576, cT128, cHM, cN2, cQT = range(12)
+    cCM, cPM, cMB, cNT = 12, 16, 18, 20
 
-    dma("Y", T.X[:], T.x[:], [], XA)
     dma("S", T.c1s[:], T.c1[:], [], ["c1s"])
-    dma("Y", T.c2s[:], T.c2[:], [], ["c2s"])
+    dma("Y", T.X[:], T.x[:], [], XA)
+    dma("S", T.X2[:, 0:4 * NH[0]], T.x[:, 0:4 * NH[0]], [], ["X20"])
+    dma("S", T.c2s[:], T.c2[:], [], ["c2s"])
+    dma("Y", T.X2[:, 4 * NH[0]:4 * C], T.x[:, 4 * NH[0]:4 * C], [], ["X21"])
     dma("Y", T.Wq[:].bitcast(dt.uint8), T.wc[:], [], ["Wq"])
     dma("Y", T.Ws[:], T.ws[:], [], ["Ws"])
     dma("Y", T.vt[:], T.v[:], [], ["vt"])
 
-    ms(T.one[:], 1.0, ["one"])
     iota(T.pci[:], [[0, 1]], 0, 1, ["pci"], flag=False)
     iota(T.IO[:], [[1, 32]], 0, 0, ["IO"])
-    iota(T.ioP[:, 0:HC], [[1, HC]], -HC, 0, ["ioPa"])
-    iota(T.ioP[:, HC:C], [[1, HC]], 1, 0, ["ioPb"])
-    IOP = ["ioPa", "ioPb"]
-    asel(T.ONt[:], T.one[:], [[-16, 8], [0, 64]], A.is_ge, 0, 1, ["one"], ["ONt"])
-    asel(T.ONt[:], T.ONt[:], [[16, 8], [0, 64]], A.is_ge, 15, -1, ["ONt"], ["ONt"])
-    asel(T.Kt[:, 48:560], T.ONt[:], [[0, 8], [-1, 64]], A.is_ge, 15, 0, ["ONt"], ["Ktb"])
+    iota(T.KI[:], [[1, 8], [100, 4], [0, 16]], 0, 0, ["KI"])
+    iota(T.PI[:], [[C, 2], [4, 18]], 0, 0, ["PI"])
+    iota(T.ioN[:, 0:HC], [[1, HC]], -HC, 0, ["ioNa"])
+    iota(T.ioN[:, HC:C], [[1, HC]], 1, 0, ["ioNb"])
+    iota(T.IO4[:], [[0, NM // 4], [1, 4]], 0, 0, ["IO4"])
+    iota(T.IM[:], [[0, 2 * C // 16], [1, 16]], 0, 0, ["IM"])
+    own = (rank + 1) * H
+    iota(T.tabF[:, 0:own], [[1, own]], N * H - own, 0, ["tabFa"])
+    if own < N * H:
+        iota(T.tabF[:, own:N * H], [[1, N * H - own]], 0, 0, ["tabFb"])
+    iota(T.ioS[:], [[1, HC + 1], [HC + 1, 2]], -HC - 1, 0, ["ioS"])
+    iota(T.KJ[:], [[1, 8], [0, 64]], 0, 0, ["KJ"])
+    iota(T.ioV[:], [[1, HC], [HC + 1, 2]], -HC, 0, ["ioV"])
+    iota(T.gm[:], [[1, 2], [0, 16]], 0, 0, ["gm"])
+    for i, (e, pts) in enumerate(WORDS):
+        for k in range(len(pts), 4):
+            iota(T.OH[:, 4 * SW * i + k:4 * SW * i + 4 * C:4], [[0, C]], 0, 0, ["OH%d%d" % (i, k)])
+    iota(T.one[:], [[0, 516]], 1, 0, ["one"])
+    asel(T.Et[:], T.one[:], [[-1, 516]], A.is_equal, 3, 4, ["one"], ["Et"])
+    for h in range(2):
+        iota(T.ix0[:, 48 * h:48 * h + QH[h]], [[4, 4], [16, QH[h] // 4]], 0, 0, ["ix0%d" % h])
+        iota(T.tp[:, 48 * h:48 * h + QH[h]], [[1, 4], [4, QH[h] // 4]], 0, 0, ["tp%d" % h])
+    iota(T.ix0[:, 40:48], [[0, 8]], 0, 0, ["ix02"])
+    iota(T.tp[:, 40:48], [[0, 8]], 0, 0, ["tp2"])
+    iota(T.ioR[:], [[1, C]], -HC, 0, ["ioR"])
+    iota(T.ioF[:], [[1, C]], 0, 0, ["ioF"])
+
     ms(T.Bt[:], 0.0, ["Bt"])
     ts(T.ci[:, 0:1], T.pci[:], 15, None, A.bitwise_and, None, ["pci"], ["ci0"])
     ts(T.ci[:, 1:2], T.pci[:], 3, None, A.bitwise_and, None, ["pci"], ["ci1"])
     ts(T.ci[:, 2:3], T.pci[:], 2, 3, A.logical_shift_right, A.bitwise_and, ["pci"], ["ci2"])
     ts(T.ci[:, 3:4], T.pci[:], 4, 1, A.logical_shift_right, A.bitwise_and, ["pci"], ["ci3"])
+    ts(T.ci[:, 4:5], T.pci[:], 4, None, A.logical_shift_right, None, ["pci"], ["ci4"])
     ms(T.rm4[:], 1.0, ["rm4"])
-    cp(T.CF[:, 0:4], T.ci[:], names("ci", 4), ["cf"])
-    for k in range(2):
-        qz("Zq", "Zs", k * ZW, k * ZW + 128, T.Bt[:], ["Bt"], ["Zpad%d" % k, "Zq%d0" % k])
+    cp(T.CF[:, 0:5], T.ci[:], names("ci", 5), ["cf"])
+    ms(T.Ct[:, 4 * KP:4 * KP + 48], 0.0, ["Kp0"])
     ms(T.rm4[:, 0:3 * C:4], 0.0, ["rm4"])
-    ts(T.CF[:, cCM:cCM + 4], T.IO[:, 0:4], col(cU), None, A.is_equal, None, ["IO", "cf"], ["cm"])
-    ts(T.CF[:, cDM:cDM + 4], T.IO[:, 0:4], col(cT), None, A.is_equal, None, ["IO", "cf"], ["dm"])
-    ts(T.CF[:, cE:cE + 4], T.IO[:, 0:4], col(cT), 1.0 / BIG, A.is_gt, A.mult, ["IO", "cf"], ["e"])
-    ts(T.CF[:, cEB:cEB + 4], T.IO[:, 0:4], col(cT), BIG, A.is_gt, A.mult, ["IO", "cf"], ["eb"])
-    ms(T.Kt[:, 0:48], 0.0, ["Kta"])
-    ms(T.RW[:, 33:34], -float(C), ["RWc"])
-    ms(T.MB[:, 0:1], 0.0, ["MBa"])
-    ms(T.KY[:, 16:17], 0.0, ["KYb"])
-    act(T.U[:, 4 * C:4 * C + 512], T.one[:], AF.Copy, ["one"], ["Ug0"])
-    act(T.U[:, 4 * C + 512:UB], T.one[:, 0:UB - 4 * C - 512], AF.Copy, ["one"], ["Ug1"])
-    act(col(cS2), col(cQ), AF.Identity, ["cf"], ["s2"], scale=2.0, bias=-float(C))
-    act(col(cN2), col(cQ), AF.Identity, ["cf"], ["n2"], scale=-2.0, bias=C - 1.0)
-    act(col(cNS), col(cQ), AF.Identity, ["cf"], ["ns"], scale=-1.0, bias=-0.5)
-    act(col(cT576), col(cT), AF.Identity, ["cf"], ["t576"], bias=float(2 * C))
-    act(col(cT128), col(cT), AF.Identity, ["cf"], ["t128"], scale=float(N * H))
-    act(col(cMB), col(cU), AF.Identity, ["cf"], ["mb"], scale=float(4 * Q), bias=col(cT))
-    act(col(cHM), col(cHB), AF.Identity, ["cf"], ["hm"], bias=-1.0)
-    act(col(cNH), col(cHB), AF.Identity, ["cf"], ["nh"], scale=-1000.0)
-    act(T.tie[:], T.IO[:, 0:H], AF.Identity, ["IO"], ["tie"], scale=-1.0 / H, bias=(H - 1.0) / H)
-    own = (rank + 1) * H
-    iota(T.ioR[:], [[1, C]], -HC, 0, ["ioR"])
-    iota(T.hf[:], [[1, 2], [0, 16]], 0, 0, ["hf"])
-    for e in range(2, 4):
-        iota(T.OH[:, 16 * C + e:20 * C:4], [[0, C]], 0, 0, ["OH4%d" % e])
-    iota(T.tabF[:, 0:own], [[1, own]], N * H - own, 0, ["tabFa"])
-    if own < N * H:
-        iota(T.tabF[:, own:N * H], [[1, N * H - own]], 0, 0, ["tabFb"])
-    for cc in range(4):
-        iota(T.tr0[:, 32 * cc:32 * cc + 32], [[1000, 2], [-2, 4], [0, 4]], H - 1 - 8 * cc, 0, ["tr0%d" % cc])
-    iota(T.r0[:], [[0, 4], [1, 32]], 0, 0, ["r0"])
-    iota(T.ix0[:], [[4, 4], [16, NP]], 0, 0, ["ix0"])
-    iota(T.cf0[:], [[1, Q]], 0, 0, ["cf0"])
-    for b in range(4):
-        asel(T.Et[:, 512 * b:512 * b + 512], T.one[:], [[-1, 512]], A.is_equal, b, 4, ["one"], ["Et%d" % b])
-
+    for h in range(2):
+        ts(col(cPM + h), col(cT), float(QH[h]), col(cU), A.mult, A.add, ["cf"], ["pm0%d" % h])
+    ms(T.Ct[:, 4 * KN:4 * KN + 48], 0.0, ["Kn0"])
+    ts(T.Ct[:, 4 * KP + 48:4 * KN], T.KI[:], col(cG), None, A.is_equal, None, ["KI", "cf"], ["Kp1"])
+    act(T.Ct[:, 4 * KN + 48:4 * OP], T.Ct[:, 4 * KP + 48:4 * KN], AF.Copy, ["Kp1"], ["Kn1"], scale=-1.0)
+    for k in range(2):
+        for h in range(2):
+            a, b = 18 * k + MO[h] // 4, 18 * k + (MO[h] + QH[h]) // 4
+            ts(T.offQ[:, a:b], T.PI[:, a:b], col(cPM + h), float(BASE[h] - MO[h]), A.add, A.add, ["PI", "pm0%d" % h], ["perm%d%d" % (k, h)])
+    PERM = names("perm0", 2) + names("perm1", 2)
     cp(T.offc[:], T.c1s[:], ["c1s"], ["offc"])
     for t in range(4):
         ts(T.offP[:, 36 * t:36 * t + 36], T.c1s[:], 4, t, A.mult, A.add, ["c1s"], ["offP%d" % t])
-    act(T.LA[:], T.ioP[:].indirect(T.offc[:]), AF.Copy, IOP + ["offc"], ["LA"])
-    cp(T.X2[:], T.X[:], XA, ["X20", "X21"])
-    for k in range(2):
-        for u in range(4):
-            act(T.PA[:, C * k + u:C * k + C:4], T.LA[:, C * k + Q * u:C * k + Q * u + Q], AF.Copy, ["LA", "cm"], ["PA%d%d" % (k, u)], scale=col(cCM + u))
-    for t in range(4):
-        act(T.D0[:, 2 * t:2 * Q:8], T.IO[:, 0:NP], AF.Identity, ["IO", "eb"], ["D0e%d" % t], scale=0.0, bias=col(cEB + t))
+    cp(T.offd[:], T.c2s[:], ["c2s"], ["offd"])
+    qz("Zq", "Zs", 0, 128, T.Bt[:], ["Bt"], ["Zpad", "Zq01"])
+    qz("Cq", "Cs", KP, OP, T.Ct[:, 4 * KP:4 * OP], ["Kp0", "Kn0", "Kp1", "Kn1"], ["Kq"])
+
+    act(col(cQT), col(cT), AF.Identity, ["cf"], ["qt"], scale=4.0, bias=col(cU))
+    act(col(cNT), col(cT), AF.Identity, ["cf"], ["nt"], scale=-1.0, bias=-0.5)
+    act(T.LA[:], T.ioN[:].indirect(T.offc[:]), AF.Copy, ["ioNa", "ioNb", "offc"], ["LA"])
+    act(T.dg[:], T.IO4[:], AF.Sign, ["IO4", "nt"], ["dg"], bias=col(cNT))
+    act(T.PR[:], T.LA[:].indirect(T.offQ[:]), AF.Copy, ["LA"] + PERM, ["PR"])
+    act(T.D0[:, 0:2 * NM:2], T.dg[:], AF.Identity, ["dg"], ["D0e"], scale=BIG / 2, bias=BIG / 2)
+    act(T.En[:], T.dg[:], AF.Identity, ["dg"], ["En"], scale=0.5 / BIG, bias=0.5 / BIG)
+    act(T.LB[:, 0:C], T.tabF[:].indirect(T.offd[:]), AF.Copy, ["tabFa", "tabFb", "offd"], ["LB0"])
+    act(col(cS2), col(cQ), AF.Identity, ["cf"], ["s2"], scale=2.0, bias=-float(C))
+    act(T.LB[:, C:3 * C], T.LB[:, 0:C].indirect(T.offc[:]), AF.Copy, ["LB0", "offc"], ["LB1"])
+    act(T.ioS[:], T.ioS[:], AF.Identity, ["ioS"], ["ioS"], bias=0.5)
+    act(col(cN2), col(cQ), AF.Identity, ["cf"], ["n2"], scale=-2.0, bias=C - 1.0)
+    act(col(cNS), col(cQ), AF.Identity, ["cf"], ["ns"], scale=-2.0, bias=-1.0)
+    act(col(cHM), col(cHB), AF.Identity, ["cf"], ["hm"], bias=-1.0)
+    act(T.tie[:], T.IO[:, 0:H], AF.Identity, ["IO"], ["tie"], scale=-1.0 / H, bias=(H - 1.0) / H)
+    act(T.kG[:], T.IO[:, 0:4], AF.Identity, ["IO"], ["kG"], scale=-0.5, bias=-float(C))
+    act(T.kS[:], T.IO[:, 0:4], AF.Identity, ["IO"], ["kS"], scale=-0.5, bias=-(H - 1.0))
+    act(T.gm[:], T.gm[:], AF.Abs, ["gm", "hm"], ["gm"], bias=col(cHM))
+    act(T.RW[:, 33:34], col(cQ), AF.Identity, ["cf"], ["RWc"], scale=0.0, bias=-float(C))
+    act(T.gm[:], T.gm[:], AF.Identity, ["gm"], ["gm"], scale=1000.0 + C, bias=-float(C))
+    act(T.MB[:, 0:1], col(cQ), AF.Copy, ["cf"], ["MBa"], scale=0.0)
+    act(T.KY[:, 16:17], col(cQ), AF.Copy, ["cf"], ["KYb"], scale=0.0)
+    act(col(cT576), col(cT), AF.Identity, ["cf"], ["t576"], bias=float(2 * C))
+    act(col(cT128), col(cT), AF.Identity, ["cf"], ["t128"], scale=float(N * H))
+    for h in range(2):
+        act(col(cMB + h), col(cU), AF.Identity, ["cf"], ["mb%d" % h], scale=float(4 * QH[h]), bias=col(cT))
 
     plan = _plan(T, topo, rank)
     sent = [0]
@@ -335,7 +364,7 @@ def rank_program(g, core, T, topo):
             eng = _feed_engines(T, topo, rank, helper)
             rid, pid = topo.addr(helper, core)
             trs.append(RemoteDMATransfer(dst_ids=[DstId(rid=rid, pnc=pid)], dma_engine_mask=_mask(eng), remote_sem=T.sem["hin%d" % t],
-                                         srcs=[src], dsts=[_view(T, kind, "h%s%d" % (kind, t), 0, H)]))
+                                         srcs=[src], dsts=[_view(T, kind, "h" + kind, H * t, H * t + H)]))
             sent[0] += len(eng)
         if direct:
             tr, n = _spread(T, topo, core, rank, kind, t, src, direct)
@@ -349,220 +378,328 @@ def rank_program(g, core, T, topo):
             for kind, (direct, helper, rest) in _plan(T, topo, s).items():
                 arrivals += len(topo.engines(T.cores[s] if rank in direct else helper, core))
 
-    def scores(k, halves):
-        base = k * ZW
-        zr = names("Z%d" % k, 4)
-        if halves:
-            for h in range(2):
-                qz("Zq", "Zs", base + PAD + h * HC, base + PAD + (h + 1) * HC,
-                   T.Z[:, 4 * C * k + 2 * C * h:4 * C * k + 2 * C * (h + 1)], zr if halves == 2 else zr[2 * h:2 * h + 2], ["Zq%d%d" % (k, h)])
-        else:
-            qz("Zq", "Zs", base + PAD, base + ZW, T.Z[:, 4 * C * k:4 * C * (k + 1)], zr, ["Zq%d0" % k, "Zq%d1" % k])
+    order = sorted(ZC, key=lambda x: ZC[x])
+
+    def zview(h, k, a=0, step=1):
+        return T.Z[:, 4 * ZC[h, k] + a:4 * (ZC[h, k] + NH[h]):step]
+
+    def part(buf, h, a=0, step=1):
+        return buf[:, 4 * BASE[h] + a:4 * (BASE[h] + NH[h]):step]
+
+    def uview(h, k):
+        return T["U%d" % h][:, 4 * NH[h] * k:4 * NH[h] * (k + 1)]
+
+    def zn(h, k):
+        return names("Z%d%d" % (h, k), 4)
+
+    def score(h, k):
+        z = PAD + ZC[h, k]
+        qz("Zq", "Zs", z, z + NH[h], zview(h, k), zn(h, k), ["Zq%d%d" % (h, k)])
+        i = order.index((h, k))
+        before = "Zpad" if i == 0 else "Zq%d%d" % order[i - 1]
         for u in range(4):
-            mm(k, 128, "Kq", "Ks", 12 - 4 * u, "Zq", "Zs", base + Q * u, u == 0, u == 3,
-               ["Kq", "Zpad%d" % k, "Zq%d0" % k] + (["Zq%d1" % k] if u >= 2 else []))
+            mm(h, 128, "Cq", "Cs", (KP if k else KN) + 12 - 4 * u, "Zq", "Zs", z + QH[h] * (u + 1) - 128, k == 1 and u == 0, k == 0 and u == 3,
+               ["Kq", before, "Zq%d%d" % (h, k)])
 
-    def zhalf(k, c, win, off, a, other, r):
-        tt(T.Z[:, 4 * C * k + 2 * C * c:4 * C * k + 2 * C * (c + 1)], win[:].indirect(off[:, a + 36 * c:a + 36 * c + 36]),
-           other[:, 2 * C * c:2 * C * (c + 1)], A.mult, r, ["Z%d%d" % (k, 2 * c), "Z%d%d" % (k, 2 * c + 1)])
+    def diff(h):
+        return T["ps%d" % h][:, 128 - QH[h]:128]
 
-    def zplane(k, e):
-        tt(T.Z[:, 4 * C * k + e:4 * C * (k + 1):4], T.X[:].indirect(T.offP[:, 36 * e + 18 * k:36 * e + 18 * k + 18]),
-           T.X2[:, e:4 * C:4], A.mult, XA + ["X20", "X21", "offP%d" % e], ["Z%d%d" % (k, e)])
+    def zgather(h, k, win, off, a, other, r):
+        tt(zview(h, k), win[:].indirect(off[:, a + MO[h]:a + MO[h] + QH[h]]), part(other, h), A.mult, r, zn(h, k))
 
-    def keep_s0():
-        act(T.s0c[:], T.ps0[:, PAD:128], AF.Copy, [], ["s0c", "ps0"])
+    def ugather(h, k, win, off, a, r):
+        act(uview(h, k), win[:].indirect(off[:, a + MO[h]:a + MO[h] + QH[h]]), AF.Copy, r, ["U%d%d" % (h, k)])
+
+    def zplain(h, k, other, r):
+        tt(zview(h, k), uview(h, k), part(other, h), A.mult, r + ["U%d%d" % (h, k)], zn(h, k))
+
+    X1 = T.X2
+    x1 = [["X20"], ["X21"]]
+
+    def again(h):
+        act(part(T.X2, h), part(T.X, h), AF.Copy, names("X%d" % h, 4), ["X2%d" % h])
+
+    def zplanes(h, k):
+        for e in range(4):
+            a = 36 * e + 18 * k + BASE[h] // 16
+            tt(zview(h, k, e, 4), T.X[:].indirect(T.offP[:, a:a + NH[h] // 16]), part(X1, h, e, 4), A.mult,
+               XA + x1[h] + ["offP%d" % e], ["Z%d%d%d" % (h, k, e)])
+
+    def choose(h):
+        ts(T.D1[:, 2 * MO[h]:2 * (MO[h] + QH[h]):2], diff(h), 0.0, None, A.is_gt, None, [], ["D1e%d" % h, "ps%d" % h])
+
+    def pointers(h):
+        a, b = 2 * MO[h], 2 * (MO[h] + QH[h])
+        scan(T.PW[:, a:b], T.D0[:, a:b], T.D1[:, a:b], 0.0, A.mult, A.add, ["D1e%d" % h, "D1o", "D0o", "D0e"], ["PW%d" % h])
+
+    def planes(i):
+        e, pts = WORDS[i]
+        for k, (h, r) in enumerate(pts):
+            c = 2 * MO[h] + 8 * r + 7
+            if e == "V":
+                ts(T.OH[:, 4 * SW * i + k:4 * SW * i + 4 * C:4], T.ioV[:], T.PW[:, c:c + 1], 2.0, A.is_equal, A.mult,
+                   ["ioV", "PW%d" % h], ["OH%d%d" % (i, k)])
+            else:
+                act(T.OH[:, 4 * SW * i + k:4 * SW * (i + 1):4], T.ioS[:], AF.Sign, ["ioS", "PW%d" % h], ["OH%d%d" % (i, k)],
+                    scale=-1.0, bias=T.PW[:, c:c + 1])
+
+    def count(i, start=False, stop=False):
+        steps = WORDS[i][0] == "S"
+        n = SW if steps else C
+        qz("OHq", "OHs", SW * i, SW * i + n, T.OH[:, 4 * SW * i:4 * (SW * i + n)], names("OH%d" % i, 4), ["OHq%d" % i])
+        mm(2, C, "Cq", "Cs", OP, "OHq", "OHs", SW * i, start, stop and not steps, ["ONq", "OHq%d" % i])
+        if steps:
+            mm(2, C, "Cq", "Cs", ON, "OHq", "OHs", SW * i + 2, False, stop, ["ONq", "OHq%d" % i])
+
+    def reorder(off, src, h, r, w):
+        m = (QH[h] + 15) // 16
+        ts(off[:, 48 * h:48 * h + 16 * m], src[:, MO[h]:MO[h] + QH[h]].indirect(T.offT[:, 4 * h:4 * h + m]), col(cT128), None, A.add, None,
+           r + ["offT%d" % h, "t128"], [w + str(h)])
+
+    spare = [
+        lambda: ts(T.DK[:], T.IO[:, 0:17], col(cQ), -10000.0, A.is_equal, A.mult, ["IO", "cf"], ["DK"]),
+        lambda: ts(T.dk2[:], T.IO[:, 0:17], col(cQ), 1.0, A.subtract, A.is_equal, ["IO", "cf"], ["dk2"]),
+        lambda: qz("Eq", "Es", 0, 128, T.Et[:, 3:515], ["Et"], ["Eq0"]),
+        lambda: ts(T.dk2[:, 16:17], T.dk2[:, 16:17], -1.0, None, A.add, None, ["dk2"], ["dk2"]),
+        lambda: qz("Eq", "Es", 128, 256, T.Et[:, 2:514], ["Et"], ["Eq1"]),
+        lambda: ts(T.dk2[:], T.dk2[:], 1024.0, None, A.mult, None, ["dk2"], ["dk2"]),
+        lambda: ts(T.tm[:], T.IM[:, 0:80], col(cQ), None, A.is_equal, None, ["IM", "cf"], ["tm"]),
+        lambda: tt(T.DK[:], T.DK[:], T.dk2[:], A.add, ["DK", "dk2"], ["DK"]),
+        lambda: ts(T.ts[:], T.IM[:, 0:80], 0.0, None, A.is_gt, None, ["IM"], ["ts"]),
+        lambda: tt(T.tp[:], T.tm[:], T.tp[:], A.mult, ["tm"] + names("tp", 3), names("tp", 3)),
+        lambda: qz("Eq", "Es", 256, 384, T.Et[:, 1:513], ["Et"], ["Eq2"]),
+        lambda: scan(T.tm[:], T.ts[:], T.tp[:], 0.0, A.mult, A.add, ["ts"] + names("tp", 3), ["tm"]),
+        lambda: ts(T.offX[:, 0:QH[0]], T.ix0[:, 0:QH[0]], col(cMB), None, A.add, None, ["ix00", "mb0"], ["offX0"]),
+        lambda: ts(T.offX[:, QH[0]:NM], T.ix0[:, 48:80], col(cMB + 1), 4.0 * BASE[1], A.add, A.add, ["ix01", "mb1"], ["offX1"]),
+        lambda: qz("Eq", "Es", 384, 512, T.Et[:, 0:512], ["Et"], ["Eq3"]),
+        lambda: cp(T.offT[:, 0:3], T.tm[:, 15:48:16], ["tm"], ["offT0"]),
+        lambda: cp(T.offT[:, 4:6], T.tm[:, 63:80:16], ["tm"], ["offT1"]),
+    ]
+
+    def fill(n):
+        for f in spare[:n]:
+            f()
+        del spare[:n]
 
     for t in range(R):
         first, last = t == 0, t == R - 1
         if first:
-            for e in range(4):
-                zplane(0, e)
-            scan(T.SA[:], T.rm4[:, 0:2 * C], T.PA[:], 0.0, A.mult, A.add, ["rm4"] + names("PA0", 4) + names("PA1", 4), ["SA"])
-            qz("Kq", "Ks", 0, 140, T.Kt[:], ["Kta", "Ktb"], ["Kq"])
-            scores(0, 0)
+            zplanes(0, 1)
+            ts(T.MK[:], T.IM[:], col(cQT), None, A.is_equal, None, ["IM", "qt"], ["MK"])
+            score(0, 1)
+            zplanes(0, 0)
+            tt(T.PR[:], T.PR[:], T.MK[:], A.mult, ["PR", "MK"], ["PR"])
+            score(0, 0)
+            scan(T.SA[:], T.rm4[:, 0:2 * C], T.PR[:], 0.0, A.mult, A.add, ["rm4", "PR"], ["SA"])
+            zplanes(1, 1)
             tt(T.dQ[:], T.SA[:, C + 3:2 * C:4], T.SA[:, 3:C:4], A.subtract, ["SA"], ["dQ"])
-            act(T.LR[:], T.ioR[:].indirect(T.offc[:]), AF.Copy, ["ioR", "offc"], ["LR"])
-            for e in range(4):
-                act(T.D1[:, 2 * e + 1:2 * Q:8], T.SA[:, 4 * e + 3:C:16], AF.Copy, ["SA", "dm"], ["D1o%d" % e], scale=col(cDM + e))
-            for e in range(4):
-                act(T.D0[:, 2 * e + 1:2 * Q:8], T.dQ[:, e:Q:4], AF.Identity, ["dQ", "dm", "e"], ["D0o%d" % e], scale=col(cDM + e), bias=col(cE + e))
-            keep_s0()
-            for e in range(4):
-                zplane(1, e)
-            qz("ONq", "ONs", 0, 128, T.ONt[:], ["ONt"], ["ONq"])
-            scores(1, 2)
-            act(T.gm0[:], T.hf[:], AF.Abs, ["hf", "hm"], ["gm0"], bias=col(cHM))
-            act(T.gm[:], T.gm0[:], AF.Identity, ["gm0"], ["gm"], scale=1000.0 + C, bias=-float(C))
-            cp(T.offd[:], T.c2s[:], ["c2s"], ["offd"])
-            ts(T.dk1[:], T.IO[:, 0:17], col(cQ), -10000.0, A.is_equal, A.mult, ["IO", "cf"], ["dk1"])
-            ts(T.dk2[:], T.IO[:, 0:17], col(cQ), 1.0, A.subtract, A.is_equal, ["IO", "cf"], ["dk2"])
+            act(T.D1[:, 1:2 * NM:2], T.SA[:, 3:C:4], AF.Copy, ["SA"], ["D1o"])
+            choose(0)
+            tt(T.D0[:, 1:2 * NM:2], T.dQ[:], T.En[:], A.add, ["dQ", "En"], ["D0o"])
+            score(1, 1)
+            pointers(0)
+            planes(0)
+            zplanes(1, 0)
+            ts(T.Ct[:, 4 * OP:4 * ON], T.KJ[:], col(cG), None, A.is_equal, None, ["KJ", "cf"], ["Op"])
+            score(1, 0)
+            ts(T.Ct[:, 4 * ON:4 * ON + 512], T.KJ[:], col(cG), -1.0, A.is_equal, A.mult, ["KJ", "cf"], ["On"])
+            ts(T.CF[:, cCM:cCM + 4], T.IO[:, 0:4], col(cU), None, A.is_equal, None, ["IO", "cf"], ["cm"])
+            qz("Cq", "Cs", OP, OP + 256, T.Ct[:, 4 * OP:4 * OP + 1024], ["Op", "On"], ["ONq"])
         else:
-            zhalf(0, 0, T.X, T.offW, 0, T.X2, XA + ["X20", "offW"])
-            zhalf(0, 1, T.X, T.offW, 0, T.X2, XA + ["X21", "offW"])
-            zhalf(1, 0, T.X, T.offW, Q, T.X2, XA + ["X20", "offW"])
-            scores(0, 0)
-            keep_s0()
-            zhalf(1, 1, T.X, T.offW, Q, T.X2, XA + ["X21", "offW"])
-            scores(1, 1)
-        tt(T.D1[:, 0:2 * Q:2], T.ps1[:, PAD:128], T.s0c[:], A.is_gt, ["s0c"], ["D1e", "ps1"])
-        scan(T.PW[:], T.D0[:], T.D1[:], 0.0, A.mult, A.add, ["D1e"] + names("D1o", 4) + names("D0o", 4) + names("D0e", 4), ["PW"])
-        for e in range(4):
-            r = 12 + e
-            act(T.ab[:, e:4 * C:4], T.ioP[:], AF.Abs, IOP + ["PW"], ["ab%d" % e], scale=-1.0, bias=T.PW[:, 8 * r + 7:8 * r + 8])
-        act(T.OH[:, 12 * C:16 * C], T.ab[:], AF.Relu, names("ab", 4), ["OH3"], scale=-1.0, bias=1.0)
-        if first:
-            act(T.tabR[:], T.tr0[:], AF.Identity, names("tr0", 4) + ["nh"], ["tabR"], bias=col(cNH))
-            act(T.rm32[:], T.r0[:], AF.Sign, ["r0"], ["rm32"])
-            act(T.LB[:, 0:C], T.tabF[:].indirect(T.offd[:]), AF.Copy, ["tabFa", "tabFb", "offd"], ["LB0"])
+            def second(h):
+                if SCALAR_GATHERS:
+                    zplain(h, 0, T.X, names("X%d" % h, 4))
+                else:
+                    zgather(h, 0, T.X, T.offW, 0, X1, XA + x1[h] + ["offW"])
 
-        def planes(i):
-            for e in range(4 if i < 4 else 2):
-                r = 4 * i + e
-                ts(T.OH[:, 4 * C * i + e:4 * C * (i + 1):4], T.ioP[:], T.PW[:, 8 * r + 7:8 * r + 8], None, A.is_equal, None,
-                   IOP + ["PW"], ["OH%d%d" % (i, e)])
-
-        def count(i, start, stop):
-            rr = ["OH3"] if i == 3 else names("OH%d" % i, 4)
-            qz("OHq", "OHs", C * i, C * i + C, T.OH[:, 4 * C * i:4 * C * (i + 1)], rr, ["OHq%d" % i])
-            mm(2, C, "ONq", "ONs", 0, "OHq", "OHs", C * i, start, stop, ["ONq", "OHq%d" % i])
-
-        planes(0)
+            if SCALAR_GATHERS:
+                ugather(0, 0, T.X, T.offW, 0, XA + ["offW"])
+            again(1)
+            if SCALAR_GATHERS:
+                ugather(1, 0, T.X, T.offW, 0, XA + ["offW"])
+            zgather(0, 1, T.X, T.offW, NM, X1, XA + x1[0] + ["offW"])
+            second(0)
+            score(0, 1)
+            score(0, 0)
+            zgather(1, 1, T.X, T.offW, NM, X1, XA + x1[1] + ["offW"])
+            second(1)
+            choose(0)
+            score(1, 1)
+            pointers(0)
+            planes(0)
+            score(1, 0)
         planes(1)
-        count(0, True, False)
         planes(2)
-        count(1, False, False)
+        choose(1)
+        count(1, start=True)
+        pointers(1)
         planes(4)
-        count(2, False, False)
+        count(2)
+        count(0)
+        planes(3)
+        fill(1)
+        count(3)
+        count(4, stop=True)
         if first:
-            ts(T.dk2[:, 16:17], T.dk2[:, 16:17], -1.0, None, A.add, None, ["dk2"], ["dk2"])
-        count(4, False, False)
-        if first:
-            ts(T.dk2[:], T.dk2[:], 1024.0, None, A.mult, None, ["dk2"], ["dk2"])
-        count(3, False, True)
-        if first:
-            tt(T.DK[:], T.dk1[:], T.dk2[:], A.add, ["dk1", "dk2"], ["DK"])
+            for u in range(4):
+                act(T.MU[:, u:2 * C:4], T.IM[:, 0:HC], AF.Identity, ["IM", "cm"], ["MU%d" % u], scale=0.0, bias=col(cCM + u))
+        fill(5)
         act(T.junk[:], T.ps2[:, 0:C], AF.Sign, ["ns"], ["junk", "ac0", "ps2"], bias=col(cNS), accum_out=ac(0))
-        act(T.junk2[:], T.ps2[:, 0:C], AF.Sign, [], ["junk2", "RWb", "ps2"], bias=-(H + 0.5), accum_out=T.RW[:, 32:33])
+        act(T.junk2[:], T.ps2[:, 0:C], AF.Sign, [], ["junk2", "RWb", "ps2"], bias=-(2 * H + 1.0), accum_out=T.RW[:, 32:33])
         ts(T.bc[:], T.gm[:], ac(0), None, A.min, None, ["gm", "ac0"], ["bc"])
+        fill(1)
         op("V", lambda: V.transpose(T.RW[:, 0:32], T.bc[:]), ["bc"], ["RWa"])
+        fill(1)
         act(T.junk[:, 0:33], T.RW[:, 0:33], AF.Sign, ["RWa", "RWb", "n2"], ["junk", "ac1"], bias=col(cN2), accum_out=ac(1))
+        ts(T.cb[:, 0:HC], T.ps2[:, 0:C:2], 2 * H + 2.0, 2 * H + 1.0, A.min, A.subtract, [], ["cb0", "ps2"])
         ts(T.MB[:, 1:34], T.RW[:, 0:33], col(cS2), -1000.0, A.is_gt, A.mult, ["RWa", "RWb", "s2"], ["MBb"])
-        ts(T.cb[:], T.ps2[:, 0:C], H + 1.0, H + 0.5, A.min, A.subtract, [], ["cb", "ps2"])
-        act(T.cnt[:], T.ps2[:, 0:C], AF.Copy, [], ["cnt", "ps2"])
+        ts(T.cb[:, HC:C], T.ps2[:, 1:C:2], 2 * H + 2.0, 2 * H + 1.0, A.min, A.subtract, [], ["cb1", "ps2"])
+        for k in range(2):
+            act(T.cnt[:, HC * k:HC * k + HC], T.ps2[:, k:C:2], AF.Copy, [], ["cnt%d" % k, "ps2"])
         scan(T.SC[:], T.MB[:], T.RW[:], -float(C), A.add, A.max, ["MBa", "MBb", "RWa", "RWb", "RWc"], ["SC"])
-        ts(T.eq[:], T.cb[:], 2.0, ac(1), A.mult, A.is_equal, ["cb", "ac1"], ["eq"])
+        ts(T.eq[:], T.cb[:], ac(1), None, A.is_equal, None, ["cb0", "cb1", "ac1"], ["eq"])
+        fill(1)
         scan(T.pf[:], T.eq[:], T.eq[:], T.SC[:, 33:34], A.add, A.add, ["eq", "SC"], ["pf"])
         act(T.junk[:], T.pf[:], AF.Sign, ["pf", "n2"], ["junk", "ac2"], bias=col(cN2), accum_out=ac(2))
+        fill(3)
         ts(T.offH[:, 0:1], ac(2), -0.5, C / 2.0, A.mult, A.add, ["ac2"], ["offH"])
-        tt(T.KY[:, 0:H], T.cnt[:].indirect(T.offH[:, 0:1]), T.tie[:], A.add, ["cnt", "offH", "tie"], ["KYa"])
+        ts(T.offG[:], T.kG[:], ac(2), -2.0, A.add, A.mult, ["kG", "ac2"], ["offG"])
+        tt(T.KY[:, 0:H], T.cnt[:].indirect(T.offH[:, 0:1]), T.tie[:], A.add, ["cnt0", "cnt1", "offH", "tie"], ["KYa"])
+        act(T.Bu[:], T.X[:].indirect(T.offG[:]), AF.Copy, XA + ["offG"], ["Bu"])
+        fill(1)
         scan(T.OW[:], T.DK[:], T.KY[:], 0.0, A.add, A.max, ["DK", "KYa", "KYb"], ["OW"])
         act(T.junk2[:, 0:H], T.KY[:, 0:H], AF.Sign, ["KYa", "OW"], ["junk2", "ac3"], scale=-1.0, bias=T.OW[:, 16:17], accum_out=ac(3))
-        ts(T.O[:], T.tabR[:], ac(3), ac(2), A.is_equal, A.mult, ["tabR", "ac3", "ac2"], ["O"])
-        op("V", lambda: V.transpose(T.OT[:], T.O[:]), ["O"], ["OT"])
-        scan(T.OS[:], T.rm32[:], T.OT[:], 0.0, A.mult, A.add, ["rm32", "OT"], ["OS"])
-        ts(T.offB[:], T.OS[:, 31:128:32], -2.0, col(cT576), A.mult, A.add, ["OS", "t576"], ["offB"])
-        cp(T.Bt[:, 0:4 * H], T.X[:].indirect(T.offB[:]), XA + ["offB"], ["Bt"])
+        fill(2)
+        ts(T.offS[:], T.kS[:], ac(3), -2.0, A.add, A.mult, ["kS", "ac3"], ["offS"])
+        ts(T.offR[:, 0:1], ac(3), -0.5, (H - 1) / 2.0, A.mult, A.add, ["ac3"], ["offR"])
+        cp(T.Bt[:, 0:4 * H].indirect(T.offS[:]), T.Bu[:], ["Bu", "offS"], ["Bt"])
+        fill(1)
         qz("Fq%d" % t, "Fs%d" % t, OWN, OWN + 128, T.Bt[:], ["Bt"], ["Fown%d" % t])
         send("q", t)
         send("s", t)
+        for h in range(2):
+            act(part(T.Xp, h), T.X[:].indirect(T.offX[:, MO[h]:MO[h] + QH[h]]), AF.Copy, XA + ["offX%d" % h], ["Xp%d" % h], scale=2.0)
         if first:
-            iota(T.tabH[:], [[1, C], [0, 4]], 0, 0, ["tabH"])
-            ts(T.offX[:], T.ix0[:], col(cMB), None, A.add, None, ["ix0", "mb"], ["offX"])
-            act(T.LB[:, C:3 * C], T.LB[:, 0:C].indirect(T.offc[:]), AF.Copy, ["LB0", "offc"], ["LB1"])
-            for k in range(3):
-                for u in range(4):
-                    act(T.PB[:, C * k + u:C * k + C:4], T.LB[:, C * k + Q * u:C * k + Q * u + Q], AF.Copy, ["LB0", "LB1", "cm"],
-                        ["PB%d%d" % (k, u)], scale=col(cCM + u))
-            qz("Eq", "Es", 0, 512, T.Et[:], names("Et", 4), ["Eq"])
-        act(T.Xp[:], T.X[:].indirect(T.offX[:]), AF.Copy, XA + ["offX"], ["Xp"])
-        ts(T.Xh[:], T.X[:], 0.5, None, A.mult, None, XA, ["Xh"])
-        if first:
-            ts(T.cfr[:], T.cf0[:], 4.0 / UB, None, A.mult, None, ["cf0"], ["cfr"])
-            qz("Vq", "Vs", 0, 128, T.vt[:], ["vt"], ["Vq"])
-            scan(T.SB[:], T.rm4[:], T.PB[:], 0.0, A.mult, A.add, ["rm4"] + names("PB0", 4) + names("PB1", 4) + names("PB2", 4), ["SB"])
+            MU = names("MU", 4)
+            for h in range(2):
+                a = 48 * h
+                act(T.ixr[:, a:a + 48 - 16 * h], T.ix0[:, a:a + 48 - 16 * h], AF.Identity, ["ix0%d" % h, "ix02", "mb%d" % h], ["ixr%d" % h], bias=col(cMB + h))
+            act(T.LR[:], T.ioR[:].indirect(T.offc[:]), AF.Copy, ["ioR", "offc"], ["LR"])
+            tt(T.PB[:, 0:C], T.LB[:, 0:C].indirect(T.offQ[:, 0:18]), T.MU[:, 0:C], A.mult, ["LB0"] + PERM + MU, ["PB0"])
+            tt(T.PB[:, C:3 * C], T.LB[:, C:3 * C].indirect(T.offQ[:]), T.MU[:], A.mult, ["LB1"] + PERM + MU, ["PB1"])
+            fill(1)
+            scan(T.SB[:], T.rm4[:], T.PB[:], 0.0, A.mult, A.add, ["rm4", "PB0", "PB1"], ["SB"])
+            fill(99)
             tt(T.dg[:], T.SB[:, 2 * C + 3:3 * C:4], T.SB[:, C + 3:2 * C:4], A.subtract, ["SB"], ["dg"])
-            for u in range(4):
-                ts(T.off0[:, NP * u:NP * u + NP], T.SB[:, 4 * u + 3:C:16], col(cT128), None, A.add, None, ["SB", "t128"], ["off0%d" % u])
-        tt(T.t1[:], T.D1[:, 0:2 * Q:2], T.dg[:], A.mult, ["D1e", "dg"], ["t1"])
-        tt(T.t2[:], T.t1[:], T.SB[:, C + 3:2 * C:4], A.add, ["t1", "SB"], ["t2"])
-        for u in range(4):
-            ts(T.off1[:, NP * u:NP * u + NP], T.t2[:, u:Q:4], col(cT128), None, A.add, None, ["t2", "t128"], ["off1%d" % u])
+            cp(T.dQ[:], T.SB[:, 3:C:4], ["SB"], ["dQ"])
+        tt(T.t1[:], T.D1[:, 0:2 * NM:2], T.dg[:], A.mult, ["D1e0", "D1e1", "dg"], ["t1"])
         if first:
-            for u in range(4):
-                act(T.PR[:, u:2 * C:4], T.LR[:, u:2 * C:4], AF.Copy, ["LR", "cm"], ["PR%d" % u], scale=col(cCM + u))
-            scan(T.SR[:], T.rm4[:, 0:2 * C], T.PR[:], 0.0, A.mult, A.add, ["rm4"] + names("PR", 4), ["SR"])
-            ts(T.offW[:], T.SR[:, 3:2 * C:4], 4.0, col(cT576), A.mult, A.add, ["SR", "t576"], ["offW"])
-        act(T.h64[:], T.tabH[:].indirect(T.offB[:]), AF.Copy, ["tabH", "offB"], ["h64"])
-        act(T.HL[:, H * t:H * t + H], T.h64[:, 0:64:4], AF.Copy, ["h64"], ["HL%d" % t])
+            for h in range(2):
+                reorder(T.off0, T.dQ, h, ["dQ"], "off0")
+        else:
+            ts(T.Xh[:], T.X[:], 0.5, None, A.mult, None, XA, ["Xh"])
+        tt(T.t2[:], T.t1[:], T.SB[:, C + 3:2 * C:4], A.add, ["t1", "SB"], ["t2"])
+        if first:
+            ts(T.Xh[:], T.X[:], 0.5, None, A.mult, None, XA, ["Xh"])
+        for h in range(2):
+            reorder(T.off1, T.t2, h, ["t2"], "off1")
+        act(T.h16[:], T.ioF[:].indirect(T.offH[:, 0:1]), AF.Copy, ["ioF", "offH"], ["h16"])
+        if first:
+            tt(T.PR[:], T.LR[:], T.MU[:], A.mult, ["LR"] + MU, ["PR"])
+        cp(T.HL[:, H * t:H * t + H].indirect(T.offR[:, 0:1]), T.h16[:], ["h16", "offR"], ["HL%d" % t])
+        if first:
+            scan(T.SR[:], T.rm4[:, 0:2 * C], T.PR[:], 0.0, A.mult, A.add, ["rm4", "PR"], ["SR"])
+        if t == 1:
+            qz("Vq", "Vs", 0, 128, T.vt[:], ["vt"], ["Vq"])
         if last:
             dma("Y", T.hl[:], T.HL[0:128:16, :], names("HL", R), [])
         for b in range(4):
-            mm(4 + b, 128, "Eq", "Es", 128 * b, "Fq%d" % t, "Fs%d" % t, 0, True, True, ["Eq", "Fown%d" % t],
+            mm(4 + b, 128, "Eq", "Es", 128 * b, "Fq%d" % t, "Fs%d" % t, 0, True, True, ["Eq%d" % b, "Fown%d" % t],
                pre=[("arr%d" % t, arrivals)] if b == 0 else ())
         for b in range(4):
+            bank = "ps%d" % (4 + b)
             if b % 2 == 1:
-                cp(T.F[:, 128 * b:128 * b + 128], T["ps%d" % (4 + b)][:, 0:128], [], ["F%d" % b, "ps%d" % (4 + b)])
+                ts(T.F[:, 128 * b:128 * b + 128], T[bank][:, 0:128], 0.5, None, A.mult, None, [], ["F%d" % b, bank])
             else:
-                act(T.F[:, 128 * b:128 * b + 128], T["ps%d" % (4 + b)][:, 0:128], AF.Copy, [], ["F%d" % b, "ps%d" % (4 + b)])
+                act(T.F[:, 128 * b:128 * b + 128], T[bank][:, 0:128], AF.Copy, [], ["F%d" % b, bank], scale=0.5)
         FA = names("F", 4)
-        for k in range(2):
-            o = "off%d" % k
-            act(T.U[:, UB * k:UB * k + 4 * C], T.F[:].indirect(T[o][:]), AF.Copy, FA + names(o, 4), ["U%d" % k], scale=0.5)
-        tt(T.Z[:, 0:4 * C], T.F[:].indirect(T.off0[:]), T.Xp[:], A.mult, FA + names("off0", 4) + ["Xp"], names("Z0", 4))
-        zhalf(1, 0, T.F, T.off1, 0, T.Xp, FA + names("off1", 4) + ["Xp"])
-        scores(0, 0)
-        zhalf(1, 1, T.F, T.off1, 0, T.Xp, FA + names("off1", 4) + ["Xp"])
-        scores(1, 1)
-        keep_s0()
-        tt(T.sel2[:], T.ps1[:, PAD:128], T.s0c[:], A.is_gt, ["s0c"], ["sel2", "ps1"])
-        tt(T.sf[:], T.sel2[:], T.cfr[:], A.add, ["sel2", "cfr"], ["sf"])
-        for u in range(4):
-            ts(T.offM[:, NP * u:NP * u + NP], T.sf[:, u:Q:4], float(UB), col(cMB), A.mult, A.add, ["sf", "mb"], ["offM%d" % u])
 
-        def evac(c, b, eng):
-            bank = "ps%d" % (4 * (1 - c) + b)
-            out = T.X[:, 2 * C * c + b:2 * C * (c + 1):4]
-            if eng == "V":
-                ts(out, T[bank][:, 0:HC], 0.03125, None, A.mult, None, [], ["X%d%d" % (c, b), bank])
+        def pick(h, step):
+            a, n = MO[h], QH[h]
+            if step == 0:
+                ts(T.sel2[:, a:a + n], diff(h), 0.0, 4.0 * NH[h], A.is_gt, A.mult, [], ["sel2%d" % h, "ps%d" % h])
+            elif step == 1:
+                m = (n + 15) // 16
+                tt(T.sf[:, 48 * h:48 * h + 16 * m], T.sel2[:, a:a + n].indirect(T.offT[:, 4 * h:4 * h + m]), T.ixr[:, 48 * h:48 * h + 16 * m], A.add,
+                   ["sel2%d" % h, "offT%d" % h, "ixr%d" % h], ["sf%d" % h])
             else:
-                act(out, T[bank][:, 0:HC], AF.Copy, [], ["X%d%d" % (c, b), bank], scale=0.03125)
+                cp(T.offM[:, a:a + n], T.sf[:, 48 * h:48 * h + n], ["sf%d" % h], ["offM%d" % h])
 
-        def finish(c):
-            if not last:
-                if c == 0:
-                    cp(T.X2[:, 0:2 * C], T.X[:, 0:2 * C], names("X0", 4), ["X20"])
-                else:
-                    act(T.X2[:, 2 * C:4 * C], T.X[:, 2 * C:4 * C], AF.Copy, names("X1", 4), ["X21"])
-                return
-            qz("Xq", "Xs", HC * c, HC * c + HC, T.X[:, 2 * C * c:2 * C * (c + 1)], names("X%d" % c, 4), ["Xq%d" % c])
-            mm(4 + c, HC, "Vq", "Vs", 0, "Xq", "Xs", HC * c, True, True, ["Vq", "Xq%d" % c])
-            dma("Y", T.oc[:, 2 * C * c:2 * C * (c + 1)], T.Xq[:, HC * c:HC * c + HC].bitcast(dt.uint8), ["Xq%d" % c], [])
+        def mix(h):
+            tt(part(T.Mt, h), T["U%d" % h][:].indirect(T.offM[:, MO[h]:MO[h] + QH[h]]), part(T.Xh, h), A.add,
+               ["U%d0" % h, "U%d1" % h, "Xh", "offM%d" % h], ["Mt%d" % h])
 
-        def mix(a, b, r, w):
-            tt(T.Mt[:, C * a:C * b], T.U[:].indirect(T.offM[:, NP * a:NP * b]), T.Xh[:, C * a:C * b], A.add, ["U0", "U1", "Ug0", "Ug1", "Xh"] + r, w)
-
-        def layer(c, r):
-            qz("Mq", "Ms", HC * c, HC * c + HC, T.Mt[:, 2 * C * c:2 * C * (c + 1)], r, ["Mq%d" % c])
+        def layer(h):
+            qz("Mq", "Ms", BASE[h], BASE[h] + NH[h], part(T.Mt, h), ["Mt%d" % h], ["Mq%d" % h])
             for b in range(4):
-                mm(4 * (1 - c) + b, HC, "Wq", "Ws", 128 * b, "Mq", "Ms", HC * c, True, True, ["Wq", "Ws", "Mq%d" % c])
+                mm(4 * (1 - h) + b, NH[h], "Wq", "Ws", 128 * b, "Mq", "Ms", BASE[h], True, True, ["Wq", "Ws", "Mq%d" % h])
 
-        mix(0, 2, ["offM0", "offM1"], ["Mt0"])
-        mix(2, 3, ["offM2"], ["Mt1"])
-        layer(0, ["Mt0"])
+        def evac(h, b, eng):
+            bank = "ps%d" % (4 * (1 - h) + b)
+            if eng == "V":
+                ts(part(T.X, h, b, 4), T[bank][:, 0:NH[h]], 0.03125, None, A.mult, None, [], ["X%d%d" % (h, b), bank])
+            else:
+                act(part(T.X, h, b, 4), T[bank][:, 0:NH[h]], AF.Copy, [], ["X%d%d" % (h, b), bank], scale=0.03125)
+
+        def finish(h):
+            a, b = BASE[h], BASE[h] + NH[h]
+            if not last:
+                if h == 0:
+                    again(0)
+                return
+            qz("Xq", "Xs", a, b, part(T.X, h), names("X%d" % h, 4), ["Xq%d" % h])
+            mm(4 + h, NH[h], "Vq", "Vs", 0, "Xq", "Xs", a, True, True, ["Vq", "Xq%d" % h])
+            dma("Y", T.oc[:, 4 * a:4 * b], T.Xq[:, a:b].bitcast(dt.uint8), ["Xq%d" % h], [])
+
+        def other(h):
+            if SCALAR_GATHERS:
+                zplain(h, 0, T.Xp, ["Xp%d" % h])
+            else:
+                zgather(h, 0, T.F, T.off0, 8 * h, T.Xp, FA + ["off0%d" % h, "Xp%d" % h])
+
+        for h, k in ((0, 0), (1, 0), (0, 1), (1, 1)):
+            ugather(h, k, T.F, T["off%d" % k], 8 * h, FA + ["off%d%d" % (k, h)])
+        zgather(0, 1, T.F, T.off1, 0, T.Xp, FA + ["off10", "Xp0"])
+        other(0)
+        score(0, 1)
+        score(0, 0)
+        zgather(1, 1, T.F, T.off1, 8, T.Xp, FA + ["off11", "Xp1"])
+        other(1)
+        pick(0, 0)
+        score(1, 1)
+        pick(0, 1)
+        score(1, 0)
+        pick(0, 2)
+        if first:
+            ts(T.offW[:], T.SR[:, 3:2 * C:4], 4.0, col(cT576), A.mult, A.add, ["SR", "t576"], ["offW"])
+        mix(0)
+        pick(1, 0)
+        layer(0)
+        pick(1, 1)
+        pick(1, 2)
         for b in range(4):
             evac(0, b, "S")
-        mix(3, 4, ["offM3"], ["Mt2"])
-        layer(1, ["Mt1", "Mt2"])
+        mix(1)
+        layer(1)
         finish(0)
         for b in range(4):
             evac(1, b, "SV"[b % 2])
         finish(1)
         if last:
-            act(T.Y[:, 0:HC], T.ps4[:, 0:HC], AF.Copy, [], ["Y0", "ps4"])
-            cp(T.Y[:, HC:C], T.ps5[:, 0:HC], [], ["Y1", "ps5"])
-            dma("S", T.y[:, 0:HC], T.Y[:, 0:HC], ["Y0"], [])
+            act(T.Y[:, 0:NH[0]], T.ps4[:, 0:NH[0]], AF.Copy, [], ["Y0", "ps4"])
+            cp(T.Y[:, BASE[1]:C], T.ps5[:, 0:NH[1]], [], ["Y1", "ps5"])
+            dma("S", T.y[:, 0:NH[0]], T.Y[:, 0:NH[0]], ["Y0"], [])
             for k in range(4):
                 dma("YS"[k // 2], T.osc[4 * k:4 * k + 4, :], T.Xs[32 * k:32 * k + 4, :], ["Xq0", "Xq1"], [])
-            dma("Y", T.y[:, HC:C], T.Y[:, HC:C], ["Y1"], [])
+            dma("Y", T.y[:, BASE[1]:C], T.Y[:, BASE[1]:C], ["Y1"], [])
     _emit(g, T, ops, [("sent", sent[0])])

@@ -10,20 +10,29 @@ QH = (40, 32)
 MO = (0, 40)
 NM = 72
 PAD = 128 - QH[0]
-ZC = {(0, 1): 0, (0, 0): 160, (1, 1): 320, (1, 0): 448}
+ZC = {(0, 1): 0, (0, 0): 160, (1, 0): 320, (1, 1): 448}
 SW = C + 2
 FW = 2 * N * H - H
 OWN = (N - 1) * H
 BIG = 4096.0
 KP, KN, OP, ON = 0, 140, 280, 408
 
-SCALAR_GATHERS = True
-WORDS = [("S", [(0, 0), (0, 1), (0, 2), (0, 3)]), ("V", [(0, 4), (0, 5), (0, 6), (0, 7)]), ("V", [(0, 8), (0, 9)]),
-         ("V", [(1, 4), (1, 5), (1, 6), (1, 7)]), ("S", [(1, 0), (1, 1), (1, 2), (1, 3)])]
+WORDS = [[(0, r) for r in range(4)], [(0, r) for r in range(4, 8)], [(0, 8), (0, 9)], [(1, r) for r in range(4)], [(1, r) for r in range(4, 8)]]
+LOW, ROUND = 2.0 ** -9, 1.5 * 2.0 ** 23
+POINT = [("gather", 0), ("plain", 0, 0), ("score", 0, 1), ("score", 0, 0), ("plain", 1, 0), ("score", 1, 0), ("plain", 1, 1), ("choose", 0),
+         ("score", 1, 1), ("pointers", 0), ("split", 0)]
+COUNT = [("planes", 0), ("planes", 1), ("planes", 2), ("choose", 1), ("count", 0, 1), ("pointers", 1), ("count", 1, 2), ("split", 1),
+         ("count", 2, 3), ("planes", 3), ("planes", 4), ("count", 3, 4), ("count", 4, 5)]
+ON_SCALAR = [(0, 8), (0, 9), (1, 6), (1, 7)]
+SLOTS = ((0, 0), (1, 0), (1, 1), (0, 1))
+CHOICE = ([("gather", 0), ("plain", 0, 0), ("score", 0, 1), ("score", 0, 0), ("plain", 1, 0), ("score", 1, 0), ("plain", 1, 1), ("pick", 0, 0),
+           ("score", 1, 1), ("pick", 0, 1), ("lists",), ("pick", 0, 2), ("select", 0, 28, 40), ("mix", 0, 0, 28), ("pick", 1, 0), ("add", 0, 28, 40),
+           ("pick", 1, 1), ("layer", 0), ("pick", 1, 2), ("select", 1, 20, 32), ("mix", 1, 0, 20)]
+          + [("evac", 0, b, "S") for b in range(4)] + [("add", 1, 20, 32), ("layer", 1), ("finish", 0)]
+          + [("evac", 1, b, "SV"[b % 2]) for b in range(4)] + [("finish", 1)])
 
-DIRECT_CODES = 3
-DIRECT_SCALES = 4
-HELPERS_ON_OTHER_DIE = True
+LOADS = {"q": (2, 2), "s": (3, 3)}
+CALLS = [("s", "feed"), ("q", "feed"), ("q", "direct"), ("s", "direct")]
 
 X4, U8, BF, F32, I32, U16 = "float8_e4m3fn_x4", "uint8", "bfloat16", "float32", "int32", "uint16"
 
@@ -38,9 +47,9 @@ SCRATCH = {
     "c1s": _sb(36, I32), "c2s": _sb(18, I32), "vt": _sb(512, BF), "Vq": _sb(128, X4), "Vs": _sb(128, U8),
     "Wq": _sb(512, X4), "Ws": _sb(512, U8),
     "pci": _sb(1, I32), "ci": _sb(5, I32), "CF": _sb(32, F32), "IO": _sb(32, F32), "IO4": _sb(NM, F32), "En": _sb(NM, F32),
-    "one": _sb(516, BF), "KI": _sb(512, BF), "KJ": _sb(512, BF), "Ct": _sb(4 * 536, BF), "Cq": _sb(536, X4), "Cs": _sb(536, U8),
+    "one": _sb(2 * C, BF), "Ct": _sb(4 * 536, BF), "Cq": _sb(536, X4), "Cs": _sb(536, U8),
     "Et": _sb(516, BF), "Eq": _sb(512, X4), "Es": _sb(512, U8),
-    "ioN": _sb(C, BF), "ioV": _sb(C, BF), "ioS": _sb(SW, F32), "ioR": _sb(C, BF), "ioF": _sb(C, F32), "tabF": _sb(128, BF),
+    "ioN": _sb(C, BF), "PC": _sb(18, BF), "PV": _sb(18, BF), "hu": _sb(HC, I32), "ioR": _sb(C, BF), "ioF": _sb(C, F32), "tabF": _sb(128, BF),
     "rm4": _sb(3 * C, BF), "IM": _sb(2 * C, BF), "MK": _sb(2 * C, BF), "MU": _sb(2 * C, BF), "PI": _sb(36, F32), "offQ": _sb(36, U16),
     "offP": _sb(144, U16), "offW": _sb(144, U16), "offc": _sb(36, U16), "offd": _sb(18, U16),
     "LA": _sb(2 * C, BF), "SA": _sb(2 * C, BF), "dQ": _sb(NM, F32),
@@ -48,8 +57,8 @@ SCRATCH = {
     "LB": _sb(3 * C, BF), "PB": _sb(3 * C, BF), "SB": _sb(3 * C, BF),
     "dg": _sb(NM, F32), "t1": _sb(NM, F32), "t2": _sb(NM, F32),
     "D0": _sb(2 * NM, F32), "D1": _sb(2 * NM, F32), "PW": _sb(2 * NM, BF),
-    "OH": _sb(20 * SW, BF), "OHq": _sb(5 * SW, X4), "OHs": _sb(5 * SW, U8),
-    "cb": _sb(C, BF), "junk": _sb(C, BF), "junk2": _sb(C, BF), "cnt": _sb(C, F32), "eq": _sb(C, BF), "pf": _sb(C, BF),
+    "OH": _sb(20 * HC, BF), "OHq": _sb(5 * HC, X4), "OHs": _sb(5 * HC, U8),
+    "cb": _sb(C, BF), "junk": _sb(C, BF), "junk2": _sb(C, BF), "cnt": _sb(C, BF), "eq": _sb(C, BF), "pf": _sb(C, BF),
     "AC": _sb(8, F32), "gm": _sb(32, F32), "bc": _sb(32, F32),
     "RW": _sb(34, F32), "MB": _sb(34, F32), "SC": _sb(34, F32),
     "offH": _sb(2, U16), "offR": _sb(2, U16), "offG": _sb(4, U16), "offS": _sb(4, U16), "kG": _sb(4, F32), "kS": _sb(4, F32),
@@ -59,7 +68,7 @@ SCRATCH = {
     "off0": _sb(80, U16), "off1": _sb(80, U16), "offM": _sb(NM, U16), "offX": _sb(NM, U16),
     "ix0": _sb(80, F32), "ixr": _sb(80, F32), "sel2": _sb(NM, F32), "sf": _sb(80, F32),
     "tp": _sb(80, F32), "tm": _sb(80, F32), "ts": _sb(80, F32), "offT": _sb(6, U16),
-    "Mt": _sb(4 * C, BF), "Mq": _sb(C, X4), "Ms": _sb(C, U8), "Xq": _sb(C, X4), "Xs": _sb(C, U8), "Y": _sb(C, F32),
+    "Mt": _sb(4 * C, BF), "Mu": _sb(4 * C, BF), "Mq": _sb(C, X4), "Ms": _sb(C, U8), "Xq": _sb(C, X4), "Xs": _sb(C, U8), "Y": _sb(C, F32),
 }
 for _t in range(R):
     SCRATCH["Fq%d" % _t] = _sb(FW, X4)
@@ -84,12 +93,17 @@ def _mask(engines):
 def _plan(T, topo, rank):
     core = T.cores[rank]
     peers = [(rank + k) % N for k in range(1, N)]
-    cand = [c for c in topo.cores_of(core) if T.rank_of(c) is None
-            and (topo.die(c) != topo.die(core)) == HELPERS_ON_OTHER_DIE
-            and all(topo.may_write(c, T.cores[d]) for d in peers)]
-    rev = peers[::-1]
-    return {"q": (peers[:DIRECT_CODES], cand[0], peers[DIRECT_CODES:]),
-            "s": (rev[:DIRECT_SCALES], cand[-1], rev[DIRECT_SCALES:])}
+    free = [c for c in topo.cores_of(core) if T.rank_of(c) is None and all(topo.may_write(c, T.cores[d]) for d in peers)]
+    free.sort(key=lambda c: topo.die(c) == topo.die(core))
+    plan = {}
+    for kind, cores in (("q", free), ("s", free[::-1])):
+        rest = peers if kind == "q" else peers[::-1]
+        loads = []
+        for c, n in zip(cores, LOADS[kind]):
+            loads.append((c, rest[:n]))
+            rest = rest[n:]
+        plan[kind] = (rest, loads)
+    return plan
 
 
 def _view(T, kind, name, a, b):
@@ -107,9 +121,9 @@ def _spread(T, topo, src_core, rank, kind, t, src, dests):
     return RemoteDMATransfer(dst_ids=ids, dma_engine_mask=_mask(eng), remote_sem=T.sem["arr%d" % t], srcs=[src], dsts=dsts), len(eng)
 
 
-def _feed_engines(T, topo, rank, helper):
+def _feed_engines(T, topo, rank, helper, shared):
     core = T.cores[rank]
-    off = topo.engines(core, T.cores[(rank + 1) % N])
+    off = topo.engines(core, T.cores[(rank + 1) % N]) if shared else []
     return [e for e in topo.engines(core, helper) if e not in off]
 
 
@@ -117,16 +131,17 @@ def _helper(g, core, T, topo):
     for rank in range(N):
         if core not in topo.cores_of(T.cores[rank]):
             continue
-        for kind, (direct, helper, rest) in _plan(T, topo, rank).items():
-            if helper != core or not rest:
-                continue
-            sent = 0
-            for t in range(R):
-                g.wait_ge(T.sem["hin%d" % t], len(_feed_engines(T, topo, rank, core)))
-                tr, n = _spread(T, topo, core, rank, kind, t, _view(T, kind, "h" + kind, H * t, H * t + H), rest)
-                g.remote_dma_fused([tr], local_sem=T.sem.sent)
-                sent += n
-            g.wait_ge(T.sem.sent, sent)
+        for kind, (direct, loads) in _plan(T, topo, rank).items():
+            for helper, rest in loads:
+                if helper != core:
+                    continue
+                sent = 0
+                for t in range(R):
+                    g.wait_ge(T.sem["hin%d" % t], len(_feed_engines(T, topo, rank, core, (kind, "both") in CALLS)))
+                    tr, n = _spread(T, topo, core, rank, kind, t, _view(T, kind, "h" + kind, H * t, H * t + H), rest)
+                    g.remote_dma_fused([tr], local_sem=T.sem.sent)
+                    sent += n
+                g.wait_ge(T.sem.sent, sent)
 
 
 def _emit(g, T, ops, tail):
@@ -259,11 +274,10 @@ def rank_program(g, core, T, topo):
 
     XA = names("X0", 4) + names("X1", 4)
     cQ, cT, cU, cHB, cG, cS2, cNS, cT576, cT128, cHM, cN2, cQT = range(12)
-    cCM, cPM, cMB, cNT = 12, 16, 18, 20
+    cCM, cPM, cMB, cNT, cRL, cTOP, cK8 = 12, 16, 18, 20, 21, 22, 24
 
     dma("S", T.c1s[:], T.c1[:], [], ["c1s"])
     dma("Y", T.X[:], T.x[:], [], XA)
-    dma("S", T.X2[:, 0:4 * NH[0]], T.x[:, 0:4 * NH[0]], [], ["X20"])
     dma("S", T.c2s[:], T.c2[:], [], ["c2s"])
     dma("Y", T.X2[:, 4 * NH[0]:4 * C], T.x[:, 4 * NH[0]:4 * C], [], ["X21"])
     dma("Y", T.Wq[:].bitcast(dt.uint8), T.wc[:], [], ["Wq"])
@@ -272,48 +286,55 @@ def rank_program(g, core, T, topo):
 
     iota(T.pci[:], [[0, 1]], 0, 1, ["pci"], flag=False)
     iota(T.IO[:], [[1, 32]], 0, 0, ["IO"])
-    iota(T.KI[:], [[1, 8], [100, 4], [0, 16]], 0, 0, ["KI"])
     iota(T.PI[:], [[C, 2], [4, 18]], 0, 0, ["PI"])
-    iota(T.ioN[:, 0:HC], [[1, HC]], -HC, 0, ["ioNa"])
+    iota(T.IM[:], [[0, 2 * C // 16], [1, 16]], 0, 0, ["IM"])
+    iota(T.ioN[:, 0:HC], [[-1, HC]], -1, 0, ["ioNa"])
     iota(T.ioN[:, HC:C], [[1, HC]], 1, 0, ["ioNb"])
     iota(T.IO4[:], [[0, NM // 4], [1, 4]], 0, 0, ["IO4"])
-    iota(T.IM[:], [[0, 2 * C // 16], [1, 16]], 0, 0, ["IM"])
+    ms(T.one[:], 1.0, ["one"])
+    ones = T.Ct[:, 4 * OP:4 * ON]
+    asel(ones, T.one[:, 0:512], [[-16, 8], [0, 64]], A.is_ge, 0, 1, ["one"], ["Op"])
+    asel(ones, ones, [[16, 8], [0, 64]], A.is_ge, 15, -1, ["Op"], ["Op"])
     own = (rank + 1) * H
     iota(T.tabF[:, 0:own], [[1, own]], N * H - own, 0, ["tabFa"])
     if own < N * H:
         iota(T.tabF[:, own:N * H], [[1, N * H - own]], 0, 0, ["tabFb"])
-    iota(T.ioS[:], [[1, HC + 1], [HC + 1, 2]], -HC - 1, 0, ["ioS"])
-    iota(T.KJ[:], [[1, 8], [0, 64]], 0, 0, ["KJ"])
-    iota(T.ioV[:], [[1, HC], [HC + 1, 2]], -HC, 0, ["ioV"])
-    iota(T.gm[:], [[1, 2], [0, 16]], 0, 0, ["gm"])
-    for i, (e, pts) in enumerate(WORDS):
+    for i, pts in enumerate(WORDS):
         for k in range(len(pts), 4):
-            iota(T.OH[:, 4 * SW * i + k:4 * SW * i + 4 * C:4], [[0, C]], 0, 0, ["OH%d%d" % (i, k)])
-    iota(T.one[:], [[0, 516]], 1, 0, ["one"])
-    asel(T.Et[:], T.one[:], [[-1, 516]], A.is_equal, 3, 4, ["one"], ["Et"])
+            iota(T.OH[:, 4 * HC * i + k:4 * HC * (i + 1):4], [[0, HC]], 0, 0, ["OH%d%d" % (i, k)])
+    iota(T.gm[:], [[1, 2], [0, 16]], 0, 0, ["gm"])
+    iota(T.RW[:, 33:34], [[0, 1]], -C, 0, ["RWc"])
+    iota(T.MB[:, 0:1], [[0, 1]], 0, 0, ["MBa"])
+    iota(T.KY[:, 16:17], [[0, 1]], 0, 0, ["KYb"])
+    iota(T.kG[:], [[1, 4]], 2 * C, 0, ["kG"])
+    iota(T.kS[:], [[1, 4]], 2 * (H - 1), 0, ["kS"])
+    asel(T.Et[:], T.one[:, 0:516], [[-1, 516]], A.is_equal, 3, 4, ["one"], ["Et"])
     for h in range(2):
         iota(T.ix0[:, 48 * h:48 * h + QH[h]], [[4, 4], [16, QH[h] // 4]], 0, 0, ["ix0%d" % h])
         iota(T.tp[:, 48 * h:48 * h + QH[h]], [[1, 4], [4, QH[h] // 4]], 0, 0, ["tp%d" % h])
     iota(T.ix0[:, 40:48], [[0, 8]], 0, 0, ["ix02"])
     iota(T.tp[:, 40:48], [[0, 8]], 0, 0, ["tp2"])
-    iota(T.ioR[:], [[1, C]], -HC, 0, ["ioR"])
-    iota(T.ioF[:], [[1, C]], 0, 0, ["ioF"])
 
-    ms(T.Bt[:], 0.0, ["Bt"])
+    ms(T.Ct[:, 4 * KP:4 * KN], 0.0, names("Kp", 8))
+    ts(T.ci[:, 4:5], T.pci[:], 4, None, A.logical_shift_right, None, ["pci"], ["ci4"])
     ts(T.ci[:, 0:1], T.pci[:], 15, None, A.bitwise_and, None, ["pci"], ["ci0"])
     ts(T.ci[:, 1:2], T.pci[:], 3, None, A.bitwise_and, None, ["pci"], ["ci1"])
     ts(T.ci[:, 2:3], T.pci[:], 2, 3, A.logical_shift_right, A.bitwise_and, ["pci"], ["ci2"])
     ts(T.ci[:, 3:4], T.pci[:], 4, 1, A.logical_shift_right, A.bitwise_and, ["pci"], ["ci3"])
-    ts(T.ci[:, 4:5], T.pci[:], 4, None, A.logical_shift_right, None, ["pci"], ["ci4"])
-    ms(T.rm4[:], 1.0, ["rm4"])
+    ms(T.Bt[:], 0.0, ["Bt"])
     cp(T.CF[:, 0:5], T.ci[:], names("ci", 5), ["cf"])
-    ms(T.Ct[:, 4 * KP:4 * KP + 48], 0.0, ["Kp0"])
-    ms(T.rm4[:, 0:3 * C:4], 0.0, ["rm4"])
+    qz("Zq", "Zs", 0, 128, T.Bt[:], ["Bt"], ["Zpad", "Zq01"])
+    ts(T.CF[:, cK8:cK8 + 8], T.IO[:, 0:8], col(cG), None, A.is_equal, None, ["IO", "cf"], ["k8"])
     for h in range(2):
         ts(col(cPM + h), col(cT), float(QH[h]), col(cU), A.mult, A.add, ["cf"], ["pm0%d" % h])
-    ms(T.Ct[:, 4 * KN:4 * KN + 48], 0.0, ["Kn0"])
-    ts(T.Ct[:, 4 * KP + 48:4 * KN], T.KI[:], col(cG), None, A.is_equal, None, ["KI", "cf"], ["Kp1"])
-    act(T.Ct[:, 4 * KN + 48:4 * OP], T.Ct[:, 4 * KP + 48:4 * KN], AF.Copy, ["Kp1"], ["Kn1"], scale=-1.0)
+    ts(col(cQT), col(cT), 4.0, col(cU), A.mult, A.add, ["cf"], ["qt"])
+    act(T.rm4[:, 0:2 * C], T.one[:], AF.Copy, ["one"], ["rm4"])
+    act(T.rm4[:, 2 * C:3 * C], T.one[:, 0:C], AF.Copy, ["one"], ["rm4b"])
+    act(T.rm4[:, 0:3 * C:4], T.one[:, 0:3 * NM], AF.Copy, ["one", "rm4b"], ["rm4"], scale=0.0)
+    for i in range(8):
+        a = 4 * KP + 48 + 64 * i
+        act(T.Ct[:, a:a + 16], T.IO[:, 0:16], AF.Identity, ["IO", "k8"], ["Kp%d" % i], scale=0.0, bias=col(cK8 + i))
+    act(T.Ct[:, 4 * KN:4 * OP], T.Ct[:, 4 * KP:4 * KN], AF.Copy, names("Kp", 8), ["Kn"], scale=-1.0)
     for k in range(2):
         for h in range(2):
             a, b = 18 * k + MO[h] // 4, 18 * k + (MO[h] + QH[h]) // 4
@@ -322,51 +343,44 @@ def rank_program(g, core, T, topo):
     cp(T.offc[:], T.c1s[:], ["c1s"], ["offc"])
     for t in range(4):
         ts(T.offP[:, 36 * t:36 * t + 36], T.c1s[:], 4, t, A.mult, A.add, ["c1s"], ["offP%d" % t])
-    cp(T.offd[:], T.c2s[:], ["c2s"], ["offd"])
-    qz("Zq", "Zs", 0, 128, T.Bt[:], ["Bt"], ["Zpad", "Zq01"])
-    qz("Cq", "Cs", KP, OP, T.Ct[:, 4 * KP:4 * OP], ["Kp0", "Kn0", "Kp1", "Kn1"], ["Kq"])
+    ts(T.MK[:], T.IM[:], col(cQT), None, A.is_equal, None, ["IM", "qt"], ["MK"])
 
-    act(col(cQT), col(cT), AF.Identity, ["cf"], ["qt"], scale=4.0, bias=col(cU))
-    act(col(cNT), col(cT), AF.Identity, ["cf"], ["nt"], scale=-1.0, bias=-0.5)
-    act(T.LA[:], T.ioN[:].indirect(T.offc[:]), AF.Copy, ["ioNa", "ioNb", "offc"], ["LA"])
-    act(T.dg[:], T.IO4[:], AF.Sign, ["IO4", "nt"], ["dg"], bias=col(cNT))
-    act(T.PR[:], T.LA[:].indirect(T.offQ[:]), AF.Copy, ["LA"] + PERM, ["PR"])
-    act(T.D0[:, 0:2 * NM:2], T.dg[:], AF.Identity, ["dg"], ["D0e"], scale=BIG / 2, bias=BIG / 2)
-    act(T.En[:], T.dg[:], AF.Identity, ["dg"], ["En"], scale=0.5 / BIG, bias=0.5 / BIG)
-    act(T.LB[:, 0:C], T.tabF[:].indirect(T.offd[:]), AF.Copy, ["tabFa", "tabFb", "offd"], ["LB0"])
-    act(col(cS2), col(cQ), AF.Identity, ["cf"], ["s2"], scale=2.0, bias=-float(C))
-    act(T.LB[:, C:3 * C], T.LB[:, 0:C].indirect(T.offc[:]), AF.Copy, ["LB0", "offc"], ["LB1"])
-    act(T.ioS[:], T.ioS[:], AF.Identity, ["ioS"], ["ioS"], bias=0.5)
-    act(col(cN2), col(cQ), AF.Identity, ["cf"], ["n2"], scale=-2.0, bias=C - 1.0)
-    act(col(cNS), col(cQ), AF.Identity, ["cf"], ["ns"], scale=-2.0, bias=-1.0)
-    act(col(cHM), col(cHB), AF.Identity, ["cf"], ["hm"], bias=-1.0)
-    act(T.tie[:], T.IO[:, 0:H], AF.Identity, ["IO"], ["tie"], scale=-1.0 / H, bias=(H - 1.0) / H)
-    act(T.kG[:], T.IO[:, 0:4], AF.Identity, ["IO"], ["kG"], scale=-0.5, bias=-float(C))
-    act(T.kS[:], T.IO[:, 0:4], AF.Identity, ["IO"], ["kS"], scale=-0.5, bias=-(H - 1.0))
-    act(T.gm[:], T.gm[:], AF.Abs, ["gm", "hm"], ["gm"], bias=col(cHM))
-    act(T.RW[:, 33:34], col(cQ), AF.Identity, ["cf"], ["RWc"], scale=0.0, bias=-float(C))
-    act(T.gm[:], T.gm[:], AF.Identity, ["gm"], ["gm"], scale=1000.0 + C, bias=-float(C))
-    act(T.MB[:, 0:1], col(cQ), AF.Copy, ["cf"], ["MBa"], scale=0.0)
-    act(T.KY[:, 16:17], col(cQ), AF.Copy, ["cf"], ["KYb"], scale=0.0)
-    act(col(cT576), col(cT), AF.Identity, ["cf"], ["t576"], bias=float(2 * C))
-    act(col(cT128), col(cT), AF.Identity, ["cf"], ["t128"], scale=float(N * H))
-    for h in range(2):
-        act(col(cMB + h), col(cU), AF.Identity, ["cf"], ["mb%d" % h], scale=float(4 * QH[h]), bias=col(cT))
+    def late_constants():
+        act(T.dg[:], T.IO4[:], AF.Sign, ["IO4", "nt"], ["dg"], bias=col(cNT))
+        act(T.tie[:], T.IO[:, 0:H], AF.Identity, ["IO"], ["tie"], scale=-LOW / H, bias=(H - 1) * LOW / H)
+        act(T.D0[:, 0:2 * NM:2], T.dg[:], AF.Identity, ["dg"], ["D0e"], scale=BIG / 2, bias=BIG / 2)
+        act(T.En[:], T.dg[:], AF.Identity, ["dg"], ["En"], scale=0.5 / BIG, bias=0.5 / BIG)
+
+    def mask4(buf, n, w, bias, which):
+        for u in which:
+            act(buf[:, u:4 * n:4], T.IM[:, 0:n], AF.Identity, ["IM", "cm"], [w + str(u)], scale=0.0, bias=bias(u))
+
+    def chain_constants():
+        act(col(cNS), col(cQ), AF.Identity, ["cf"], ["ns"], scale=-LOW, bias=-LOW / 2)
+        act(col(cTOP), col(cQ), AF.Identity, ["cf"], ["top"], scale=0.0, bias=-(H + 0.5) * LOW)
+        for h in range(2):
+            act(col(cMB + h), col(cU), AF.Identity, ["cf"], ["mb%d" % h], scale=float(4 * QH[h]), bias=col(cT))
+        act(col(cHM), col(cHB), AF.Identity, ["cf"], ["hm"], bias=-1.0)
+        act(col(cN2), col(cQ), AF.Identity, ["cf"], ["n2"], scale=-2.0, bias=C - 1.0)
+        act(T.gm[:], T.gm[:], AF.Abs, ["gm", "hm"], ["gm"], bias=col(cHM))
+        act(col(cS2), col(cQ), AF.Identity, ["cf"], ["s2"], scale=2.0, bias=-float(C))
+        act(T.gm[:], T.gm[:], AF.Identity, ["gm"], ["gm"], scale=1000.0 + C, bias=-float(C))
+        ts(T.CF[:, cCM:cCM + 4], T.IO[:, 0:4], col(cU), None, A.is_equal, None, ["IO", "cf"], ["cm"])
 
     plan = _plan(T, topo, rank)
     sent = [0]
 
-    def send(kind, t):
-        direct, helper, rest = plan[kind]
+    def send(kind, what, t):
+        direct, loads = plan[kind]
         src = _view(T, kind, "F%s%d" % (kind, t), OWN, OWN + H)
         trs = []
-        if rest:
-            eng = _feed_engines(T, topo, rank, helper)
-            rid, pid = topo.addr(helper, core)
-            trs.append(RemoteDMATransfer(dst_ids=[DstId(rid=rid, pnc=pid)], dma_engine_mask=_mask(eng), remote_sem=T.sem["hin%d" % t],
-                                         srcs=[src], dsts=[_view(T, kind, "h" + kind, H * t, H * t + H)]))
+        if what != "direct":
+            eng = _feed_engines(T, topo, rank, loads[0][0], what == "both")
+            ids = [DstId(rid=topo.addr(c, core)[0], pnc=topo.addr(c, core)[1]) for c, rest in loads]
+            trs.append(RemoteDMATransfer(dst_ids=ids, dma_engine_mask=_mask(eng), remote_sem=T.sem["hin%d" % t],
+                                         srcs=[src], dsts=[_view(T, kind, "h" + kind, H * t, H * t + H) for c in loads]))
             sent[0] += len(eng)
-        if direct:
+        if what != "feed":
             tr, n = _spread(T, topo, core, rank, kind, t, src, direct)
             trs.append(tr)
             sent[0] += n
@@ -375,10 +389,14 @@ def rank_program(g, core, T, topo):
     arrivals = 0
     for s in range(N):
         if s != rank:
-            for kind, (direct, helper, rest) in _plan(T, topo, s).items():
-                arrivals += len(topo.engines(T.cores[s] if rank in direct else helper, core))
+            for kind, (direct, loads) in _plan(T, topo, s).items():
+                for c, dests in loads + [(T.cores[s], direct)]:
+                    if rank in dests:
+                        arrivals += len(topo.engines(c, core))
 
     order = sorted(ZC, key=lambda x: ZC[x])
+    begun = [False, False]
+    minus = []
 
     def zview(h, k, a=0, step=1):
         return T.Z[:, 4 * ZC[h, k] + a:4 * (ZC[h, k] + NH[h]):step]
@@ -397,8 +415,10 @@ def rank_program(g, core, T, topo):
         qz("Zq", "Zs", z, z + NH[h], zview(h, k), zn(h, k), ["Zq%d%d" % (h, k)])
         i = order.index((h, k))
         before = "Zpad" if i == 0 else "Zq%d%d" % order[i - 1]
+        second = begun[h]
+        begun[h] = not second
         for u in range(4):
-            mm(h, 128, "Cq", "Cs", (KP if k else KN) + 12 - 4 * u, "Zq", "Zs", z + QH[h] * (u + 1) - 128, k == 1 and u == 0, k == 0 and u == 3,
+            mm(h, 128, "Cq", "Cs", (KP if k else KN) + 12 - 4 * u, "Zq", "Zs", z + QH[h] * (u + 1) - 128, not second and u == 0, second and u == 3,
                ["Kq", before, "Zq%d%d" % (h, k)])
 
     def diff(h):
@@ -410,14 +430,19 @@ def rank_program(g, core, T, topo):
     def ugather(h, k, win, off, a, r):
         act(uview(h, k), win[:].indirect(off[:, a + MO[h]:a + MO[h] + QH[h]]), AF.Copy, r, ["U%d%d" % (h, k)])
 
-    def zplain(h, k, other, r):
-        tt(zview(h, k), uview(h, k), part(other, h), A.mult, r + ["U%d%d" % (h, k)], zn(h, k))
+    def zplain(h, k, other, r, pieces=0):
+        tt(zview(h, k), uview(h, k), part(other, h), A.mult, r + ["U%d%d" % (h, k)] + names("Ue%d" % h, pieces), zn(h, k))
+
+    def uplanes(h):
+        for e in range(4):
+            a = 36 * e + BASE[h] // 16
+            act(T["U%d" % h][:, e:4 * NH[h]:4], T.X[:].indirect(T.offP[:, a:a + NH[h] // 16]), AF.Copy, XA + ["offP%d" % e], ["Ue%d%d" % (h, e)])
 
     X1 = T.X2
     x1 = [["X20"], ["X21"]]
 
     def again(h):
-        act(part(T.X2, h), part(T.X, h), AF.Copy, names("X%d" % h, 4), ["X2%d" % h])
+        cp(part(T.X2, h), part(T.X, h), names("X%d" % h, 4), ["X2%d" % h])
 
     def zplanes(h, k):
         for e in range(4):
@@ -432,24 +457,28 @@ def rank_program(g, core, T, topo):
         a, b = 2 * MO[h], 2 * (MO[h] + QH[h])
         scan(T.PW[:, a:b], T.D0[:, a:b], T.D1[:, a:b], 0.0, A.mult, A.add, ["D1e%d" % h, "D1o", "D0o", "D0e"], ["PW%d" % h])
 
-    def planes(i):
-        e, pts = WORDS[i]
-        for k, (h, r) in enumerate(pts):
-            c = 2 * MO[h] + 8 * r + 7
-            if e == "V":
-                ts(T.OH[:, 4 * SW * i + k:4 * SW * i + 4 * C:4], T.ioV[:], T.PW[:, c:c + 1], 2.0, A.is_equal, A.mult,
-                   ["ioV", "PW%d" % h], ["OH%d%d" % (i, k)])
-            else:
-                act(T.OH[:, 4 * SW * i + k:4 * SW * (i + 1):4], T.ioS[:], AF.Sign, ["ioS", "PW%d" % h], ["OH%d%d" % (i, k)],
-                    scale=-1.0, bias=T.PW[:, c:c + 1])
+    def split(h):
+        a, b, c = 2 * MO[h] + 7, 2 * (MO[h] + QH[h]), MO[h] // 4
+        act(T.PC[:, c:c + QH[h] // 4], T.PW[:, a:b:8], AF.Abs, ["PW%d" % h], ["PC%d" % h])
+        ts(T.PV[:, c:c + QH[h] // 4], T.PW[:, a:b:8], 0.0, LOW, A.is_gt, A.max, ["PW%d" % h], ["PV%d" % h])
+        mine = [(i, k, c + r) for i, w in enumerate(WORDS) for k, (h2, r) in enumerate(w) if h2 == h and (h, r) in ON_SCALAR]
+        for n, (i, k, c) in enumerate(mine):
+            act(T.junk[:, HC * n:HC * n + HC], T.ioN[:, HC:C], AF.Abs, ["ioNb", "PC%d" % h], ["junk" + "ab"[n]], scale=-1.0, bias=T.PC[:, c:c + 1])
+        for n, (i, k, c) in enumerate(mine):
+            act(T.OH[:, 4 * HC * i + k:4 * HC * (i + 1):4], T.junk[:, HC * n:HC * n + HC], AF.Relu, ["junk" + "ab"[n], "PV%d" % h], ["OH%d%d" % (i, k)],
+                scale=-1.0, bias=T.PV[:, c:c + 1])
 
-    def count(i, start=False, stop=False):
-        steps = WORDS[i][0] == "S"
-        n = SW if steps else C
-        qz("OHq", "OHs", SW * i, SW * i + n, T.OH[:, 4 * SW * i:4 * (SW * i + n)], names("OH%d" % i, 4), ["OHq%d" % i])
-        mm(2, C, "Cq", "Cs", OP, "OHq", "OHs", SW * i, start, stop and not steps, ["ONq", "OHq%d" % i])
-        if steps:
-            mm(2, C, "Cq", "Cs", ON, "OHq", "OHs", SW * i + 2, False, stop, ["ONq", "OHq%d" % i])
+    def planes(i):
+        for k, (h, r) in enumerate(WORDS[i]):
+            c = MO[h] // 4 + r
+            if (h, r) not in ON_SCALAR:
+                ts(T.OH[:, 4 * HC * i + k:4 * HC * (i + 1):4], T.ioN[:, HC:C], T.PC[:, c:c + 1], T.PV[:, c:c + 1], A.is_equal, A.mult,
+                   ["ioNb", "PC%d" % h, "PV%d" % h], ["OH%d%d" % (i, k)])
+
+    def count(a, b):
+        qz("OHq", "OHs", HC * a, HC * b, T.OH[:, 4 * HC * a:4 * HC * b], sum([names("OH%d" % i, 4) for i in range(a, b)], []), names("OHq", b)[a:])
+        for i in range(a, b):
+            mm(2, HC, "Cq", "Cs", OP, "OHq", "OHs", HC * i, i == 0, i == len(WORDS) - 1, ["Oq0", "OHq%d" % i])
 
     def reorder(off, src, h, r, w):
         m = (QH[h] + 15) // 16
@@ -457,12 +486,12 @@ def rank_program(g, core, T, topo):
            r + ["offT%d" % h, "t128"], [w + str(h)])
 
     spare = [
-        lambda: ts(T.DK[:], T.IO[:, 0:17], col(cQ), -10000.0, A.is_equal, A.mult, ["IO", "cf"], ["DK"]),
+        lambda: ts(T.DK[:], T.IO[:, 0:17], col(cQ), -16.0, A.is_equal, A.mult, ["IO", "cf"], ["DK"]),
         lambda: ts(T.dk2[:], T.IO[:, 0:17], col(cQ), 1.0, A.subtract, A.is_equal, ["IO", "cf"], ["dk2"]),
         lambda: qz("Eq", "Es", 0, 128, T.Et[:, 3:515], ["Et"], ["Eq0"]),
         lambda: ts(T.dk2[:, 16:17], T.dk2[:, 16:17], -1.0, None, A.add, None, ["dk2"], ["dk2"]),
         lambda: qz("Eq", "Es", 128, 256, T.Et[:, 2:514], ["Et"], ["Eq1"]),
-        lambda: ts(T.dk2[:], T.dk2[:], 1024.0, None, A.mult, None, ["dk2"], ["dk2"]),
+        lambda: ts(T.dk2[:], T.dk2[:], 2.0, None, A.mult, None, ["dk2"], ["dk2"]),
         lambda: ts(T.tm[:], T.IM[:, 0:80], col(cQ), None, A.is_equal, None, ["IM", "cf"], ["tm"]),
         lambda: tt(T.DK[:], T.DK[:], T.dk2[:], A.add, ["DK", "dk2"], ["DK"]),
         lambda: ts(T.ts[:], T.IM[:, 0:80], 0.0, None, A.is_gt, None, ["IM"], ["ts"]),
@@ -476,6 +505,10 @@ def rank_program(g, core, T, topo):
         lambda: cp(T.offT[:, 4:6], T.tm[:, 63:80:16], ["tm"], ["offT1"]),
     ]
 
+    def run(steps, calls):
+        for s in steps:
+            calls[s[0]](*s[1:])
+
     def fill(n):
         for f in spare[:n]:
             f()
@@ -484,99 +517,89 @@ def rank_program(g, core, T, topo):
     for t in range(R):
         first, last = t == 0, t == R - 1
         if first:
+            uplanes(0)
+            act(T.LA[:], T.ioN[:].indirect(T.offc[:]), AF.Copy, ["ioNa", "ioNb", "offc"], ["LA"])
+            act(col(cNT), col(cT), AF.Identity, ["cf"], ["nt"], scale=-1.0, bias=-0.5)
+            act(T.PR[:], T.LA[:].indirect(T.offQ[:]), AF.Copy, ["LA"] + PERM, ["PR"])
+            uplanes(1)
+            late_constants()
+            cp(part(T.X2, 0), part(T.X, 0), names("X0", 4), ["X20"])
+            qz("Cq", "Cs", KP, OP, T.Ct[:, 4 * KP:4 * OP], names("Kp", 8) + ["Kn"], ["Kq"])
             zplanes(0, 1)
-            ts(T.MK[:], T.IM[:], col(cQT), None, A.is_equal, None, ["IM", "qt"], ["MK"])
+            zplain(0, 0, T.X, names("X0", 4), 4)
             score(0, 1)
-            zplanes(0, 0)
-            tt(T.PR[:], T.PR[:], T.MK[:], A.mult, ["PR", "MK"], ["PR"])
             score(0, 0)
-            scan(T.SA[:], T.rm4[:, 0:2 * C], T.PR[:], 0.0, A.mult, A.add, ["rm4", "PR"], ["SA"])
             zplanes(1, 1)
-            tt(T.dQ[:], T.SA[:, C + 3:2 * C:4], T.SA[:, 3:C:4], A.subtract, ["SA"], ["dQ"])
-            act(T.D1[:, 1:2 * NM:2], T.SA[:, 3:C:4], AF.Copy, ["SA"], ["D1o"])
+            tt(T.PR[:], T.PR[:], T.MK[:], A.mult, ["PR", "MK"], ["PR"])
             choose(0)
+            scan(T.SA[:], T.rm4[:, 0:2 * C], T.PR[:], 0.0, A.mult, A.add, ["rm4", "PR"], ["SA"])
+            zplain(1, 0, T.X, names("X1", 4), 4)
+            act(T.D1[:, 1:2 * NM:2], T.SA[:, 3:C:4], AF.Copy, ["SA"], ["D1o"])
+            tt(T.dQ[:], T.SA[:, C + 3:2 * C:4], T.SA[:, 3:C:4], A.subtract, ["SA"], ["dQ"])
+            score(1, 0)
             tt(T.D0[:, 1:2 * NM:2], T.dQ[:], T.En[:], A.add, ["dQ", "En"], ["D0o"])
             score(1, 1)
             pointers(0)
-            planes(0)
-            zplanes(1, 0)
-            ts(T.Ct[:, 4 * OP:4 * ON], T.KJ[:], col(cG), None, A.is_equal, None, ["KJ", "cf"], ["Op"])
-            score(1, 0)
-            ts(T.Ct[:, 4 * ON:4 * ON + 512], T.KJ[:], col(cG), -1.0, A.is_equal, A.mult, ["KJ", "cf"], ["On"])
-            ts(T.CF[:, cCM:cCM + 4], T.IO[:, 0:4], col(cU), None, A.is_equal, None, ["IO", "cf"], ["cm"])
-            qz("Cq", "Cs", OP, OP + 256, T.Ct[:, 4 * OP:4 * OP + 1024], ["Op", "On"], ["ONq"])
+            qz("Cq", "Cs", OP, ON, T.Ct[:, 4 * OP:4 * ON], ["Op"], ["Oq0"])
+            split(0)
+            cp(T.offd[:], T.c2s[:], ["c2s"], ["offd"])
+            act(T.LB[:, 0:C], T.tabF[:].indirect(T.offd[:]), AF.Copy, ["tabFa", "tabFb", "offd"], ["LB0"])
         else:
-            def second(h):
-                if SCALAR_GATHERS:
-                    zplain(h, 0, T.X, names("X%d" % h, 4))
-                else:
-                    zgather(h, 0, T.X, T.offW, 0, X1, XA + x1[h] + ["offW"])
-
-            if SCALAR_GATHERS:
-                ugather(0, 0, T.X, T.offW, 0, XA + ["offW"])
-            again(1)
-            if SCALAR_GATHERS:
-                ugather(1, 0, T.X, T.offW, 0, XA + ["offW"])
-            zgather(0, 1, T.X, T.offW, NM, X1, XA + x1[0] + ["offW"])
-            second(0)
-            score(0, 1)
-            score(0, 0)
-            zgather(1, 1, T.X, T.offW, NM, X1, XA + x1[1] + ["offW"])
-            second(1)
-            choose(0)
-            score(1, 1)
-            pointers(0)
-            planes(0)
-            score(1, 0)
-        planes(1)
-        planes(2)
-        choose(1)
-        count(1, start=True)
-        pointers(1)
-        planes(4)
-        count(2)
-        count(0)
-        planes(3)
-        fill(1)
-        count(3)
-        count(4, stop=True)
+            for h, k in ((0, 0), (1, 0), (1, 1)):
+                ugather(h, k, T.X, T.offW, NM * k, XA + ["offW"])
+            run(POINT, {"gather": lambda h: zgather(h, 1, T.X, T.offW, NM, X1, XA + x1[h] + ["offW"]),
+                        "plain": lambda h, k: zplain(h, k, T.X, names("X%d" % h, 4)),
+                        "score": score, "choose": choose, "pointers": pointers, "split": split})
+        run(COUNT, {"choose": choose, "pointers": pointers, "planes": planes, "split": split, "count": count})
         if first:
-            for u in range(4):
-                act(T.MU[:, u:2 * C:4], T.IM[:, 0:HC], AF.Identity, ["IM", "cm"], ["MU%d" % u], scale=0.0, bias=col(cCM + u))
-        fill(5)
-        act(T.junk[:], T.ps2[:, 0:C], AF.Sign, ["ns"], ["junk", "ac0", "ps2"], bias=col(cNS), accum_out=ac(0))
-        act(T.junk2[:], T.ps2[:, 0:C], AF.Sign, [], ["junk2", "RWb", "ps2"], bias=-(2 * H + 1.0), accum_out=T.RW[:, 32:33])
+            chain_constants()
+        fill(2)
+        ts(T.hu[:], T.ps2[:, 0:HC], -LOW * HC, None, A.add, None, [], ["hu", "ps2"])
+        fill(1)
+        tt(T.cnt[:, 0:HC], T.ps2[:, 0:HC], T.hu[:], A.subtract, ["hu"], ["cnt0", "ps2"])
+        ts(T.cnt[:, HC:C], T.hu[:], LOW, None, A.mult, None, ["hu"], ["cnt1"])
+        CNT = ["cnt0", "cnt1"]
+        act(T.junk[:], T.cnt[:], AF.Sign, CNT + ["ns"], ["junk", "junka", "junkb", "ac0"], bias=col(cNS), accum_out=ac(0))
+        act(T.junk2[:], T.cnt[:], AF.Sign, CNT + ["top"], ["junk2", "RWb"], bias=col(cTOP), accum_out=T.RW[:, 32:33])
+        fill(1)
+        ts(T.cb[:], T.cnt[:], (H + 1) * LOW, 2 / LOW, A.min, A.mult, CNT, ["cb"])
+        fill(1)
         ts(T.bc[:], T.gm[:], ac(0), None, A.min, None, ["gm", "ac0"], ["bc"])
         fill(1)
         op("V", lambda: V.transpose(T.RW[:, 0:32], T.bc[:]), ["bc"], ["RWa"])
-        fill(1)
+        fill(2)
         act(T.junk[:, 0:33], T.RW[:, 0:33], AF.Sign, ["RWa", "RWb", "n2"], ["junk", "ac1"], bias=col(cN2), accum_out=ac(1))
-        ts(T.cb[:, 0:HC], T.ps2[:, 0:C:2], 2 * H + 2.0, 2 * H + 1.0, A.min, A.subtract, [], ["cb0", "ps2"])
         ts(T.MB[:, 1:34], T.RW[:, 0:33], col(cS2), -1000.0, A.is_gt, A.mult, ["RWa", "RWb", "s2"], ["MBb"])
-        ts(T.cb[:, HC:C], T.ps2[:, 1:C:2], 2 * H + 2.0, 2 * H + 1.0, A.min, A.subtract, [], ["cb1", "ps2"])
-        for k in range(2):
-            act(T.cnt[:, HC * k:HC * k + HC], T.ps2[:, k:C:2], AF.Copy, [], ["cnt%d" % k, "ps2"])
+        ts(T.eq[:], T.cb[:], 2 * H + 1.0, ac(1), A.subtract, A.is_equal, ["cb", "ac1"], ["eq"])
         scan(T.SC[:], T.MB[:], T.RW[:], -float(C), A.add, A.max, ["MBa", "MBb", "RWa", "RWb", "RWc"], ["SC"])
-        ts(T.eq[:], T.cb[:], ac(1), None, A.is_equal, None, ["cb0", "cb1", "ac1"], ["eq"])
+        if first:
+            mask4(T.MU, HC, "MU", lambda u: col(cCM + u), (0, 1))
         fill(1)
         scan(T.pf[:], T.eq[:], T.eq[:], T.SC[:, 33:34], A.add, A.add, ["eq", "SC"], ["pf"])
-        act(T.junk[:], T.pf[:], AF.Sign, ["pf", "n2"], ["junk", "ac2"], bias=col(cN2), accum_out=ac(2))
+        act(T.junk[:], T.pf[:], AF.Sign, ["pf", "n2"], ["junk", "junka", "junkb", "ac2"], bias=col(cN2), accum_out=ac(2))
+        if first:
+            mask4(T.MU, HC, "MU", lambda u: col(cCM + u), (2, 3))
         fill(3)
         ts(T.offH[:, 0:1], ac(2), -0.5, C / 2.0, A.mult, A.add, ["ac2"], ["offH"])
-        ts(T.offG[:], T.kG[:], ac(2), -2.0, A.add, A.mult, ["kG", "ac2"], ["offG"])
-        tt(T.KY[:, 0:H], T.cnt[:].indirect(T.offH[:, 0:1]), T.tie[:], A.add, ["cnt0", "cnt1", "offH", "tie"], ["KYa"])
+        ts(T.offG[:], T.kG[:], ac(2), ac(2), A.subtract, A.subtract, ["kG", "ac2"], ["offG"])
+        tt(T.KY[:, 0:H], T.cnt[:].indirect(T.offH[:, 0:1]), T.tie[:], A.add, CNT + ["offH", "tie"], ["KYa"])
         act(T.Bu[:], T.X[:].indirect(T.offG[:]), AF.Copy, XA + ["offG"], ["Bu"])
         fill(1)
         scan(T.OW[:], T.DK[:], T.KY[:], 0.0, A.add, A.max, ["DK", "KYa", "KYb"], ["OW"])
         act(T.junk2[:, 0:H], T.KY[:, 0:H], AF.Sign, ["KYa", "OW"], ["junk2", "ac3"], scale=-1.0, bias=T.OW[:, 16:17], accum_out=ac(3))
         fill(2)
-        ts(T.offS[:], T.kS[:], ac(3), -2.0, A.add, A.mult, ["kS", "ac3"], ["offS"])
+        ts(T.offS[:], T.kS[:], ac(3), ac(3), A.subtract, A.subtract, ["kS", "ac3"], ["offS"])
         ts(T.offR[:, 0:1], ac(3), -0.5, (H - 1) / 2.0, A.mult, A.add, ["ac3"], ["offR"])
         cp(T.Bt[:, 0:4 * H].indirect(T.offS[:]), T.Bu[:], ["Bu", "offS"], ["Bt"])
         fill(1)
         qz("Fq%d" % t, "Fs%d" % t, OWN, OWN + 128, T.Bt[:], ["Bt"], ["Fown%d" % t])
-        send("q", t)
-        send("s", t)
+        for kind, what in CALLS:
+            send(kind, what, t)
+        if first:
+            iota(T.ioR[:], [[1, C]], -HC, 0, ["ioR"])
+            iota(T.ioF[:], [[1, C]], 0, 0, ["ioF"])
+            act(T.LB[:, C:3 * C], T.LB[:, 0:C].indirect(T.offc[:]), AF.Copy, ["LB0", "offc"], ["LB1"])
+            act(col(cT128), col(cT), AF.Identity, ["cf"], ["t128"], scale=float(N * H))
         for h in range(2):
             act(part(T.Xp, h), T.X[:].indirect(T.offX[:, MO[h]:MO[h] + QH[h]]), AF.Copy, XA + ["offX%d" % h], ["Xp%d" % h], scale=2.0)
         if first:
@@ -585,6 +608,7 @@ def rank_program(g, core, T, topo):
                 a = 48 * h
                 act(T.ixr[:, a:a + 48 - 16 * h], T.ix0[:, a:a + 48 - 16 * h], AF.Identity, ["ix0%d" % h, "ix02", "mb%d" % h], ["ixr%d" % h], bias=col(cMB + h))
             act(T.LR[:], T.ioR[:].indirect(T.offc[:]), AF.Copy, ["ioR", "offc"], ["LR"])
+            act(col(cT576), col(cT), AF.Identity, ["cf"], ["t576"], bias=float(2 * C))
             tt(T.PB[:, 0:C], T.LB[:, 0:C].indirect(T.offQ[:, 0:18]), T.MU[:, 0:C], A.mult, ["LB0"] + PERM + MU, ["PB0"])
             tt(T.PB[:, C:3 * C], T.LB[:, C:3 * C].indirect(T.offQ[:]), T.MU[:], A.mult, ["LB1"] + PERM + MU, ["PB1"])
             fill(1)
@@ -635,12 +659,24 @@ def rank_program(g, core, T, topo):
             else:
                 cp(T.offM[:, a:a + n], T.sf[:, 48 * h:48 * h + n], ["sf%d" % h], ["offM%d" % h])
 
-        def mix(h):
-            tt(part(T.Mt, h), T["U%d" % h][:].indirect(T.offM[:, MO[h]:MO[h] + QH[h]]), part(T.Xh, h), A.add,
-               ["U%d0" % h, "U%d1" % h, "Xh", "offM%d" % h], ["Mt%d" % h])
+        def mix(h, a, b):
+            c, d = 4 * BASE[h] + 16 * a, 4 * BASE[h] + 16 * b
+            tt(T.Mt[:, c:d], T["U%d" % h][:].indirect(T.offM[:, MO[h] + a:MO[h] + b]), T.Xh[:, c:d], A.add,
+               ["U%d0" % h, "U%d1" % h, "Xh", "offM%d" % h], ["Mt%d%d" % (h, a > 0)])
+
+        def select(h, a, b):
+            c, d = 4 * BASE[h] + 16 * a, 4 * BASE[h] + 16 * b
+            act(T.Mu[:, c:d], T["U%d" % h][:].indirect(T.offM[:, MO[h] + a:MO[h] + b]), AF.Copy, ["U%d0" % h, "U%d1" % h, "offM%d" % h], ["Mu%d" % h])
+
+        def add(h, a, b):
+            c, d = 4 * BASE[h] + 16 * a, 4 * BASE[h] + 16 * b
+            tt(T.Mt[:, c:d], T.Mu[:, c:d], T.Xh[:, c:d], A.add, ["Mu%d" % h, "Xh"], ["Mt%d%d" % (h, a > 0)])
+
+        def fetch(h, k):
+            cp(uview(h, k), T.F[:].indirect(T["off%d" % k][:, 48 * h:48 * h + QH[h]]), FA + ["off%d%d" % (k, h)], ["U%d%d" % (h, k)])
 
         def layer(h):
-            qz("Mq", "Ms", BASE[h], BASE[h] + NH[h], part(T.Mt, h), ["Mt%d" % h], ["Mq%d" % h])
+            qz("Mq", "Ms", BASE[h], BASE[h] + NH[h], part(T.Mt, h), names("Mt%d" % h, 2), ["Mq%d" % h])
             for b in range(4):
                 mm(4 * (1 - h) + b, NH[h], "Wq", "Ws", 128 * b, "Mq", "Ms", BASE[h], True, True, ["Wq", "Ws", "Mq%d" % h])
 
@@ -661,40 +697,16 @@ def rank_program(g, core, T, topo):
             mm(4 + h, NH[h], "Vq", "Vs", 0, "Xq", "Xs", a, True, True, ["Vq", "Xq%d" % h])
             dma("Y", T.oc[:, 4 * a:4 * b], T.Xq[:, a:b].bitcast(dt.uint8), ["Xq%d" % h], [])
 
-        def other(h):
-            if SCALAR_GATHERS:
-                zplain(h, 0, T.Xp, ["Xp%d" % h])
-            else:
-                zgather(h, 0, T.F, T.off0, 8 * h, T.Xp, FA + ["off0%d" % h, "Xp%d" % h])
-
-        for h, k in ((0, 0), (1, 0), (0, 1), (1, 1)):
+        for h, k in SLOTS:
             ugather(h, k, T.F, T["off%d" % k], 8 * h, FA + ["off%d%d" % (k, h)])
-        zgather(0, 1, T.F, T.off1, 0, T.Xp, FA + ["off10", "Xp0"])
-        other(0)
-        score(0, 1)
-        score(0, 0)
-        zgather(1, 1, T.F, T.off1, 8, T.Xp, FA + ["off11", "Xp1"])
-        other(1)
-        pick(0, 0)
-        score(1, 1)
-        pick(0, 1)
-        score(1, 0)
-        pick(0, 2)
-        if first:
-            ts(T.offW[:], T.SR[:, 3:2 * C:4], 4.0, col(cT576), A.mult, A.add, ["SR", "t576"], ["offW"])
-        mix(0)
-        pick(1, 0)
-        layer(0)
-        pick(1, 1)
-        pick(1, 2)
-        for b in range(4):
-            evac(0, b, "S")
-        mix(1)
-        layer(1)
-        finish(0)
-        for b in range(4):
-            evac(1, b, "SV"[b % 2])
-        finish(1)
+        def lists():
+            if first:
+                ts(T.offW[:], T.SR[:, 3:2 * C:4], 4.0, col(cT576), A.mult, A.add, ["SR", "t576"], ["offW"])
+
+        run(CHOICE, {"gather": lambda h: zgather(h, 1, T.F, T.off1, 8 * h, T.Xp, FA + ["off1%d" % h, "Xp%d" % h]),
+                     "plain": lambda h, k: zplain(h, k, T.Xp, ["Xp%d" % h]),
+                     "score": score, "pick": pick, "mix": mix, "layer": layer, "evac": evac, "finish": finish, "lists": lists,
+                     "select": select, "add": add, "fetch": fetch})
         if last:
             act(T.Y[:, 0:NH[0]], T.ps4[:, 0:NH[0]], AF.Copy, [], ["Y0", "ps4"])
             cp(T.Y[:, BASE[1]:C], T.ps5[:, 0:NH[1]], [], ["Y1", "ps5"])

from concourse.bass import DstId, RemoteDMATransfer
from concourse.mybir import dt, AluOpType, ActivationFunctionType

A = AluOpType
AF = ActivationFunctionType
C, H, R, N = 288, 16, 3, 8
HC = C // 2
BASE, NH = (0, 160), (160, 128)
QH = (40, 32)
MO = (0, 40)
NM = 72
PAD = 128 - QH[0]
ZC = {(0, 1): 0, (0, 0): 160, (1, 0): 320, (1, 1): 448}
SW = C + 2
FW = 2 * N * H - H
OWN = (N - 1) * H
BIG = 4096.0
KP, KN, OP, ON = 0, 140, 280, 408

WORDS = [[(0, r) for r in range(4)], [(0, r) for r in range(4, 8)], [(0, 8), (0, 9)], [(1, r) for r in range(4)], [(1, r) for r in range(4, 8)]]
LOW, ROUND = 2.0 ** -9, 1.5 * 2.0 ** 23
POINT = [("gather", 0), ("plain", 0, 0), ("score", 0, 1), ("score", 0, 0), ("plain", 1, 0), ("score", 1, 0), ("plain", 1, 1), ("choose", 0),
         ("score", 1, 1), ("pointers", 0), ("split", 0)]
COUNT = [("planes", 0), ("planes", 1), ("planes", 2), ("choose", 1), ("count", 0, 1), ("pointers", 1), ("count", 1, 2), ("split", 1),
         ("count", 2, 3), ("planes", 3), ("planes", 4), ("count", 3, 4), ("count", 4, 5)]
ON_SCALAR = [(0, 8), (0, 9), (1, 6), (1, 7)]
SLOTS = ((0, 0), (1, 0), (1, 1), (0, 1))
CHOICE = ([("gather", 0), ("plain", 0, 0), ("score", 0, 1), ("score", 0, 0), ("plain", 1, 0), ("score", 1, 0), ("plain", 1, 1), ("pick", 0, 0),
           ("score", 1, 1), ("pick", 0, 1), ("lists",), ("pick", 0, 2), ("select", 0, 28, 40), ("mix", 0, 0, 28), ("pick", 1, 0), ("add", 0, 28, 40),
           ("pick", 1, 1), ("layer", 0), ("pick", 1, 2), ("select", 1, 20, 32), ("mix", 1, 0, 20)]
          + [("evac", 0, b, "S") for b in range(4)] + [("add", 1, 20, 32), ("layer", 1), ("finish", 0)]
          + [("evac", 1, b, "SV"[b % 2]) for b in range(4)] + [("finish", 1)])

LOADS = {"q": (2, 2), "s": (3, 3)}
CALLS = [("s", "feed"), ("q", "feed"), ("q", "direct"), ("s", "direct")]

X4, U8, BF, F32, I32, U16 = "float8_e4m3fn_x4", "uint8", "bfloat16", "float32", "int32", "uint16"


def _sb(n, d):
    return ("sbuf", [128, n], d)


SCRATCH = {
    "X": _sb(4 * C, BF), "X2": _sb(4 * C, BF), "Xh": _sb(4 * C, BF), "Xp": _sb(4 * C, BF), "Z": _sb(8 * C, BF),
    "Zq": _sb(PAD + 2 * C, X4), "Zs": _sb(PAD + 2 * C, U8),
    "c1s": _sb(36, I32), "c2s": _sb(18, I32), "vt": _sb(512, BF), "Vq": _sb(128, X4), "Vs": _sb(128, U8),
    "Wq": _sb(512, X4), "Ws": _sb(512, U8),
    "pci": _sb(1, I32), "ci": _sb(5, I32), "CF": _sb(32, F32), "IO": _sb(32, F32), "IO4": _sb(NM, F32), "En": _sb(NM, F32),
    "one": _sb(2 * C, BF), "Ct": _sb(4 * 536, BF), "Cq": _sb(536, X4), "Cs": _sb(536, U8),
    "Et": _sb(516, BF), "Eq": _sb(512, X4), "Es": _sb(512, U8),
    "ioN": _sb(C, BF), "PC": _sb(18, BF), "PV": _sb(18, BF), "hu": _sb(HC, I32), "ioR": _sb(C, BF), "ioF": _sb(C, F32), "tabF": _sb(128, BF),
    "rm4": _sb(3 * C, BF), "IM": _sb(2 * C, BF), "MK": _sb(2 * C, BF), "MU": _sb(2 * C, BF), "PI": _sb(36, F32), "offQ": _sb(36, U16),
    "offP": _sb(144, U16), "offW": _sb(144, U16), "offc": _sb(36, U16), "offd": _sb(18, U16),
    "LA": _sb(2 * C, BF), "SA": _sb(2 * C, BF), "dQ": _sb(NM, F32),
    "LR": _sb(2 * C, BF), "PR": _sb(2 * C, BF), "SR": _sb(2 * C, BF),
    "LB": _sb(3 * C, BF), "PB": _sb(3 * C, BF), "SB": _sb(3 * C, BF),
    "dg": _sb(NM, F32), "t1": _sb(NM, F32), "t2": _sb(NM, F32),
    "D0": _sb(2 * NM, F32), "D1": _sb(2 * NM, F32), "PW": _sb(2 * NM, BF),
    "OH": _sb(20 * HC, BF), "OHq": _sb(5 * HC, X4), "OHs": _sb(5 * HC, U8),
    "cb": _sb(C, BF), "junk": _sb(C, BF), "junk2": _sb(C, BF), "cnt": _sb(C, BF), "eq": _sb(C, BF), "pf": _sb(C, BF),
    "AC": _sb(8, F32), "gm": _sb(32, F32), "bc": _sb(32, F32),
    "RW": _sb(34, F32), "MB": _sb(34, F32), "SC": _sb(34, F32),
    "offH": _sb(2, U16), "offR": _sb(2, U16), "offG": _sb(4, U16), "offS": _sb(4, U16), "kG": _sb(4, F32), "kS": _sb(4, F32),
    "tie": _sb(16, F32), "KY": _sb(17, F32), "DK": _sb(17, F32), "dk2": _sb(17, F32), "OW": _sb(17, F32),
    "Bu": _sb(64, BF), "Bt": _sb(512, BF), "h16": _sb(16, F32), "HL": _sb(R * H, F32),
    "F": _sb(512, BF), "U0": _sb(8 * NH[0], BF), "U1": _sb(8 * NH[1], BF),
    "off0": _sb(80, U16), "off1": _sb(80, U16), "offM": _sb(NM, U16), "offX": _sb(NM, U16),
    "ix0": _sb(80, F32), "ixr": _sb(80, F32), "sel2": _sb(NM, F32), "sf": _sb(80, F32),
    "tp": _sb(80, F32), "tm": _sb(80, F32), "ts": _sb(80, F32), "offT": _sb(6, U16),
    "Mt": _sb(4 * C, BF), "Mu": _sb(4 * C, BF), "Mq": _sb(C, X4), "Ms": _sb(C, U8), "Xq": _sb(C, X4), "Xs": _sb(C, U8), "Y": _sb(C, F32),
}
for _t in range(R):
    SCRATCH["Fq%d" % _t] = _sb(FW, X4)
    SCRATCH["Fs%d" % _t] = _sb(FW, U8)
SCRATCH["hq"] = _sb(R * H, X4)
SCRATCH["hs"] = _sb(R * H, U8)
for _b in range(8):
    SCRATCH["ps%d" % _b] = ("psum", [128, 512], F32)

NDMA = 20
SEMAPHORES = (["cV", "cS", "cP", "cG", "sent"] + ["dma%d" % i for i in range(NDMA)]
              + ["arr%d" % t for t in range(R)] + ["hin%d" % t for t in range(R)])


def _mask(engines):
    m = 0
    for e in engines:
        m |= 1 << e
    return m


def _plan(T, topo, rank):
    core = T.cores[rank]
    peers = [(rank + k) % N for k in range(1, N)]
    free = [c for c in topo.cores_of(core) if T.rank_of(c) is None and all(topo.may_write(c, T.cores[d]) for d in peers)]
    free.sort(key=lambda c: topo.die(c) == topo.die(core))
    plan = {}
    for kind, cores in (("q", free), ("s", free[::-1])):
        rest = peers if kind == "q" else peers[::-1]
        loads = []
        for c, n in zip(cores, LOADS[kind]):
            loads.append((c, rest[:n]))
            rest = rest[n:]
        plan[kind] = (rest, loads)
    return plan


def _view(T, kind, name, a, b):
    return T[name][:, a:b].bitcast(dt.uint8) if kind == "q" else T[name][:, a:b]


def _spread(T, topo, src_core, rank, kind, t, src, dests):
    ids, dsts = [], []
    for d in dests:
        rid, pid = topo.addr(T.cores[d], src_core)
        ids.append(DstId(rid=rid, pnc=pid))
        pos = ((rank - d - 1) % N) * H
        dsts.append(_view(T, kind, "F%s%d" % (kind, t), pos, pos + H))
    eng = topo.engines(src_core, T.cores[dests[0]])
    return RemoteDMATransfer(dst_ids=ids, dma_engine_mask=_mask(eng), remote_sem=T.sem["arr%d" % t], srcs=[src], dsts=dsts), len(eng)


def _feed_engines(T, topo, rank, helper, shared):
    core = T.cores[rank]
    off = topo.engines(core, T.cores[(rank + 1) % N]) if shared else []
    return [e for e in topo.engines(core, helper) if e not in off]


def _helper(g, core, T, topo):
    for rank in range(N):
        if core not in topo.cores_of(T.cores[rank]):
            continue
        for kind, (direct, loads) in _plan(T, topo, rank).items():
            for helper, rest in loads:
                if helper != core:
                    continue
                sent = 0
                for t in range(R):
                    g.wait_ge(T.sem["hin%d" % t], len(_feed_engines(T, topo, rank, core, (kind, "both") in CALLS)))
                    tr, n = _spread(T, topo, core, rank, kind, t, _view(T, kind, "h" + kind, H * t, H * t + H), rest)
                    g.remote_dma_fused([tr], local_sem=T.sem.sent)
                    sent += n
                g.wait_ge(T.sem.sent, sent)


def _emit(g, T, ops, tail):
    queue = {"V": g.vector, "S": g.scalar, "P": g.tensor, "G": g, "Y": g.sync}
    writer, readers = {}, {}
    known = {e: {} for e in queue}
    marked = set()
    ndma = 0
    for i, o in enumerate(ops):
        e = o["e"]
        deps = set()
        for k in o["r"]:
            if k in writer:
                deps.add(writer[k])
        for k in o["w"]:
            if k in writer:
                deps.add(writer[k])
            deps.update(readers.get(k, ()))
        need = {}
        for d in deps:
            u = ops[d]["u"]
            if d == i or u is None or (u == "P" and e == "P"):
                continue
            if d > need.get(u, -1):
                need[u] = d
        waits = []
        kn = known[e]
        for u, d in sorted(need.items(), key=lambda x: -x[1]):
            if kn.get(u, -1) >= d:
                continue
            waits.append(d)
            marked.add(d)
            for u2, d2 in ops[d]["clock"].items():
                if d2 > kn.get(u2, -1):
                    kn[u2] = d2
        o["waits"] = waits
        if o["dma"]:
            o["u"] = "dma%d" % ndma
            ndma += 1
        o["clock"] = dict(kn)
        if o["u"] is not None:
            o["clock"][o["u"]] = i
        for k in o["r"]:
            readers.setdefault(k, []).append(i)
        for k in o["w"]:
            writer[k] = i
            readers[k] = []
    count = {e: 0 for e in queue}
    for i, o in enumerate(ops):
        q = queue[o["e"]]
        for sem, val in o["pre"]:
            q.wait_ge(T.sem[sem], val)
        for d in o["waits"]:
            q.wait_ge(T.sem[ops[d]["sem"]], ops[d]["val"])
        ins = o["f"]()
        if o["dma"]:
            o["sem"], o["val"] = o["u"], 16
            ins.then_inc(T.sem[o["sem"]], 16)
        elif i in marked:
            count[o["e"]] += 1
            o["sem"], o["val"] = "c" + o["e"], count[o["e"]]
            ins.then_inc(T.sem[o["sem"]], 1)
    for i, o in enumerate(ops):
        if o["dma"] and i not in marked:
            queue[o["e"]].wait_ge(T.sem[o["sem"]], 16)
    for sem, val in tail:
        g.wait_ge(T.sem[sem], val)


def rank_program(g, core, T, topo):
    rank = T.rank_of(core)
    if rank is None:
        _helper(g, core, T, topo)
        return
    ops = []
    V, S, P, Y = g.vector, g.scalar, g.tensor, g.sync

    def op(e, f, r, w, dma=False, pre=(), remote=False):
        ops.append({"e": e, "f": f, "r": list(r), "w": list(w), "dma": dma, "pre": list(pre), "u": None if (dma or remote) else e})

    def ts(out, in0, s1, s2, o0, o1, r, w):
        if o1 is None:
            op("V", lambda: V.tensor_scalar(out, in0, s1, None, o0), r, w)
        else:
            op("V", lambda: V.tensor_scalar(out, in0, s1, s2, o0, o1), r, w)

    def tt(out, in0, in1, o, r, w):
        op("V", lambda: V.tensor_tensor(out, in0, in1, o), r, w)

    def cp(out, in_, r, w):
        op("V", lambda: V.tensor_copy(out, in_), r, w)

    def ms(ap, c, w):
        op("V", lambda: V.memset(ap, c), [], w)

    def scan(out, d0, d1, init, o0, o1, r, w):
        op("V", lambda: V.tensor_tensor_scan(out, d0, d1, init, o0, o1), r, w)

    def qz(q, s, a, b, tile, r, w):
        op("V", lambda: V.quantize_mx(T[q][:, a:b], T[s][:, a:b], tile), r, w)

    def act(out, in_, func, r, w, **kw):
        op("S", lambda: S.activation(out, in_, func, **kw), r, w)

    def mm(bank, n, lq, ls, la, rq, rs, ra, start, stop, r, pre=()):
        op("P", lambda: P.matmul_mx(T["ps%d" % bank][:, 0:n], T[lq][:, la:la + 128], T[ls][:, la:la + 128],
                                    T[rq][:, ra:ra + n], T[rs][:, ra:ra + n], start, stop), r, ["ps%d" % bank], pre=pre)

    def iota(out, pat, base, cm, w, flag=True):
        if flag:
            op("G", lambda: g.iota(out, pat, base, cm, allow_small_or_imprecise_dtypes=True), [], w)
        else:
            op("G", lambda: g.iota(out, pat, base, cm), [], w)

    def asel(out, in_, pat, cmp, base, cm, r, w):
        op("G", lambda: g.affine_select(out, in_, pat, cmp, 0.0, base, cm), r, w)

    def dma(e, out, in_, r, w):
        q = Y if e == "Y" else S
        op(e, lambda: q.dma_start(out, in_), r, w, dma=True)

    def col(i):
        return T.CF[:, i:i + 1]

    def ac(i):
        return T.AC[:, i:i + 1]

    def names(p, n):
        return [p + str(i) for i in range(n)]

    XA = names("X0", 4) + names("X1", 4)
    cQ, cT, cU, cHB, cG, cS2, cNS, cT576, cT128, cHM, cN2, cQT = range(12)
    cCM, cPM, cMB, cNT, cRL, cTOP, cK8 = 12, 16, 18, 20, 21, 22, 24

    dma("S", T.c1s[:], T.c1[:], [], ["c1s"])
    dma("Y", T.X[:], T.x[:], [], XA)
    dma("S", T.c2s[:], T.c2[:], [], ["c2s"])
    dma("Y", T.X2[:, 4 * NH[0]:4 * C], T.x[:, 4 * NH[0]:4 * C], [], ["X21"])
    dma("Y", T.Wq[:].bitcast(dt.uint8), T.wc[:], [], ["Wq"])
    dma("Y", T.Ws[:], T.ws[:], [], ["Ws"])
    dma("Y", T.vt[:], T.v[:], [], ["vt"])

    iota(T.pci[:], [[0, 1]], 0, 1, ["pci"], flag=False)
    iota(T.IO[:], [[1, 32]], 0, 0, ["IO"])
    iota(T.PI[:], [[C, 2], [4, 18]], 0, 0, ["PI"])
    iota(T.IM[:], [[0, 2 * C // 16], [1, 16]], 0, 0, ["IM"])
    iota(T.ioN[:, 0:HC], [[-1, HC]], -1, 0, ["ioNa"])
    iota(T.ioN[:, HC:C], [[1, HC]], 1, 0, ["ioNb"])
    iota(T.IO4[:], [[0, NM // 4], [1, 4]], 0, 0, ["IO4"])
    ms(T.one[:], 1.0, ["one"])
    ones = T.Ct[:, 4 * OP:4 * ON]
    asel(ones, T.one[:, 0:512], [[-16, 8], [0, 64]], A.is_ge, 0, 1, ["one"], ["Op"])
    asel(ones, ones, [[16, 8], [0, 64]], A.is_ge, 15, -1, ["Op"], ["Op"])
    own = (rank + 1) * H
    iota(T.tabF[:, 0:own], [[1, own]], N * H - own, 0, ["tabFa"])
    if own < N * H:
        iota(T.tabF[:, own:N * H], [[1, N * H - own]], 0, 0, ["tabFb"])
    for i, pts in enumerate(WORDS):
        for k in range(len(pts), 4):
            iota(T.OH[:, 4 * HC * i + k:4 * HC * (i + 1):4], [[0, HC]], 0, 0, ["OH%d%d" % (i, k)])
    iota(T.gm[:], [[1, 2], [0, 16]], 0, 0, ["gm"])
    iota(T.RW[:, 33:34], [[0, 1]], -C, 0, ["RWc"])
    iota(T.MB[:, 0:1], [[0, 1]], 0, 0, ["MBa"])
    iota(T.KY[:, 16:17], [[0, 1]], 0, 0, ["KYb"])
    iota(T.kG[:], [[1, 4]], 2 * C, 0, ["kG"])
    iota(T.kS[:], [[1, 4]], 2 * (H - 1), 0, ["kS"])
    asel(T.Et[:], T.one[:, 0:516], [[-1, 516]], A.is_equal, 3, 4, ["one"], ["Et"])
    for h in range(2):
        iota(T.ix0[:, 48 * h:48 * h + QH[h]], [[4, 4], [16, QH[h] // 4]], 0, 0, ["ix0%d" % h])
        iota(T.tp[:, 48 * h:48 * h + QH[h]], [[1, 4], [4, QH[h] // 4]], 0, 0, ["tp%d" % h])
    iota(T.ix0[:, 40:48], [[0, 8]], 0, 0, ["ix02"])
    iota(T.tp[:, 40:48], [[0, 8]], 0, 0, ["tp2"])

    ms(T.Ct[:, 4 * KP:4 * KN], 0.0, names("Kp", 8))
    ts(T.ci[:, 4:5], T.pci[:], 4, None, A.logical_shift_right, None, ["pci"], ["ci4"])
    ts(T.ci[:, 0:1], T.pci[:], 15, None, A.bitwise_and, None, ["pci"], ["ci0"])
    ts(T.ci[:, 1:2], T.pci[:], 3, None, A.bitwise_and, None, ["pci"], ["ci1"])
    ts(T.ci[:, 2:3], T.pci[:], 2, 3, A.logical_shift_right, A.bitwise_and, ["pci"], ["ci2"])
    ts(T.ci[:, 3:4], T.pci[:], 4, 1, A.logical_shift_right, A.bitwise_and, ["pci"], ["ci3"])
    ms(T.Bt[:], 0.0, ["Bt"])
    cp(T.CF[:, 0:5], T.ci[:], names("ci", 5), ["cf"])
    qz("Zq", "Zs", 0, 128, T.Bt[:], ["Bt"], ["Zpad", "Zq01"])
    ts(T.CF[:, cK8:cK8 + 8], T.IO[:, 0:8], col(cG), None, A.is_equal, None, ["IO", "cf"], ["k8"])
    for h in range(2):
        ts(col(cPM + h), col(cT), float(QH[h]), col(cU), A.mult, A.add, ["cf"], ["pm0%d" % h])
    ts(col(cQT), col(cT), 4.0, col(cU), A.mult, A.add, ["cf"], ["qt"])
    act(T.rm4[:, 0:2 * C], T.one[:], AF.Copy, ["one"], ["rm4"])
    act(T.rm4[:, 2 * C:3 * C], T.one[:, 0:C], AF.Copy, ["one"], ["rm4b"])
    act(T.rm4[:, 0:3 * C:4], T.one[:, 0:3 * NM], AF.Copy, ["one", "rm4b"], ["rm4"], scale=0.0)
    for i in range(8):
        a = 4 * KP + 48 + 64 * i
        act(T.Ct[:, a:a + 16], T.IO[:, 0:16], AF.Identity, ["IO", "k8"], ["Kp%d" % i], scale=0.0, bias=col(cK8 + i))
    act(T.Ct[:, 4 * KN:4 * OP], T.Ct[:, 4 * KP:4 * KN], AF.Copy, names("Kp", 8), ["Kn"], scale=-1.0)
    for k in range(2):
        for h in range(2):
            a, b = 18 * k + MO[h] // 4, 18 * k + (MO[h] + QH[h]) // 4
            ts(T.offQ[:, a:b], T.PI[:, a:b], col(cPM + h), float(BASE[h] - MO[h]), A.add, A.add, ["PI", "pm0%d" % h], ["perm%d%d" % (k, h)])
    PERM = names("perm0", 2) + names("perm1", 2)
    cp(T.offc[:], T.c1s[:], ["c1s"], ["offc"])
    for t in range(4):
        ts(T.offP[:, 36 * t:36 * t + 36], T.c1s[:], 4, t, A.mult, A.add, ["c1s"], ["offP%d" % t])
    ts(T.MK[:], T.IM[:], col(cQT), None, A.is_equal, None, ["IM", "qt"], ["MK"])

    def late_constants():
        act(T.dg[:], T.IO4[:], AF.Sign, ["IO4", "nt"], ["dg"], bias=col(cNT))
        act(T.tie[:], T.IO[:, 0:H], AF.Identity, ["IO"], ["tie"], scale=-LOW / H, bias=(H - 1) * LOW / H)
        act(T.D0[:, 0:2 * NM:2], T.dg[:], AF.Identity, ["dg"], ["D0e"], scale=BIG / 2, bias=BIG / 2)
        act(T.En[:], T.dg[:], AF.Identity, ["dg"], ["En"], scale=0.5 / BIG, bias=0.5 / BIG)

    def mask4(buf, n, w, bias, which):
        for u in which:
            act(buf[:, u:4 * n:4], T.IM[:, 0:n], AF.Identity, ["IM", "cm"], [w + str(u)], scale=0.0, bias=bias(u))

    def chain_constants():
        act(col(cNS), col(cQ), AF.Identity, ["cf"], ["ns"], scale=-LOW, bias=-LOW / 2)
        act(col(cTOP), col(cQ), AF.Identity, ["cf"], ["top"], scale=0.0, bias=-(H + 0.5) * LOW)
        for h in range(2):
            act(col(cMB + h), col(cU), AF.Identity, ["cf"], ["mb%d" % h], scale=float(4 * QH[h]), bias=col(cT))
        act(col(cHM), col(cHB), AF.Identity, ["cf"], ["hm"], bias=-1.0)
        act(col(cN2), col(cQ), AF.Identity, ["cf"], ["n2"], scale=-2.0, bias=C - 1.0)
        act(T.gm[:], T.gm[:], AF.Abs, ["gm", "hm"], ["gm"], bias=col(cHM))
        act(col(cS2), col(cQ), AF.Identity, ["cf"], ["s2"], scale=2.0, bias=-float(C))
        act(T.gm[:], T.gm[:], AF.Identity, ["gm"], ["gm"], scale=1000.0 + C, bias=-float(C))
        ts(T.CF[:, cCM:cCM + 4], T.IO[:, 0:4], col(cU), None, A.is_equal, None, ["IO", "cf"], ["cm"])

    plan = _plan(T, topo, rank)
    sent = [0]

    def send(kind, what, t):
        direct, loads = plan[kind]
        src = _view(T, kind, "F%s%d" % (kind, t), OWN, OWN + H)
        trs = []
        if what != "direct":
            eng = _feed_engines(T, topo, rank, loads[0][0], what == "both")
            ids = [DstId(rid=topo.addr(c, core)[0], pnc=topo.addr(c, core)[1]) for c, rest in loads]
            trs.append(RemoteDMATransfer(dst_ids=ids, dma_engine_mask=_mask(eng), remote_sem=T.sem["hin%d" % t],
                                         srcs=[src], dsts=[_view(T, kind, "h" + kind, H * t, H * t + H) for c in loads]))
            sent[0] += len(eng)
        if what != "feed":
            tr, n = _spread(T, topo, core, rank, kind, t, src, direct)
            trs.append(tr)
            sent[0] += n
        op("G", lambda: g.remote_dma_fused(trs, local_sem=T.sem.sent), ["Fown%d" % t], [], remote=True)

    arrivals = 0
    for s in range(N):
        if s != rank:
            for kind, (direct, loads) in _plan(T, topo, s).items():
                for c, dests in loads + [(T.cores[s], direct)]:
                    if rank in dests:
                        arrivals += len(topo.engines(c, core))

    order = sorted(ZC, key=lambda x: ZC[x])
    begun = [False, False]
    minus = []

    def zview(h, k, a=0, step=1):
        return T.Z[:, 4 * ZC[h, k] + a:4 * (ZC[h, k] + NH[h]):step]

    def part(buf, h, a=0, step=1):
        return buf[:, 4 * BASE[h] + a:4 * (BASE[h] + NH[h]):step]

    def uview(h, k):
        return T["U%d" % h][:, 4 * NH[h] * k:4 * NH[h] * (k + 1)]

    def zn(h, k):
        return names("Z%d%d" % (h, k), 4)

    def score(h, k):
        z = PAD + ZC[h, k]
        qz("Zq", "Zs", z, z + NH[h], zview(h, k), zn(h, k), ["Zq%d%d" % (h, k)])
        i = order.index((h, k))
        before = "Zpad" if i == 0 else "Zq%d%d" % order[i - 1]
        second = begun[h]
        begun[h] = not second
        for u in range(4):
            mm(h, 128, "Cq", "Cs", (KP if k else KN) + 12 - 4 * u, "Zq", "Zs", z + QH[h] * (u + 1) - 128, not second and u == 0, second and u == 3,
               ["Kq", before, "Zq%d%d" % (h, k)])

    def diff(h):
        return T["ps%d" % h][:, 128 - QH[h]:128]

    def zgather(h, k, win, off, a, other, r):
        tt(zview(h, k), win[:].indirect(off[:, a + MO[h]:a + MO[h] + QH[h]]), part(other, h), A.mult, r, zn(h, k))

    def ugather(h, k, win, off, a, r):
        act(uview(h, k), win[:].indirect(off[:, a + MO[h]:a + MO[h] + QH[h]]), AF.Copy, r, ["U%d%d" % (h, k)])

    def zplain(h, k, other, r, pieces=0):
        tt(zview(h, k), uview(h, k), part(other, h), A.mult, r + ["U%d%d" % (h, k)] + names("Ue%d" % h, pieces), zn(h, k))

    def uplanes(h):
        for e in range(4):
            a = 36 * e + BASE[h] // 16
            act(T["U%d" % h][:, e:4 * NH[h]:4], T.X[:].indirect(T.offP[:, a:a + NH[h] // 16]), AF.Copy, XA + ["offP%d" % e], ["Ue%d%d" % (h, e)])

    X1 = T.X2
    x1 = [["X20"], ["X21"]]

    def again(h):
        cp(part(T.X2, h), part(T.X, h), names("X%d" % h, 4), ["X2%d" % h])

    def zplanes(h, k):
        for e in range(4):
            a = 36 * e + 18 * k + BASE[h] // 16
            tt(zview(h, k, e, 4), T.X[:].indirect(T.offP[:, a:a + NH[h] // 16]), part(X1, h, e, 4), A.mult,
               XA + x1[h] + ["offP%d" % e], ["Z%d%d%d" % (h, k, e)])

    def choose(h):
        ts(T.D1[:, 2 * MO[h]:2 * (MO[h] + QH[h]):2], diff(h), 0.0, None, A.is_gt, None, [], ["D1e%d" % h, "ps%d" % h])

    def pointers(h):
        a, b = 2 * MO[h], 2 * (MO[h] + QH[h])
        scan(T.PW[:, a:b], T.D0[:, a:b], T.D1[:, a:b], 0.0, A.mult, A.add, ["D1e%d" % h, "D1o", "D0o", "D0e"], ["PW%d" % h])

    def split(h):
        a, b, c = 2 * MO[h] + 7, 2 * (MO[h] + QH[h]), MO[h] // 4
        act(T.PC[:, c:c + QH[h] // 4], T.PW[:, a:b:8], AF.Abs, ["PW%d" % h], ["PC%d" % h])
        ts(T.PV[:, c:c + QH[h] // 4], T.PW[:, a:b:8], 0.0, LOW, A.is_gt, A.max, ["PW%d" % h], ["PV%d" % h])
        mine = [(i, k, c + r) for i, w in enumerate(WORDS) for k, (h2, r) in enumerate(w) if h2 == h and (h, r) in ON_SCALAR]
        for n, (i, k, c) in enumerate(mine):
            act(T.junk[:, HC * n:HC * n + HC], T.ioN[:, HC:C], AF.Abs, ["ioNb", "PC%d" % h], ["junk" + "ab"[n]], scale=-1.0, bias=T.PC[:, c:c + 1])
        for n, (i, k, c) in enumerate(mine):
            act(T.OH[:, 4 * HC * i + k:4 * HC * (i + 1):4], T.junk[:, HC * n:HC * n + HC], AF.Relu, ["junk" + "ab"[n], "PV%d" % h], ["OH%d%d" % (i, k)],
                scale=-1.0, bias=T.PV[:, c:c + 1])

    def planes(i):
        for k, (h, r) in enumerate(WORDS[i]):
            c = MO[h] // 4 + r
            if (h, r) not in ON_SCALAR:
                ts(T.OH[:, 4 * HC * i + k:4 * HC * (i + 1):4], T.ioN[:, HC:C], T.PC[:, c:c + 1], T.PV[:, c:c + 1], A.is_equal, A.mult,
                   ["ioNb", "PC%d" % h, "PV%d" % h], ["OH%d%d" % (i, k)])

    def count(a, b):
        qz("OHq", "OHs", HC * a, HC * b, T.OH[:, 4 * HC * a:4 * HC * b], sum([names("OH%d" % i, 4) for i in range(a, b)], []), names("OHq", b)[a:])
        for i in range(a, b):
            mm(2, HC, "Cq", "Cs", OP, "OHq", "OHs", HC * i, i == 0, i == len(WORDS) - 1, ["Oq0", "OHq%d" % i])

    def reorder(off, src, h, r, w):
        m = (QH[h] + 15) // 16
        ts(off[:, 48 * h:48 * h + 16 * m], src[:, MO[h]:MO[h] + QH[h]].indirect(T.offT[:, 4 * h:4 * h + m]), col(cT128), None, A.add, None,
           r + ["offT%d" % h, "t128"], [w + str(h)])

    spare = [
        lambda: ts(T.DK[:], T.IO[:, 0:17], col(cQ), -16.0, A.is_equal, A.mult, ["IO", "cf"], ["DK"]),
        lambda: ts(T.dk2[:], T.IO[:, 0:17], col(cQ), 1.0, A.subtract, A.is_equal, ["IO", "cf"], ["dk2"]),
        lambda: qz("Eq", "Es", 0, 128, T.Et[:, 3:515], ["Et"], ["Eq0"]),
        lambda: ts(T.dk2[:, 16:17], T.dk2[:, 16:17], -1.0, None, A.add, None, ["dk2"], ["dk2"]),
        lambda: qz("Eq", "Es", 128, 256, T.Et[:, 2:514], ["Et"], ["Eq1"]),
        lambda: ts(T.dk2[:], T.dk2[:], 2.0, None, A.mult, None, ["dk2"], ["dk2"]),
        lambda: ts(T.tm[:], T.IM[:, 0:80], col(cQ), None, A.is_equal, None, ["IM", "cf"], ["tm"]),
        lambda: tt(T.DK[:], T.DK[:], T.dk2[:], A.add, ["DK", "dk2"], ["DK"]),
        lambda: ts(T.ts[:], T.IM[:, 0:80], 0.0, None, A.is_gt, None, ["IM"], ["ts"]),
        lambda: tt(T.tp[:], T.tm[:], T.tp[:], A.mult, ["tm"] + names("tp", 3), names("tp", 3)),
        lambda: qz("Eq", "Es", 256, 384, T.Et[:, 1:513], ["Et"], ["Eq2"]),
        lambda: scan(T.tm[:], T.ts[:], T.tp[:], 0.0, A.mult, A.add, ["ts"] + names("tp", 3), ["tm"]),
        lambda: ts(T.offX[:, 0:QH[0]], T.ix0[:, 0:QH[0]], col(cMB), None, A.add, None, ["ix00", "mb0"], ["offX0"]),
        lambda: ts(T.offX[:, QH[0]:NM], T.ix0[:, 48:80], col(cMB + 1), 4.0 * BASE[1], A.add, A.add, ["ix01", "mb1"], ["offX1"]),
        lambda: qz("Eq", "Es", 384, 512, T.Et[:, 0:512], ["Et"], ["Eq3"]),
        lambda: cp(T.offT[:, 0:3], T.tm[:, 15:48:16], ["tm"], ["offT0"]),
        lambda: cp(T.offT[:, 4:6], T.tm[:, 63:80:16], ["tm"], ["offT1"]),
    ]

    def run(steps, calls):
        for s in steps:
            calls[s[0]](*s[1:])

    def fill(n):
        for f in spare[:n]:
            f()
        del spare[:n]

    for t in range(R):
        first, last = t == 0, t == R - 1
        if first:
            uplanes(0)
            act(T.LA[:], T.ioN[:].indirect(T.offc[:]), AF.Copy, ["ioNa", "ioNb", "offc"], ["LA"])
            act(col(cNT), col(cT), AF.Identity, ["cf"], ["nt"], scale=-1.0, bias=-0.5)
            act(T.PR[:], T.LA[:].indirect(T.offQ[:]), AF.Copy, ["LA"] + PERM, ["PR"])
            uplanes(1)
            late_constants()
            cp(part(T.X2, 0), part(T.X, 0), names("X0", 4), ["X20"])
            qz("Cq", "Cs", KP, OP, T.Ct[:, 4 * KP:4 * OP], names("Kp", 8) + ["Kn"], ["Kq"])
            zplanes(0, 1)
            zplain(0, 0, T.X, names("X0", 4), 4)
            score(0, 1)
            score(0, 0)
            zplanes(1, 1)
            tt(T.PR[:], T.PR[:], T.MK[:], A.mult, ["PR", "MK"], ["PR"])
            choose(0)
            scan(T.SA[:], T.rm4[:, 0:2 * C], T.PR[:], 0.0, A.mult, A.add, ["rm4", "PR"], ["SA"])
            zplain(1, 0, T.X, names("X1", 4), 4)
            act(T.D1[:, 1:2 * NM:2], T.SA[:, 3:C:4], AF.Copy, ["SA"], ["D1o"])
            tt(T.dQ[:], T.SA[:, C + 3:2 * C:4], T.SA[:, 3:C:4], A.subtract, ["SA"], ["dQ"])
            score(1, 0)
            tt(T.D0[:, 1:2 * NM:2], T.dQ[:], T.En[:], A.add, ["dQ", "En"], ["D0o"])
            score(1, 1)
            pointers(0)
            qz("Cq", "Cs", OP, ON, T.Ct[:, 4 * OP:4 * ON], ["Op"], ["Oq0"])
            split(0)
            cp(T.offd[:], T.c2s[:], ["c2s"], ["offd"])
            act(T.LB[:, 0:C], T.tabF[:].indirect(T.offd[:]), AF.Copy, ["tabFa", "tabFb", "offd"], ["LB0"])
        else:
            for h, k in ((0, 0), (1, 0), (1, 1)):
                ugather(h, k, T.X, T.offW, NM * k, XA + ["offW"])
            run(POINT, {"gather": lambda h: zgather(h, 1, T.X, T.offW, NM, X1, XA + x1[h] + ["offW"]),
                        "plain": lambda h, k: zplain(h, k, T.X, names("X%d" % h, 4)),
                        "score": score, "choose": choose, "pointers": pointers, "split": split})
        run(COUNT, {"choose": choose, "pointers": pointers, "planes": planes, "split": split, "count": count})
        if first:
            chain_constants()
        fill(2)
        ts(T.hu[:], T.ps2[:, 0:HC], -LOW * HC, None, A.add, None, [], ["hu", "ps2"])
        fill(1)
        tt(T.cnt[:, 0:HC], T.ps2[:, 0:HC], T.hu[:], A.subtract, ["hu"], ["cnt0", "ps2"])
        ts(T.cnt[:, HC:C], T.hu[:], LOW, None, A.mult, None, ["hu"], ["cnt1"])
        CNT = ["cnt0", "cnt1"]
        act(T.junk[:], T.cnt[:], AF.Sign, CNT + ["ns"], ["junk", "junka", "junkb", "ac0"], bias=col(cNS), accum_out=ac(0))
        act(T.junk2[:], T.cnt[:], AF.Sign, CNT + ["top"], ["junk2", "RWb"], bias=col(cTOP), accum_out=T.RW[:, 32:33])
        fill(1)
        ts(T.cb[:], T.cnt[:], (H + 1) * LOW, 2 / LOW, A.min, A.mult, CNT, ["cb"])
        fill(1)
        ts(T.bc[:], T.gm[:], ac(0), None, A.min, None, ["gm", "ac0"], ["bc"])
        fill(1)
        op("V", lambda: V.transpose(T.RW[:, 0:32], T.bc[:]), ["bc"], ["RWa"])
        fill(2)
        act(T.junk[:, 0:33], T.RW[:, 0:33], AF.Sign, ["RWa", "RWb", "n2"], ["junk", "ac1"], bias=col(cN2), accum_out=ac(1))
        ts(T.MB[:, 1:34], T.RW[:, 0:33], col(cS2), -1000.0, A.is_gt, A.mult, ["RWa", "RWb", "s2"], ["MBb"])
        ts(T.eq[:], T.cb[:], 2 * H + 1.0, ac(1), A.subtract, A.is_equal, ["cb", "ac1"], ["eq"])
        scan(T.SC[:], T.MB[:], T.RW[:], -float(C), A.add, A.max, ["MBa", "MBb", "RWa", "RWb", "RWc"], ["SC"])
        if first:
            mask4(T.MU, HC, "MU", lambda u: col(cCM + u), (0, 1))
        fill(1)
        scan(T.pf[:], T.eq[:], T.eq[:], T.SC[:, 33:34], A.add, A.add, ["eq", "SC"], ["pf"])
        act(T.junk[:], T.pf[:], AF.Sign, ["pf", "n2"], ["junk", "junka", "junkb", "ac2"], bias=col(cN2), accum_out=ac(2))
        if first:
            mask4(T.MU, HC, "MU", lambda u: col(cCM + u), (2, 3))
        fill(3)
        ts(T.offH[:, 0:1], ac(2), -0.5, C / 2.0, A.mult, A.add, ["ac2"], ["offH"])
        ts(T.offG[:], T.kG[:], ac(2), ac(2), A.subtract, A.subtract, ["kG", "ac2"], ["offG"])
        tt(T.KY[:, 0:H], T.cnt[:].indirect(T.offH[:, 0:1]), T.tie[:], A.add, CNT + ["offH", "tie"], ["KYa"])
        act(T.Bu[:], T.X[:].indirect(T.offG[:]), AF.Copy, XA + ["offG"], ["Bu"])
        fill(1)
        scan(T.OW[:], T.DK[:], T.KY[:], 0.0, A.add, A.max, ["DK", "KYa", "KYb"], ["OW"])
        act(T.junk2[:, 0:H], T.KY[:, 0:H], AF.Sign, ["KYa", "OW"], ["junk2", "ac3"], scale=-1.0, bias=T.OW[:, 16:17], accum_out=ac(3))
        fill(2)
        ts(T.offS[:], T.kS[:], ac(3), ac(3), A.subtract, A.subtract, ["kS", "ac3"], ["offS"])
        ts(T.offR[:, 0:1], ac(3), -0.5, (H - 1) / 2.0, A.mult, A.add, ["ac3"], ["offR"])
        cp(T.Bt[:, 0:4 * H].indirect(T.offS[:]), T.Bu[:], ["Bu", "offS"], ["Bt"])
        fill(1)
        qz("Fq%d" % t, "Fs%d" % t, OWN, OWN + 128, T.Bt[:], ["Bt"], ["Fown%d" % t])
        for kind, what in CALLS:
            send(kind, what, t)
        if first:
            iota(T.ioR[:], [[1, C]], -HC, 0, ["ioR"])
            iota(T.ioF[:], [[1, C]], 0, 0, ["ioF"])
            act(T.LB[:, C:3 * C], T.LB[:, 0:C].indirect(T.offc[:]), AF.Copy, ["LB0", "offc"], ["LB1"])
            act(col(cT128), col(cT), AF.Identity, ["cf"], ["t128"], scale=float(N * H))
        for h in range(2):
            act(part(T.Xp, h), T.X[:].indirect(T.offX[:, MO[h]:MO[h] + QH[h]]), AF.Copy, XA + ["offX%d" % h], ["Xp%d" % h], scale=2.0)
        if first:
            MU = names("MU", 4)
            for h in range(2):
                a = 48 * h
                act(T.ixr[:, a:a + 48 - 16 * h], T.ix0[:, a:a + 48 - 16 * h], AF.Identity, ["ix0%d" % h, "ix02", "mb%d" % h], ["ixr%d" % h], bias=col(cMB + h))
            act(T.LR[:], T.ioR[:].indirect(T.offc[:]), AF.Copy, ["ioR", "offc"], ["LR"])
            act(col(cT576), col(cT), AF.Identity, ["cf"], ["t576"], bias=float(2 * C))
            tt(T.PB[:, 0:C], T.LB[:, 0:C].indirect(T.offQ[:, 0:18]), T.MU[:, 0:C], A.mult, ["LB0"] + PERM + MU, ["PB0"])
            tt(T.PB[:, C:3 * C], T.LB[:, C:3 * C].indirect(T.offQ[:]), T.MU[:], A.mult, ["LB1"] + PERM + MU, ["PB1"])
            fill(1)
            scan(T.SB[:], T.rm4[:], T.PB[:], 0.0, A.mult, A.add, ["rm4", "PB0", "PB1"], ["SB"])
            fill(99)
            tt(T.dg[:], T.SB[:, 2 * C + 3:3 * C:4], T.SB[:, C + 3:2 * C:4], A.subtract, ["SB"], ["dg"])
            cp(T.dQ[:], T.SB[:, 3:C:4], ["SB"], ["dQ"])
        tt(T.t1[:], T.D1[:, 0:2 * NM:2], T.dg[:], A.mult, ["D1e0", "D1e1", "dg"], ["t1"])
        if first:
            for h in range(2):
                reorder(T.off0, T.dQ, h, ["dQ"], "off0")
        else:
            ts(T.Xh[:], T.X[:], 0.5, None, A.mult, None, XA, ["Xh"])
        tt(T.t2[:], T.t1[:], T.SB[:, C + 3:2 * C:4], A.add, ["t1", "SB"], ["t2"])
        if first:
            ts(T.Xh[:], T.X[:], 0.5, None, A.mult, None, XA, ["Xh"])
        for h in range(2):
            reorder(T.off1, T.t2, h, ["t2"], "off1")
        act(T.h16[:], T.ioF[:].indirect(T.offH[:, 0:1]), AF.Copy, ["ioF", "offH"], ["h16"])
        if first:
            tt(T.PR[:], T.LR[:], T.MU[:], A.mult, ["LR"] + MU, ["PR"])
        cp(T.HL[:, H * t:H * t + H].indirect(T.offR[:, 0:1]), T.h16[:], ["h16", "offR"], ["HL%d" % t])
        if first:
            scan(T.SR[:], T.rm4[:, 0:2 * C], T.PR[:], 0.0, A.mult, A.add, ["rm4", "PR"], ["SR"])
        if t == 1:
            qz("Vq", "Vs", 0, 128, T.vt[:], ["vt"], ["Vq"])
        if last:
            dma("Y", T.hl[:], T.HL[0:128:16, :], names("HL", R), [])
        for b in range(4):
            mm(4 + b, 128, "Eq", "Es", 128 * b, "Fq%d" % t, "Fs%d" % t, 0, True, True, ["Eq%d" % b, "Fown%d" % t],
               pre=[("arr%d" % t, arrivals)] if b == 0 else ())
        for b in range(4):
            bank = "ps%d" % (4 + b)
            if b % 2 == 1:
                ts(T.F[:, 128 * b:128 * b + 128], T[bank][:, 0:128], 0.5, None, A.mult, None, [], ["F%d" % b, bank])
            else:
                act(T.F[:, 128 * b:128 * b + 128], T[bank][:, 0:128], AF.Copy, [], ["F%d" % b, bank], scale=0.5)
        FA = names("F", 4)

        def pick(h, step):
            a, n = MO[h], QH[h]
            if step == 0:
                ts(T.sel2[:, a:a + n], diff(h), 0.0, 4.0 * NH[h], A.is_gt, A.mult, [], ["sel2%d" % h, "ps%d" % h])
            elif step == 1:
                m = (n + 15) // 16
                tt(T.sf[:, 48 * h:48 * h + 16 * m], T.sel2[:, a:a + n].indirect(T.offT[:, 4 * h:4 * h + m]), T.ixr[:, 48 * h:48 * h + 16 * m], A.add,
                   ["sel2%d" % h, "offT%d" % h, "ixr%d" % h], ["sf%d" % h])
            else:
                cp(T.offM[:, a:a + n], T.sf[:, 48 * h:48 * h + n], ["sf%d" % h], ["offM%d" % h])

        def mix(h, a, b):
            c, d = 4 * BASE[h] + 16 * a, 4 * BASE[h] + 16 * b
            tt(T.Mt[:, c:d], T["U%d" % h][:].indirect(T.offM[:, MO[h] + a:MO[h] + b]), T.Xh[:, c:d], A.add,
               ["U%d0" % h, "U%d1" % h, "Xh", "offM%d" % h], ["Mt%d%d" % (h, a > 0)])

        def select(h, a, b):
            c, d = 4 * BASE[h] + 16 * a, 4 * BASE[h] + 16 * b
            act(T.Mu[:, c:d], T["U%d" % h][:].indirect(T.offM[:, MO[h] + a:MO[h] + b]), AF.Copy, ["U%d0" % h, "U%d1" % h, "offM%d" % h], ["Mu%d" % h])

        def add(h, a, b):
            c, d = 4 * BASE[h] + 16 * a, 4 * BASE[h] + 16 * b
            tt(T.Mt[:, c:d], T.Mu[:, c:d], T.Xh[:, c:d], A.add, ["Mu%d" % h, "Xh"], ["Mt%d%d" % (h, a > 0)])

        def fetch(h, k):
            cp(uview(h, k), T.F[:].indirect(T["off%d" % k][:, 48 * h:48 * h + QH[h]]), FA + ["off%d%d" % (k, h)], ["U%d%d" % (h, k)])

        def layer(h):
            qz("Mq", "Ms", BASE[h], BASE[h] + NH[h], part(T.Mt, h), names("Mt%d" % h, 2), ["Mq%d" % h])
            for b in range(4):
                mm(4 * (1 - h) + b, NH[h], "Wq", "Ws", 128 * b, "Mq", "Ms", BASE[h], True, True, ["Wq", "Ws", "Mq%d" % h])

        def evac(h, b, eng):
            bank = "ps%d" % (4 * (1 - h) + b)
            if eng == "V":
                ts(part(T.X, h, b, 4), T[bank][:, 0:NH[h]], 0.03125, None, A.mult, None, [], ["X%d%d" % (h, b), bank])
            else:
                act(part(T.X, h, b, 4), T[bank][:, 0:NH[h]], AF.Copy, [], ["X%d%d" % (h, b), bank], scale=0.03125)

        def finish(h):
            a, b = BASE[h], BASE[h] + NH[h]
            if not last:
                if h == 0:
                    again(0)
                return
            qz("Xq", "Xs", a, b, part(T.X, h), names("X%d" % h, 4), ["Xq%d" % h])
            mm(4 + h, NH[h], "Vq", "Vs", 0, "Xq", "Xs", a, True, True, ["Vq", "Xq%d" % h])
            dma("Y", T.oc[:, 4 * a:4 * b], T.Xq[:, a:b].bitcast(dt.uint8), ["Xq%d" % h], [])

        for h, k in SLOTS:
            ugather(h, k, T.F, T["off%d" % k], 8 * h, FA + ["off%d%d" % (k, h)])
        def lists():
            if first:
                ts(T.offW[:], T.SR[:, 3:2 * C:4], 4.0, col(cT576), A.mult, A.add, ["SR", "t576"], ["offW"])

        run(CHOICE, {"gather": lambda h: zgather(h, 1, T.F, T.off1, 8 * h, T.Xp, FA + ["off1%d" % h, "Xp%d" % h]),
                     "plain": lambda h, k: zplain(h, k, T.Xp, ["Xp%d" % h]),
                     "score": score, "pick": pick, "mix": mix, "layer": layer, "evac": evac, "finish": finish, "lists": lists,
                     "select": select, "add": add, "fetch": fetch})
        if last:
            act(T.Y[:, 0:NH[0]], T.ps4[:, 0:NH[0]], AF.Copy, [], ["Y0", "ps4"])
            cp(T.Y[:, BASE[1]:C], T.ps5[:, 0:NH[1]], [], ["Y1", "ps5"])
            dma("S", T.y[:, 0:NH[0]], T.Y[:, 0:NH[0]], ["Y0"], [])
            for k in range(4):
                dma("YS"[k // 2], T.osc[4 * k:4 * k + 4, :], T.Xs[32 * k:32 * k + 4, :], ["Xq0", "Xq1"], [])
            dma("Y", T.y[:, BASE[1]:C], T.Y[:, BASE[1]:C], ["Y1"], [])
    _emit(g, T, ops, [("sent", sent[0])])
